import numpy as np, ml_dtypes
CORES = [40,64,80,88,96,104,120,144]
N = 8
BF = ml_dtypes.bfloat16
def gentries(a):
    return np.ascontiguousarray(a.reshape(8, 16, -1).transpose(0, 2, 1)).reshape(8, -1)
def gtable(e):
    e = np.asarray(e); return np.ascontiguousarray(e.reshape(8, -1, 16).transpose(0, 2, 1)).reshape(128, -1).astype(np.int32)
M, K, D, CAP, A, RO = 256, 960, 16, 32, 3, 4
W, S, L = N * M, K // D, K // N
PS, ST = 0.0078125, 0.015625
LIM = np.float32(4.0)
HOT = np.array([4.0, 2.0, 1.3359375, 1.0, 0.80078125, 0.66796875, 0.57421875])
COLD = np.array([3.984375, 1.9921875, 1.328125, 0.99609375, 0.796875, 0.6640625, 0.5703125])
def pay(rng, a):
    v = 1.0 + 0.2 * rng.standard_normal((N, 128, W), dtype=np.float32) + 0.1 * rng.integers(-1, 2, (N, 128, 1)) + a * (2.0 * rng.random((N, 1, W)) - 1.0)
    return np.clip(v, 0.5, 1.5).astype(BF)
def parts(rng):
    e = pay(rng, 0.0); w = np.exp2(4.0 * rng.random((N, 8, W)) - 2.0)
    share = rng.choice(np.array([0.05, 0.2, 0.5, 0.9]), (N, 8, N, 1))
    l = np.where(rng.random((N, 8, N, M)) < share, rng.integers(1, 8, (N, 8, N, M)), 0).reshape(N, 8, W)
    b = np.ascontiguousarray(np.argsort(rng.random((N, 8, RO, W)), axis=-1)[..., :2 * K]).reshape(N, 8, RO, 2, K)
    t = np.clip(0.625 * rng.standard_normal((N, 16, RO * S)), -1.0, 1.0).astype(BF)
    return e, w, l, b, t
def pack(e, w, l, b, t):
    return {"e0": e, "wt": np.asarray(w).astype(BF), "lag": np.asarray(l).astype(np.int32), "bt": np.stack([gtable(a.reshape(8, -1)) for a in b]), "tg": t}
def close(rng, n):
    v = (np.exp2(np.arange(-9.0, -5.0))[:, None] * np.arange(128, 256)).reshape(-1)
    x = (v[:, None] * (A * (RO - 1) + np.arange(8))).reshape(-1); o = np.argsort(x, kind="stable"); k = x[o]
    i = rng.choice(np.flatnonzero((k[1:] > k[:-1]) & (k[1:].astype(np.float16) == k[:-1].astype(np.float16))), n)
    lo = o[i]; hi = o[i + 1]
    return v[lo // 8], lo % 8, v[hi // 8], hi % 8
def herd(rng, w, l, b, g, q, lo):
    x = np.stack([np.concatenate([np.array([M - 1, 0]), 1 + rng.permutation(M - 2)]) + h * M for h in range(N)])
    m = x[:, :L]; a = x[:, L:2 * L]; o = x[:, 2 * L:]
    w[:, g] = 0.25; w[:, g][:, m] = 4.0
    l[:, g] = 0; l[:, g][:, m] = 7
    near = np.zeros(L // 2, bool); kind = np.arange(16) % 6
    if q >= 0:
        X = min(CAP, L - CAP); l[q, g][m[:, 2:X]] = rng.choice(np.array([lo, 7]), (N, X - 2))
        if lo > 0:
            w[q, g][m[:, 2:10]] = 0.75; l[q, g][m[:, 2:10]] = 7
            w[q, g][o[:, :8]] = (6.5 + (N - 1 + A) * (RO - 1)) * 0.75 * 0.142857142857; l[q, g][o[:, :8]] = 7
    else:
        y = CAP // 2 + rng.permutation(L // 2 - CAP // 2)[:(L - CAP) // 4]; near[y] = True
        wl, al, wh, ah = close(rng, len(y))
        w[:, g][:, m[:, 2 * y]] = wl; l[:, g][:, m[:, 2 * y]] = al; w[:, g][:, m[:, 2 * y + 1]] = wh; l[:, g][:, m[:, 2 * y + 1]] = ah
        w[:, g][:, o[:, :16]] = np.array([4.0, 4.0, 2.0, 2.0, 4.0, 4.0])[kind]
        l[:, g][:, o[:, :16]] = np.array([A, A, 2 * A - 1, 2 * A + 1, A + 1, A - 1])[kind]
    k = int(rng.integers(0, N)); k2 = (k + 1) % N
    j = np.arange(K); h = j % N; i = j // N
    for r in range(N):
        b[r, g, :, 0] = m[h, L - 1 - i if r == q else i]; b[r, g, :, 1] = a[h, i]
        if q == -2:
            f = m.copy(); s = a.copy(); f[k] = a[k2]; s[k2] = m[k]
            b[r, g, RO - 2, 0] = f[h, i]; b[r, g, RO - 2, 1] = s[h, i]
        sp = np.arange(0); first = np.zeros(0, bool)
        if q < 0:
            z = 1 + rng.permutation(CAP // 2 - 1)[:8]; sp = rng.permutation(np.concatenate([2 * z, 2 * z + 1])); first = kind % 2 == 1
        elif r == q and lo > 0:
            sp = np.arange(2, 10); first = rng.random(8) < 0.5
        n = len(sp); c = n // 2; p = m[:, sp]; v = o[:, :n]
        z = np.concatenate([rng.permutation(np.setdiff1d(np.arange(1, L // 2), sp // 2)), np.array([0])])
        f = np.concatenate([np.where(first, v, p), a[:, c:L // 2], m[:, 2 * z]], axis=1)
        s = np.concatenate([np.where(first, p, v), a[:, L // 2 + c:], m[:, 2 * z + 1]], axis=1)
        t = rng.random((N, L)) < 0.5; t[:, :n] = True; t[:, L // 2 + c:] |= near[z]
        if q == -1:
            f[k2] = m[k2]; s[k2] = m[k]; f[k] = a[k2]; s[k] = a[k]; t[k2] = True
        b[r, g, RO - 1, 0] = np.where(t, f, s)[h, i]; b[r, g, RO - 1, 1] = np.where(t, s, f)[h, i]
def leave(rng, w, l, b, g, q, v):
    x = np.stack([np.concatenate([np.array([M - 1, 0]), 1 + rng.permutation(M - 2)]) + h * M for h in range(N)])
    m = x[:, :L]; a = x[:, L:2 * L]; j = np.arange(K); h = j % N; i = j // N
    w[:, g] = 0.25; w[:, g][:, m] = 4.0
    l[:, g] = 0; l[:, g][:, m] = 7
    w[q, g][m[:, CAP:CAP + 16]] = v
    b[:, g, :RO - 1, 0] = m[h, i]; b[:, g, :RO - 1, 1] = a[h, i]
    b[q, g, RO - 2, 0] = m[h, L - 1 - i]
    z = rng.permutation(np.setdiff1d(np.arange(M), np.concatenate([np.arange(16), CAP + np.arange(16)])))[:2 * L - 32]
    f = np.concatenate([m[:, :16], x[:, z[:L - 16]]], axis=1); s = np.concatenate([m[:, CAP:CAP + 16], x[:, z[L - 16:]]], axis=1)
    t = rng.random((N, L)) < 0.5
    b[q, g, RO - 1, 0] = np.where(t, f, s)[h, i]; b[q, g, RO - 1, 1] = np.where(t, s, f)[h, i]
def full(rng, w, l, b, r, g, h):
    Q = K // 8; T = K - M - Q; k = (h + 1) % N; x = np.arange(W).reshape(N, M)
    y = rng.permutation(x[k]); z = rng.permutation(x[[v for v in range(N) if v != h and v != k]].reshape(-1))
    n = np.concatenate([rng.permutation(np.concatenate([x[h], z[:T]])), y[:Q]]); o = rng.permutation(np.concatenate([z[T:], y[Q:]]))[:K]
    v = rng.integers(1, 8, K); w[r, g][n] = HOT[v - 1]; l[r, g][n] = v
    v = rng.integers(0, 8, K); w[r, g][o] = np.where(v == 0, 4.0, COLD[v - 1]); l[r, g][o] = v
    t = rng.random(K) < 0.5
    b[r, g, 0, 0] = np.where(t, n, o); b[r, g, 0, 1] = np.where(t, o, n)
def setup_inputs(rng):
    return pack(*parts(rng))
def setup_inputs_spread(rng):
    e, w, l, b, t = parts(rng)
    e = np.where(rng.random((N, 1, W)) > 0.0625, pay(rng, 0.5).astype(np.float32), np.float32(0.5)).astype(BF)
    return pack(e, w, l, b, t)
def setup_inputs_ends(rng):
    e, w, l, b, t = parts(rng)
    w = rng.choice(np.array([0.25, 4.0]), (N, 8, W)); l = rng.choice(np.array([0, 7]), (N, 8, W))
    o = 1 + np.argsort(rng.random((N, 8, RO, W - 2)), axis=-1)[..., :2 * K - 2]
    b[..., 0, :K - 1] = o[..., :K - 1]; b[..., 1, :K - 1] = o[..., K - 1:]
    b[..., 0, K - 1] = W - 1; b[..., 1, K - 1] = 0
    l[..., 0] = 7; l[..., W - 1] = 7; w[..., 0] = 4.0; w[..., W - 1] = 4.0
    for g in (1, 3, 5, 7): herd(rng, w, l, b, g, N - 1 if g == 7 else int(rng.integers(0, N)), 0)
    t = rng.choice(np.array([-1.0, 1.0]), t.shape).astype(BF)
    q = int(rng.integers(0, N)); v = rng.choice(np.array([0.5, 1.5]), (N, 8, W)); v[q] = 1.5
    k = (q + int(rng.integers(1, N))) % N; y = rng.choice(np.array([0.5, 1.5]), (N, 8, W)); y[k] = 0.5
    t[k, 14, S - 1] = 1.0; t[k, 14, 0] = 1.0
    z = w * l; na = b[:, :, 0, 0]; nb = b[:, :, 0, 1]
    n = np.where(np.take_along_axis(z, nb, 2) > np.take_along_axis(z, na, 2), nb, na)
    for g in range(8):
        v[n[q, g] // M, g, n[q, g]] = 1.5
        y[n[k, g] // M, g, n[k, g]] = 0.5
    e = e.reshape(N, 8, 16, W).copy(); e[:, :, 15] = v.astype(BF); e[:, :, 14] = y.astype(BF); e = e.reshape(N, 128, W)
    return pack(e, w, l, b, t)
def setup_inputs_corners(rng):
    e, w, l, b, t = parts(rng)
    for r in range(N):
        for g in range(8):
            if r > 0 and (r + g) % 3 == 0:
                full(rng, w, l, b, r, g, (r + g) % N); continue
            sl = rng.permutation(K).reshape(N, L)
            for h in range(N):
                n = int(rng.choice(np.array([0, 1, CAP - 1, CAP, CAP + 1, L])))
                if r == 0 and h == 1: n = (CAP, 0, 1, CAP - 1, CAP + 1, L, CAP, CAP + 1)[g]
                nm = (h * M + rng.permutation(M))[:2 * L].reshape(2, L)
                z = rng.integers(1, 8, (2, L)); hot = np.zeros((2, L), bool); k = rng.permutation(L)[:n]; y = rng.integers(0, 3, n)
                z[1] = np.where(rng.random(L) < 0.3, z[0], z[1])
                hot[0, k] = y != 1; hot[1, k] = y != 0
                none = (rng.random((2, L)) < 0.4) & ~hot
                w[r, g][nm] = np.where(none, rng.choice(np.array([0.25, 4.0]), (2, L)), np.where(hot, HOT[z - 1], COLD[z - 1]))
                l[r, g][nm] = np.where(none, 0, z)
                b[r, g, 0][:, sl[h]] = nm
    return pack(e, w, l, b, t)
def setup_inputs_crowd(rng):
    e, w, l, b, t = parts(rng)
    for g, q in ((0, -1), (2, int(rng.integers(0, N))), (4, -2), (6, int(rng.integers(0, N))), (7, N - 1)): herd(rng, w, l, b, g, q, 6)
    leave(rng, w, l, b, 1, int(rng.integers(0, N)), 4.0 * (N - 1 + 2 * A + np.where(np.arange(16) % 4 == 3, 0.5, -0.5)) / (7 + A * (RO - 1)))
    return pack(e, w, l, b, t)
def setup_inputs_calm(rng):
    e, w, l, b, t = parts(rng)
    w = rng.choice(np.concatenate([HOT, COLD, np.array([0.5, 0.498046875])]), (N, 8, W))
    act = (rng.permutation(N)[:, None] < (np.arange(8) % 4)[None, :])[:, :, None]
    w = np.where(act | (rng.random((N, 8, W)) < 0.25), w, 0.25)
    l = rng.integers(0, 4, (N, 8, W)) * (np.arange(8) % 2)[None, :, None]
    return pack(e, w, l, b, t)
def cand(bt):
    return np.stack([gentries(np.asarray(a)) for a in bt]).astype(np.int64).reshape(N, 8, RO, 2, K)
def check_ranges(d):
    bad = []
    for k, lo, hi in (("e0", 0.5, 1.5), ("wt", 0.25, 4), ("lag", 0, 7), ("bt", 0, W - 1), ("tg", -1, 1)):
        v = np.asarray(d[k]).astype(np.float64)
        if not (np.min(v) >= lo and np.max(v) <= hi): bad.append("range of " + k)
    b = np.sort(cand(d["bt"]).reshape(N, 8, RO, 2 * K), axis=-1)
    if np.any(b[..., 1:] == b[..., :-1]): bad.append("candidates of a round differ")
    return bad
def reference(e0, wt, lag, bt, tg):
    R = e0.astype(np.float64).reshape(N, 8, 16, W).copy(); P = np.zeros((N, 8, 16, W)); u = np.zeros((N, 8, W), np.int64)
    H = np.concatenate([R[h, :, :, h * M:(h + 1) * M] for h in range(N)], axis=2)
    c = np.zeros((8, W), np.int64); seen = -lag.astype(np.int64); b = cand(bt); w32 = wt.astype(np.float32); tgt = tg.astype(np.float64)
    for t in range(RO):
        sc = w32 * (c[None] - seen + A * u).astype(np.float32)
        took = []; asked = []
        for r in range(N):
            na = b[r, :, t, 0]; nb = b[r, :, t, 1]; sa = np.take_along_axis(sc[r], na, 1); sb = np.take_along_axis(sc[r], nb, 1)
            n = np.where(sb > sa, nb, na); due = np.where(sb > sa, sb, sa) >= LIM; home = n // M; ok = np.zeros((8, K), bool)
            for h in range(N):
                m = due & (home == h); ok = ok | (m & (np.add.accumulate(m.astype(np.int64), axis=1) <= CAP))
            took.append(n); asked.append([n[g][ok[g]] for g in range(8)])
        for r in range(N):
            for g in range(8):
                ix = asked[r][g]; H[g][:, ix] += P[r, g][:, ix]; c[g][ix] += 1
        for r in range(N):
            for g in range(8):
                ix = asked[r][g]; R[r, g][:, ix] = H[g][:, ix]; P[r, g][:, ix] = 0.0; u[r, g][ix] = 0; seen[r, g][ix] = c[g][ix]
        for r in range(N):
            n = took[r]; ix = np.broadcast_to(n[:, None, :], (8, 16, K)); x = np.take_along_axis(R[r], ix, 2); y = x.reshape(8, 16, D, S)
            p = np.add.reduce(y[:, :, :D // 2] * y[:, :, D // 2:], axis=(0, 2))
            e = np.tanh(tgt[r][:, t * S:(t + 1) * S] - PS * p)
            step = (ST * e[None, :, None, :] * np.concatenate([y[:, :, D // 2:], y[:, :, :D // 2]], axis=2)).reshape(8, 16, K)
            np.put_along_axis(R[r], ix, x + step, 2)
            if t < RO - 1:
                np.put_along_axis(P[r], ix, np.take_along_axis(P[r], ix, 2) + step, 2)
                np.put_along_axis(u[r], n, np.take_along_axis(u[r], n, 1) + 1, 1)
    return {"yr": R.reshape(N, 128, W).astype(np.float32), "yh": np.stack([H[:, :, h * M:(h + 1) * M].reshape(128, M) for h in range(N)]).astype(np.float32)}

def check_inputs(d):
    bad = list(check_ranges(d))
    if not bad:
        for name, y in reference(**d).items():
            for q in range(N):
                v = np.abs(np.asarray(y[q], np.float64)); s = np.sqrt(np.mean(v * v))
                if v.max() > 2 * s or s < 2.0 ** -2: bad.append('%s of rank %d is uneven or too small' % (name, q))
    return bad

@@ -1,0 +1,723 @@
+from concourse.bass import DstId, RemoteDMATransfer
+from concourse.mybir import AluOpType as OP, AxisListType as AX, ActivationFunctionType as AF
+
+N, M, K, CAP, RO, S = 8, 256, 960, 32, 4, 60
+W = N * M
+PS, ST = 0.0078125, 0.015625
+HB = 2048
+XB = [4096, 5312, 6528, 7744]
+AN = [0, 5056, 6272, 7488]
+LEN = 8704
+REG = W + M
+MW = 68
+HW = M + 64
+F, B, I32, U = "float32", "bfloat16", "int32", "uint16"
+
+SCRATCH = {
+    "L": ("sbuf", [128, LEN], F), "V": ("sbuf", [128, REG + M], B), "TW": ("sbuf", [128, W], B),
+    "MK": ("sbuf", [128, 7680], B), "y": ("sbuf", [128, 1920], B), "wl": ("sbuf", [128, 480], F),
+    "sl": ("sbuf", [128, 120], F), "oh": ("sbuf", [128, 16], F), "ag": ("sbuf", [128, 128], B),
+    "bli": ("sbuf", [128, 480], I32), "blu": ("sbuf", [128, 480], U),
+    "hb": ("sbuf", [128, W], B), "yo": ("sbuf", [128, W], F), "Hw": ("sbuf", [128, 2 * HW], F),
+    "bti": ("sbuf", [128, 480], I32), "btf": ("sbuf", [128, 480], F), "btu": ("sbuf", [128, 480], U),
+    "dn": ("sbuf", [128, 240], F), "wts": ("sbuf", [128, 128], B), "lags": ("sbuf", [128, 128], I32),
+    "tgs": ("sbuf", [128, 240], B), "pre": ("sbuf", [128, 128], B),
+    "c1": ("sbuf", [128, 128], F), "c2": ("sbuf", [128, 128], F), "c3": ("sbuf", [128, 128], F),
+    "c4": ("sbuf", [128, 128], F),
+    "ioi": ("sbuf", [128, 144], I32), "iof": ("sbuf", [128, 144], F), "pci": ("sbuf", [128, 4], I32),
+    "ia": ("sbuf", [128, 256], I32), "col": ("sbuf", [128, 64], F),
+    "Z": ("sbuf", [128, 144], B), "EX": ("sbuf", [128, 6 * 144], B), "CPY": ("sbuf", [128, 128], B),
+    "TA": ("sbuf", [128, W], B), "BO": ("sbuf", [128, 128], B),
+    "BK": ("sbuf", [128, 1024], B), "UU": ("sbuf", [128, 128], B), "u1": ("sbuf", [128, 384], B),
+    "ID": ("sbuf", [128, 1024], B), "I1": ("sbuf", [128, 128], B), "SG": ("sbuf", [128, 128], F),
+    "RP": ("sbuf", [128, 128], B), "Q0": ("sbuf", [128, 256], B), "RST": ("sbuf", [128, 256], B),
+    "OVQ": ("sbuf", [128, 256], B), "stat": ("sbuf", [128, K], B), "c33": ("sbuf", [128, 64], F),
+    "Gr": ("sbuf", [128, K], B),
+    "Gs": ("sbuf", [128, K], B), "Dh": ("sbuf", [128, 480], B), "sel": ("sbuf", [128, 480], B),
+    "Ec": ("sbuf", [128, 64], B), "s1": ("sbuf", [128, 64], F), "nf": ("sbuf", [128, 64], F),
+    "hi": ("sbuf", [128, 480], I32), "dh": ("sbuf", [128, 240], F), "key": ("sbuf", [128, 64], F), "n16": ("sbuf", [128, 64], U),
+    "qb": ("sbuf", [128, 64], F), "gm": ("sbuf", [128, 64], F), "s2": ("sbuf", [128, 64], F),
+    "s3": ("sbuf", [128, 64], F), "of": ("sbuf", [128, 64], F), "o16": ("sbuf", [128, 64], U),
+    "xo": ("sbuf", [128, 256], U), "rq16": ("sbuf", [128, 16], U), "j16": ("sbuf", [128, 16], U),
+    "pr16": ("sbuf", [128, 16], U), "pb16": ("sbuf", [128, 16], U), "ovt": ("sbuf", [128, 256], B),
+    "Gq": ("sbuf", [128, 256], B), "RB": ("sbuf", [128, 256], F),
+    "FL": ("sbuf", [128, 3 * 1024], B), "MSG": ("sbuf", [128, 3 * 4 * MW], F),
+    "RQ": ("sbuf", [128, 3 * 8 * MW], F), "ho": ("sbuf", [128, 32], U), "ht": ("sbuf", [128, 64], F),
+    "AO": ("sbuf", [128, 3 * 256], F), "x": ("sbuf", [128, K], F), "er": ("sbuf", [128, 64], F),
+    "prod": ("sbuf", [128, 480], F), "f16": ("sbuf", [128, 128], U),
+    "rlh": ("sbuf", [128, 256], B), "rlf": ("sbuf", [128, 384], B), "rlq": ("sbuf", [128, 6 * MW], F),
+}
+for _b in range(8):
+    SCRATCH["P%d" % _b] = ("psum", [128, 512], F)
+SEMAPHORES = (["cv", "ca", "cp", "cg", "snt", "hbs", "hbo", "rh"] + ["d%d" % i for i in range(24)]
+              + [n + str(t) for n in ("fs", "fo", "qs", "qo", "an", "rf", "rr") for t in range(4)])
+
+
+def bits_of(es):
+    m = 0
+    for e in es:
+        m |= 1 << e
+    return m
+
+
+def layout(T, topo):
+    cores = list(T.cores)
+    a = [r for r in range(N) if r == 0 or topo.may_write(cores[0], cores[r])]
+    b = [r for r in range(N) if r not in a]
+    rel = []
+    for r in range(N):
+        far = cores[(b if r in a else a)[0]]
+        cs = [c for c in topo.cores_of(cores[r]) if c != cores[r] and topo.may_write(c, far)]
+        cs = [c for c in cs if topo.die(c) == topo.die(cores[r])] + [c for c in cs if topo.die(c) != topo.die(cores[r])]
+        rel.append(cs[:2])
+    return cores, a, b, rel
+
+
+def xfer(topo, src_core, dst_core, es, sem, src, dst):
+    rid, pid = topo.addr(dst_core, src_core)
+    return RemoteDMATransfer(dst_ids=[DstId(rid=rid, pnc=pid)], dma_engine_mask=bits_of(es), remote_sem=sem, src=src, dst=dst)
+
+
+def relay_program(g, core, T, topo, r, k, cores, a, b):
+    mine, other = (a, b) if r in a else (b, a)
+    p = mine.index(r)
+    es = topo.engines(core, cores[other[0]])
+    h = len(es) // 2
+    n = [0]
+
+    def fwd(sem, cnt, rsem, srcs, dst):
+        g.wait_ge(T.sem[sem], cnt)
+        g.remote_dma_fused([xfer(topo, core, cores[other[2 * k + i]], es[h * i:h * i + h], T.sem[rsem], srcs[i], dst)
+                            for i in range(2)], local_sem=T.sem.snt)
+        n[0] += 2 * h
+
+    fwd("rh", 8, "hbo", [T.rlh[:]] * 2, T.hb[:, M * r:M * r + M])
+    for t in range(RO):
+        if t < RO - 1:
+            c = 1024 * t + 128 * (4 + p)
+            fwd("rf%d" % t, 8, "fo%d" % t, [T.rlf[:, 128 * t:128 * t + 128]] * 2, T.FL[:, c:c + 128])
+        if t > 0:
+            c = ((t - 1) * 8 + 4 + p) * MW
+            s = (t - 1) * 2 * MW
+            fwd("rr%d" % t, 8, "qo%d" % t, [T.rlq[:, s + MW * i:s + MW * i + MW] for i in range(2)], T.RQ[:, c:c + MW])
+    g.wait_ge(T.sem.snt, n[0])
+
+
+def rank_program(g, core, T, topo):
+    cores, a, b, rel = layout(T, topo)
+    me = T.rank_of(core)
+    if me is None:
+        for r in range(N):
+            if core in rel[r]:
+                relay_program(g, core, T, topo, r, rel[r].index(core), cores, a, b)
+        return
+    mine, other = (a, b) if me in a else (b, a)
+    pm = mine.index(me)
+    order = [h for p in range(4) for h in (a[p], b[p])]
+    peers = [(pm + i) % 4 for i in (1, 2, 3)]
+    e_off = topo.engines(core, cores[mine[peers[0]]])
+    e_on = [e for e in topo.engines(core, rel[me][0]) if e not in e_off]
+
+    QU = {"v": g.vector, "a": g.scalar, "p": g.tensor, "g": g, "s": g.sync}
+    recs, waited, cnt = {}, {q: {} for q in QU}, {"v": 0, "a": 0, "p": 0, "g": 0, "d": 0, "snt": 0}
+    dtok = []
+
+    def R(name, c0=None, c1=None, step=1, parts=None):
+        if c0 is None:
+            c0, c1 = 0, SCRATCH[name][1][1]
+        p = parts if parts is not None else slice(0, 128)
+        return (T[name][p, c0:c1:step] if step > 1 else T[name][p, c0:c1], [(name, c0, c1)])
+
+    def IX(win, off):
+        return (win[0].indirect(off[0]), win[1] + off[1], win[1])
+
+    def need(q, tok):
+        if waited[q].get(tok[0], 0) < tok[1]:
+            QU[q].wait_ge(T.sem[tok[0]], tok[1])
+            waited[q][tok[0]] = tok[1]
+
+    def deps(q, reads, writes):
+        best = {}
+        for regs, w in ((reads, False), (writes, True)):
+            for name, c0, c1 in regs:
+                ps = SCRATCH[name][0] == "psum"
+                for d0, d1, w0, q0, tok in recs.get(name, []):
+                    if ps and q0 != q:
+                        hit = True
+                    elif ps and q == "p":
+                        hit = False
+                    else:
+                        hit = (w or w0) and c0 < d1 and d0 < c1
+                    if hit and best.get(tok[0], 0) < tok[1]:
+                        best[tok[0]] = tok[1]
+        for s_, c_ in best.items():
+            need(q, (s_, c_))
+
+    def note(q, reads, writes, tok):
+        for name, c0, c1 in writes:
+            recs[name] = [x_ for x_ in recs.get(name, []) if not (c0 <= x_[0] and x_[1] <= c1)] + [(c0, c1, True, q, tok)]
+        for name, c0, c1 in reads:
+            recs[name] = [x_ for x_ in recs.get(name, []) if not (x_[3] == q and not x_[2] and x_[4][0] == tok[0] and c0 <= x_[0] and x_[1] <= c1)] + [(c0, c1, False, q, tok)]
+
+    def op(q, out, ins, fn):
+        reads = [x_ for i_ in ins if isinstance(i_, tuple) for x_ in i_[1]]
+        if len(out) == 3:
+            writes = out[2]
+            reads = reads + [x_ for x_ in out[1] if x_ not in writes]
+        else:
+            writes = out[1]
+        deps(q, reads, writes)
+        cnt[q] += 1
+        fn().then_inc(T.sem["c" + q], 1)
+        note(q, reads, writes, ("c" + q, cnt[q]))
+
+    def val(x_):
+        return x_[0] if isinstance(x_, tuple) else x_
+
+    def cp(out, in_):
+        op("v", out, [in_], lambda: g.vector.tensor_copy(out[0], in_[0]))
+
+    def tt(out, i0, i1, o):
+        op("v", out, [i0, i1], lambda: g.vector.tensor_tensor(out[0], i0[0], i1[0], o))
+
+    def ts(out, i0, s1, o0, s2=None, o1=None):
+        if o1 is None:
+            op("v", out, [i0, s1], lambda: g.vector.tensor_scalar(out[0], i0[0], val(s1), None, o0))
+        else:
+            op("v", out, [i0, s1, s2], lambda: g.vector.tensor_scalar(out[0], i0[0], val(s1), val(s2), o0, o1))
+
+    def red(out, in_):
+        op("v", out, [in_], lambda: g.vector.tensor_reduce(out[0], in_[0], AX.X, OP.add))
+
+    def fill(out, c):
+        op("v", out, [], lambda: g.vector.memset(out[0], c))
+
+    def act(out, in_, func=AF.Identity, bias=0.0, scale=1.0):
+        op("a", out, [in_, bias, scale], lambda: g.scalar.activation(out[0], in_[0], func, bias=val(bias), scale=val(scale)))
+
+    def iota(out, pat, base, cm, small=False):
+        if small:
+            op("g", out, [], lambda: g.iota(out[0], pat, base, cm, allow_small_or_imprecise_dtypes=True))
+        else:
+            op("g", out, [], lambda: g.iota(out[0], pat, base, cm))
+
+    def pick(out, in_, cmp_, c, base=0):
+        op("g", out, [in_], lambda: g.affine_select(out[0], in_[0], [[-1, 128]], cmp_, c, base, 1))
+
+    def mm(lst, start=True, stop=True):
+        reads = [x_ for o_, l_, r_ in lst for x_ in l_[1] + r_[1]]
+        writes = [x_ for o_, l_, r_ in lst for x_ in o_[1]]
+        deps("p", reads, writes)
+        for i_, (o_, l_, r_) in enumerate(lst):
+            ins = g.tensor.matmul(o_[0], l_[0], r_[0], start and i_ == 0, stop and i_ == len(lst) - 1)
+        cnt["p"] += 1
+        ins.then_inc(T.sem.cp, 1)
+        note("p", reads, writes, ("cp", cnt["p"]))
+
+    def dma(q, out, in_):
+        reads = in_[1] if isinstance(in_, tuple) else []
+        writes = out[1] if isinstance(out, tuple) else []
+        deps(q, reads, writes)
+        tok = ("d%d" % cnt["d"], 16)
+        cnt["d"] += 1
+        QU[q].dma_start(val(out), val(in_)).then_inc(T.sem[tok[0]], 16)
+        note("d" + tok[0], reads, writes, tok)
+        dtok.append(tok)
+
+    def send(items):
+        deps("g", [x_ for it in items for x_ in it[3][1]], [])
+        g.remote_dma_fused([xfer(topo, core, d_, es, T.sem[s_], src[0], dst[0]) for d_, es, s_, src, dst in items], local_sem=T.sem.snt)
+        cnt["snt"] += sum(len(it[1]) for it in items)
+
+    def lands(reg, sem, n_):
+        note("r" + sem, [], reg[1], (sem, n_))
+
+    def to_all(src, dst, sems, semr, rdst):
+        send([(rel[me][k], (e_on, e_off)[k], semr, src, rdst) for k in range(2)])
+        to_peers(sems, lambda p: src, dst)
+
+    def to_peers(sem, src, dst):
+        send([(cores[mine[peers[i]]], e_off[4 * i:4 * i + 4], sem, src(peers[i]), dst) for i in range(2)])
+        send([(cores[mine[peers[2]]], e_off, sem, src(peers[2]), dst)])
+
+    def C(i, n_=1):
+        return R("col", i, i + n_)
+
+    def ext(out, qn, src, c0, n_):
+        nm, b0 = ("Z", 0) if qn is None else ("EX", 144 * qn)
+        mm([(out, R(nm, b0 + 15 - i, b0 + 143 - i), R(src, c0 + i, c0 + 16 * n_, 16)) for i in range(16)])
+
+    OLD, NAME, PR, PB, REL, TAG = range(6)
+    RC, GC, PC, G15, OH, W3, MK, WREL, BETA, ALN, AL, AL2, CH, R6, SCX, WND, GSS, GSB, OVS, OVB, RSA, T0 = (
+        0, 1, 2, 3, 4, 12, 15, 18, 19, 20, 21, 22, 24, 32, 33, 34, 35, 36, 40, 44, 48, 50)
+
+    for p in range(4):
+        if p != pm:
+            lands(R("hb", M * mine[p], M * mine[p] + M), "hbs", 16)
+        lands(R("hb", M * other[p], M * other[p] + M), "hbo", 16)
+        for t in range(RO - 1):
+            if p != pm:
+                lands(R("FL", 1024 * t + 128 * p, 1024 * t + 128 * p + 128), "fs%d" % t, 16)
+                lands(R("RQ", (8 * t + p) * MW, (8 * t + p + 1) * MW), "qs%d" % (t + 1), 16)
+                lands(R("L", AN[t + 1] + 64 * p, AN[t + 1] + 64 * p + 64), "an%d" % (t + 1), 16)
+            lands(R("FL", 1024 * t + 128 * (4 + p), 1024 * t + 128 * (5 + p)), "fo%d" % t, 16)
+            lands(R("RQ", (8 * t + 4 + p) * MW, (8 * t + 5 + p) * MW), "qo%d" % (t + 1), 16)
+
+    def init():
+        dma("s", R("wts"), T.wt[:])
+        dma("a", R("bti"), T.bt[:])
+        dma("s", R("lags"), T.lag[:])
+        dma("a", R("hb", M * me, M * me + M), T.e0[:, M * me:M * me + M])
+        dma("s", R("tgs", parts=slice(0, 16)), T.tg[:])
+        iota(R("pci", 0, 1), [[0, 1]], 0, 1)
+        iota(R("ioi"), [[1, 144]], 0, 0)
+        fill(R("V", W, REG), 0.0)
+        fill(R("c33"), 33.0)
+        ts(R("pci", 1, 2), R("pci", 0, 1), 15, OP.bitwise_and)
+        ts(R("pci", 2, 3), R("pci", 0, 1), 112, OP.bitwise_and)
+        cp(C(PC), R("pci", 0, 1))
+        cp(R("iof"), R("ioi"))
+        cp(C(RC, 2), R("pci", 1, 3))
+        ts(R("ia", 0, 128), R("ioi", 0, 128), 112, OP.bitwise_and)
+        ts(R("oh"), R("iof", 0, 16), C(RC), OP.is_equal, 256.0, OP.mult)
+        ts(C(OH, 8), R("iof", 0, 8), C(RC), OP.is_equal)
+        ts(C(G15), C(GC), 15.0, OP.add)
+        ts(R("BO"), R("ia", 0, 128), C(GC), OP.is_equal)
+        act(R("u1", 0, 128), R("BO"), scale=-1.0)
+        pick(R("I1"), R("BO"), OP.is_equal, 0.0)
+        pick(R("u1", 128, 256), R("u1", 0, 128), OP.is_gt, 0.0)
+        pick(R("UU"), R("u1", 128, 256), OP.not_equal, -64.0)
+        to_all(R("hb", M * me, M * me + M), R("hb", M * me, M * me + M), "hbs", "rh", R("rlh"))
+        for i in range(1, 8):
+            pick(R("ID", 128 * i, 128 * i + 128), R("V", W, W + 128), OP.not_equal, 32.0 * i)
+        dma("g", R("L", 0, W), T.e0[:])
+        pick(R("u1", 256, 384), R("BO"), OP.is_equal, 0.0, 6)
+        red(C(BETA), R("col", OH + 1, OH + 6, 2))
+        red(C(ALN), R("col", OH, OH + 6, 2))
+        ts(R("Z"), R("iof"), C(G15), OP.is_equal)
+        for i in range(5):
+            act(R("BK", 128 * i, 128 * i + 128), R("BO"), scale=C(OH + i))
+        ts(R("Q0", 0, 64), R("iof", 0, 64), C(BETA), OP.mult)
+        tt(C(AL), C(ALN), C(OH + 6), OP.add)
+        ts(C(CH, 8), R("iof", 0, 8), C(ALN), OP.mult, 4.0, OP.mult)
+        ts(R("Q0", 64, 128), R("Q0", 0, 64), C(AL), OP.add)
+        ts(C(AL2), C(AL), 2.0, OP.mult)
+        ts(R("Q0", 128, 256), R("Q0", 0, 128), C(AL2), OP.add)
+        cp(R("btu", 0, 120), R("bti", 0, 120))
+        for k in range(16):
+            if k < 6:
+                act(R("TW", 128 * k, 128 * k + 128), R("wts"), scale=R("oh", k, k + 1))
+            else:
+                ts(R("TW", 128 * k, 128 * k + 128), R("wts"), R("oh", k, k + 1), OP.mult)
+        ts(R("bli", 0, 120), R("bti", 0, 120), 127, OP.bitwise_and)
+        cp(R("blu", 0, 120), R("bli", 0, 120))
+        cp(R("btf", 0, 120), R("bti", 0, 120))
+
+    def init2():
+        ts(R("hi", 0, 120), R("bti", 0, 120), 8, OP.arith_shift_right)
+        tt(R("dn", 0, 60), R("btf", 60, 120), R("btf", 0, 60), OP.subtract)
+        tt(R("dh", 0, 60), R("hi", 60, 120), R("hi", 0, 60), OP.subtract)
+        for h in range(N):
+            if h % 2:
+                act(R("V", M * h, M * h + M), R("Q0"), bias=C(CH + h))
+            else:
+                ts(R("V", M * h, M * h + M), R("Q0"), C(CH + h), OP.add)
+        for i in range(5, 8):
+            act(R("BK", 128 * i, 128 * i + 128), R("BO"), scale=C(OH + i))
+
+    def init2b():
+        tt(C(MK, 3), R("col", OH, OH + 6, 2), R("col", OH + 1, OH + 6, 2), OP.add)
+        ts(C(T0 + 5), C(OH + 7), 2.0, OP.mult)
+        ts(C(T0 + 4), C(MK + 1), C(OH + 7), OP.add, -1.0, OP.mult)
+        ts(C(T0 + 6), C(OH + 2), 19.0, OP.mult, C(T0 + 5), OP.add)
+        ts(C(T0 + 7), C(OH + 2), 64.0, OP.mult, C(T0 + 5), OP.add)
+        ts(C(GSS), C(T0 + 4), 1.0, OP.add)
+        ts(C(GSB, 4), R("iof", 0, 4), C(T0 + 6), OP.mult, C(T0 + 7), OP.add)
+
+    def masks(t, n_=2):
+        c, w_ = 120 * t, 120 // n_
+        for i in range(n_):
+            act(R("MK", 16 * (c + w_ * i), 16 * (c + w_ * i + w_)), IX(R("TW"), R("btu", c + w_ * i, c + w_ * i + w_)))
+
+    def weights(t):
+        ext(R("P2", 0, 120), None, "MK", 1920 * t, 120)
+        act(R("wl", 120 * t, 120 * t + 120), R("P2", 0, 120), scale=(1.0 / 256 if t == 0 else 1.0 / 65536))
+
+    def init3():
+        ts(C(T0 + 1, 3), R("col", OH, OH + 6, 2), 64.0, OP.mult)
+        ts(C(WREL), C(OH + 6), 64.0, OP.mult, C(OH + 1), OP.add)
+        ts(R("stat"), R("V", 0, K), C(MK + 1), OP.mult)
+        tt(C(W3, 3), C(T0 + 1, 3), R("col", OH + 1, OH + 6, 2), OP.add)
+
+    def init3b():
+        cp(R("btu", 120, 240), R("bti", 120, 240))
+        ts(C(T0 + 8), C(OH + 6), 4.0, OP.mult)
+        ts(C(T0 + 9), C(OH + 4), 19.0, OP.mult)
+        ts(C(T0 + 10), C(OH + 4), 60.0, OP.mult, C(OH + 7), OP.add)
+        ts(C(RSA), C(OH), 32.0, OP.mult, C(T0 + 8), OP.add)
+        ts(C(OVS), C(MK + 2), -1.0, OP.mult, 1.0, OP.add)
+        ts(C(OVB, 4), R("iof", 0, 4), C(T0 + 9), OP.mult, C(T0 + 10), OP.add)
+        ts(R("RST"), R("Q0"), C(MK), OP.mult, C(RSA), OP.add)
+        ts(C(OVB), C(OH + 4), 32.0, OP.mult, C(OH + 7), OP.add)
+        cp(R("V", REG, REG + M), R("RST"))
+
+    def init4():
+        for qn, c in ((NAME, W3), (TAG, OH + 7), (PR, W3 + 1), (PB, W3 + 2), (REL, WREL)):
+            act(R("EX", 144 * qn, 144 * qn + 144), R("Z"), scale=C(c))
+
+    def init5():
+        ts(R("ia", 128, 256), R("ioi", 0, 128), 15, OP.bitwise_and)
+        ts(R("OVQ"), R("Q0"), C(MK + 2), OP.mult)
+        ts(R("RP"), R("ia", 128, 256), C(RC), OP.is_equal)
+        ts(R("SG"), R("ia", 128, 256), C(RC), OP.is_equal, -PS, OP.mult)
+
+    def init6():
+        cp(R("btu", 240, 480), R("bti", 240, 480))
+        cp(R("btf", 120, 480), R("bti", 120, 480))
+        ts(R("hi", 120, 480), R("bti", 120, 480), 8, OP.arith_shift_right)
+        for t in range(1, RO):
+            tt(R("dh", 60 * t, 60 * t + 60), R("hi", 120 * t + 60, 120 * t + 120), R("hi", 120 * t, 120 * t + 60), OP.subtract)
+            tt(R("dn", 60 * t, 60 * t + 60), R("btf", 120 * t + 60, 120 * t + 120), R("btf", 120 * t, 120 * t + 60), OP.subtract)
+        fill(R("Hw", M, HW), 0.0)
+        fill(R("Hw", HW + M, 2 * HW), 0.0)
+        ts(C(T0), R("oh", 8, 9), R("oh", 9, 10), OP.add, -1.0 / 256, OP.mult)
+        ts(C(T0 + 1), R("oh", 8, 9), 0.25, OP.mult)
+        ts(R("u1", 0, 128), R("u1", 256, 384), C(MK + 1), OP.mult)
+        tt(C(T0 + 2), C(T0), C(GSS), OP.add)
+        ts(C(WND), R("oh", 9, 10), 1.0 / 256, OP.mult, C(T0 + 1), OP.add)
+        ts(R("u1", 128, 256), R("I1"), C(T0 + 2), OP.mult)
+        act(R("EX", 144 * OLD, 144 * OLD + 144), R("Z"), scale=C(WND))
+        tt(R("CPY"), R("u1", 0, 128), R("u1", 128, 256), OP.add)
+
+    def head(t):
+        f0 = 1024 * (t - 1)
+        cp(R("V", REG, REG + M), R("RST"))
+        mm([(R("P0", 0, 128), R("I1"), R("pre"))]
+           + [(R("P0", 0, 128), R("I1"), R("FL", f0 + 128 * p, f0 + 128 * p + 128)) for p in peers], True, False)
+        mm([(R("P0", 0, 128), R("I1"), R("FL", f0 + 128 * p, f0 + 128 * p + 128)) for p in range(4, 8)], False, True)
+        tt(R("ag"), R("P0", 0, 128), R("c2"), OP.max)
+
+    def choice(t, mid=None, end=None):
+        c = 120 * t
+        if t == 0:
+            for c0 in range(0, 120, 20):
+                c1 = c0 + 20
+                tt(R("y", 16 * c0, 16 * c1), IX(R("lags"), R("blu", c0, c1)), R("MK", 16 * c0, 16 * c1), OP.min)
+                if c1 % 60 == 0:
+                    ext(R("P1", c1 - 60, c1), None, "y", 16 * (c1 - 60), 60)
+                if c1 == 100:
+                    weights(0)
+        else:
+            for k in range(16):
+                if k % 3 == 2:
+                    act(R("TA", 128 * k, 128 * k + 128), R("ag"), scale=R("oh", k, k + 1))
+                else:
+                    ts(R("TA", 128 * k, 128 * k + 128), R("ag"), R("oh", k, k + 1), OP.mult)
+            for h in (0, 60):
+                act(R("y", 16 * h, 16 * h + 480), IX(R("TA"), R("btu", c + h, c + h + 30)))
+                cp(R("y", 16 * h + 480, 16 * h + 960), IX(R("TA"), R("btu", c + h + 30, c + h + 60)))
+                ext(R("P1", h, h + 60), None, "y", 16 * h, 60)
+        if mid:
+            mid()
+        k = [R("P4", 64 * i, 64 * i + 60) for i in range(6)]
+        tt(R("sl", 0, 60), R("P1", 0, 60), R("wl", c, c + 60), OP.mult)
+        tt(k[0], R("P1", 60, 120), R("wl", c + 60, c + 120), OP.mult)
+        tt(k[1], k[0], R("sl", 0, 60), OP.is_gt)
+        tt(R("s3", 0, 60), k[0], R("sl", 0, 60), OP.max)
+        tt(k[2], k[1], R("dh", 60 * t, 60 * t + 60), OP.mult)
+        ts(R("gm", 0, 60), R("s3", 0, 60), 4.0, OP.is_lt, 8.0, OP.mult)
+        tt(k[3], k[1], R("dn", 60 * t, 60 * t + 60), OP.mult)
+        tt(k[4], k[2], R("hi", c, c + 60), OP.add)
+        tt(R("nf", 0, 60), k[3], R("btf", c, c + 60), OP.add)
+        tt(R("key", 0, 60), k[4], R("gm", 0, 60), OP.add)
+        cp(R("n16", 0, 60), R("nf", 0, 60))
+        for i in range(8):
+            ts(R("Dh", 60 * i, 60 * i + 60), R("key", 0, 60), float(order[i]), OP.is_equal)
+        act(R("Gr", 0, 480), IX(R("V", 0, W), R("n16", 0, 30)))
+        mm([(R("P2", 0, 60), R("Z", 15 - i, 143 - i), R("Dh", 60 * i, 60 * i + 60)) for i in range(8)])
+        mm([(R("P3", 0, 480), R("UU"), R("Dh"))], True, False)
+        mm([(R("P0", 0, 60), R("ID", 128 * i, 128 * i + 128), R("Dh", 60 * i, 60 * i + 60)) for i in range(1, 8)])
+        if end:
+            end()
+        act(R("Gr", 480, 960), IX(R("V", 0, W), R("n16", 30, 60)))
+
+    def carry(t, h):
+        if t == 0:
+            act(R("Gs", 480 * h, 480 * h + 480), R("Gr", 480 * h, 480 * h + 480), bias=C(GSB + t), scale=C(GSS))
+        else:
+            pb = ("P5", "P7")[h]
+            mm([(R(pb, 0, 480), R("CPY"), R("Gr", 480 * h, 480 * h + 480))])
+            act(R("Gs", 480 * h, 480 * h + 480), R(pb, 0, 480), bias=C(GSB + t))
+
+    def prefix(t, mid=None, end=None):
+        o_, d0, d1 = R("Ec", 0, 60), R("c33", 0, 60), R("P2", 0, 60)
+        op("v", o_, [d0, d1], lambda: g.vector.tensor_tensor_scan(o_[0], d0[0], d1[0], 0.0, OP.min, OP.add))
+        mm([(R("P3", 60 * i, 60 * i + 60), R("BK", 128 * i, 128 * i + 128), R("Ec", 0, 60)) for i in range(8)], False, True)
+        tt(R("s1", 0, 60), R("P0", 0, 60), R("nf", 0, 60), OP.subtract)
+        ts(R("qb", 0, 60), R("s1", 0, 60), float(REG + 63), OP.add)
+        if mid:
+            mid()
+        carry(t, 0)
+        tt(R("sel"), R("P3", 0, 480), R("Dh"), OP.mult)
+        mm([(R("P1", 0, 60), R("I1"), R("sel", 60 * i, 60 * i + 60)) for i in range(8)])
+        carry(t, 1)
+        if end:
+            end()
+        tt(R("P1", 64, 124), R("P1", 0, 60), R("qb", 0, 60), OP.add)
+        ts(R("gm", 0, 60), R("P1", 0, 60), -31.5, OP.is_le)
+        tt(R("P1", 128, 188), R("P1", 64, 124), R("gm", 0, 60), OP.mult)
+        tt(R("of", 0, 60), R("P1", 128, 188), R("nf", 0, 60), OP.add)
+        cp(R("o16", 0, 60), R("of", 0, 60))
+        if t > 0:
+            ext(R("P4", 0, 60), PR, "Gr", 0, 60)
+
+    def scatter(t):
+        tt(IX(R("V"), R("o16", 0, 60)), R("Gs"), R("stat"), OP.add)
+        ext(R("P2", 0, 16), NAME, "V", REG, 16)
+        act(R("ovt"), R("V", REG, REG + M), bias=C(OVB + t), scale=(C(OVS) if t > 0 else 1.0))
+
+    def places(t):
+        o_ = R("xo", 64 * t, 64 * t + 60)
+        if t == 0:
+            ts(R("s2", 0, 60), R("gm", 0, 60), float(HB), OP.mult)
+            tt(R("s3", 0, 60), R("s2", 0, 60), R("nf", 0, 60), OP.add)
+        else:
+            tt(R("s1", 0, 60), R("of", 0, 60), R("P4", 0, 60), OP.subtract)
+            ts(R("s2", 0, 60), R("s1", 0, 60), float(AN[t] - REG), OP.add)
+            tt(R("s1", 0, 60), R("s2", 0, 60), R("gm", 0, 60), OP.mult)
+            tt(R("s3", 0, 60), R("s1", 0, 60), R("P4", 0, 60), OP.add)
+        cp(o_, R("s3", 0, 60))
+
+    def override(t):
+        if t == 0:
+            cp(IX(R("V", 0, REG), R("rq16")), R("ovt"))
+        else:
+            tt(IX(R("V", 0, REG), R("rq16")), R("ovt"), R("OVQ"), OP.add)
+
+    def rel_out(t):
+        ext(R("P3", 0, 16), REL, "V", REG, 16)
+        for p in range(4):
+            c = ((t - 1) * 4 + p) * MW + 64
+            act(R("MSG", c, c + 4), R("P3", 4 * p, 4 * p + 4))
+
+    def flags(t):
+        mm([(R("P0", 0, 128), R("EX", 144 * TAG + 15 - k, 144 * TAG + 143 - k), R("V", 128 * k, 128 * k + 128)) for k in range(16)])
+        if t == 0:
+            places(0)
+            init5()
+        own = R("FL", 1024 * t + 128 * pm, 1024 * t + 128 * pm + 128)
+        ts(own, R("P0", 0, 128), 2 * t + 2.5, OP.is_ge)
+        send([(rel[me][k], (e_on, e_off)[k], "rf%d" % t, own, R("rlf", 128 * t, 128 * t + 128)) for k in range(2)])
+        if t != 1:
+            flags_near(t)
+
+    def flags_near(t):
+        own = R("FL", 1024 * t + 128 * pm, 1024 * t + 128 * pm + 128)
+        to_peers("fs%d" % t, lambda p: own, own)
+
+    def tail(t):
+        cp(R("rq16"), R("P2", 0, 16))
+        if t > 0:
+            ext(R("P1", 0, 16), OLD, "V", REG, 16)
+            ext(R("P2", 0, 16), PB, "V", REG, 16)
+        override(t)
+        if t == 1:
+            pointers()
+            values(1)
+        if t == 2:
+            products(1)
+        flags(t)
+        if t == 2:
+            errors(1)
+        if t > 0:
+            rel_out(t)
+
+    def pointers():
+        cp(R("pb16"), R("P2", 0, 16))
+        cp(R("pr16"), R("P1", 0, 16))
+
+    def state(t):
+        ts(R("c1"), R("P0", 0, 128), 2 * t + 1.5, OP.is_ge, 3.0, OP.mult)
+        ts(R("c3"), R("P0", 0, 128), 2 * t + 2.5, OP.is_ge, -128.0, OP.mult)
+        ts(R("c2"), R("P0", 0, 128), 2 * t + 2.5, OP.is_ge, 3.0, OP.mult)
+        tt(R("c4"), R("c1"), R("lags" if t == 0 else "ag"), OP.add)
+        tt(R("pre"), R("c4"), R("c3"), OP.add)
+
+    def bases(t):
+        act(R("RB"), IX(R("L", 0, XB[t - 1]), R("pb16")))
+
+    def values(t):
+        win = R("L", 0, AN[t])
+        m0 = (t - 1) * 4 * MW
+        if t == 1:
+            bases(t)
+        for p in range(4):
+            tt(R("MSG", m0 + p * MW, m0 + p * MW + 64), IX(win, R("pr16", 4 * p, 4 * p + 4)), R("RB", 64 * p, 64 * p + 64), OP.subtract)
+
+    def request(t):
+        m0 = (t - 1) * 4 * MW
+        s = (t - 1) * 2 * MW
+        send([(rel[me][k], (e_on, e_off)[k], "rr%d" % t, R("MSG", m0 + 2 * k * MW, m0 + (2 * k + 2) * MW), R("rlq", s, s + 2 * MW)) for k in range(2)])
+        if t == 1:
+            flags_near(t)
+        c = ((t - 1) * 8 + pm) * MW
+        to_peers("qs%d" % t, lambda p: R("MSG", m0 + p * MW, m0 + (p + 1) * MW), R("RQ", c, c + MW))
+
+    def adds(t, srcs, alone=False):
+        blk = []
+        for s in srcs:
+            nm, c = ("MSG", ((t - 1) * 4 + s) * MW) if s == pm else ("RQ", ((t - 1) * 8 + s) * MW)
+            cp(R("ho", 4 * s, 4 * s + 4), R(nm, c + 64, c + MW))
+            blk.append((s, nm, c))
+        for s, nm, c in blk:
+            if alone:
+                ws = [IX(R("Hw", HW * h, HW * h + HW), R("ho", 4 * s + 2 * h, 4 * s + 2 * h + 2)) for h in range(2)]
+                for h in range(2):
+                    tt(R("ht", 32 * h, 32 * h + 32), ws[h], R(nm, c + 32 * h, c + 32 * h + 32), OP.add)
+                for h in range(2):
+                    cp(ws[h], R("ht", 32 * h, 32 * h + 32))
+                continue
+            for h in range(2):
+                w_ = IX(R("Hw", HW * h, HW * h + HW), R("ho", 4 * s + 2 * h, 4 * s + 2 * h + 2))
+                act(R("ht", 32 * h, 32 * h + 32), w_)
+                tt(w_, R("ht", 32 * h, 32 * h + 32), R(nm, c + 32 * h, c + 32 * h + 32), OP.add)
+
+    def answer(t):
+        a0 = 256 * (t - 1)
+        for h in range(2):
+            for i, p in enumerate(peers + [pm]):
+                c = a0 + 64 * p + 32 * h
+                w_ = IX(R("Hw", HW * h, HW * h + HW), R("ho", 4 * p + 2 * h, 4 * p + 2 * h + 2))
+                if h == 1 and i < 3 and t == RO - 1:
+                    cp(R("AO", c, c + 32), w_)
+                else:
+                    act(R("AO", c, c + 32), w_)
+        mineslot = R("L", AN[t] + 64 * pm, AN[t] + 64 * pm + 64)
+        to_peers("an%d" % t, lambda p: R("AO", a0 + 64 * p, a0 + 64 * p + 64), mineslot)
+        act(mineslot, R("AO", a0 + 64 * pm, a0 + 64 * pm + 64))
+
+    def step_a(t):
+        products(t)
+        errors(t)
+
+    def products(t):
+        win = R("L", 0, XB[t])
+        c = 64 * t
+        cuts = ((0, 8), (8, 20), (20, 30))
+        for c0, c1 in cuts:
+            act(R("x", 480 + 16 * c0, 480 + 16 * c1), IX(win, R("xo", c + 30 + c0, c + 30 + c1)))
+        for c0, c1 in cuts:
+            tt(R("prod", 16 * c0, 16 * c1), IX(win, R("xo", c + c0, c + c1)), R("x", 480 + 16 * c0, 480 + 16 * c1), OP.mult)
+        act(R("x", 0, 480), IX(win, R("xo", c, c + 30)))
+
+    def errors(t):
+        top = slice(0, 16)
+        mm([(R("P5", 0, 60), R("RP", parts=top), R("tgs", 60 * t, 60 * t + 60, parts=top))], True, False)
+        for k0, k1 in ((0, 2), (2, 5), (5, 8)):
+            mm([(R("P5", 0, 60), R("SG"), R("prod", 60 * k, 60 * k + 60)) for k in range(k0, k1)], False, k1 == 8)
+        act(R("er", 0, 60), R("P5", 0, 60), AF.Tanh)
+        act(R("P6", 0, 60), R("er", 0, 60), scale=ST)
+
+    def step_b(t, h):
+        for k in range(8):
+            c = 480 * (1 - h) + 60 * k
+            tt(R("P7", 60 * k, 60 * k + 60), R("P6", 0, 60), R("x", c, c + 60), OP.mult)
+        tt(R("L", XB[t] + 480 * h, XB[t] + 480 * h + 480), R("P7", 0, 480), R("x", 480 * h, 480 * h + 480), OP.add)
+
+    init()
+    masks(0, 6)
+    choice(0, init2, init2b)
+    prefix(0, init3, init3b)
+    init4()
+    masks(1)
+    scatter(0)
+    act(R("L", HB, HB + W), R("hb"))
+    act(R("P6", 0, 8), R("iof", 0, 8), AF.Tanh)
+    tail(0)
+    step_a(0)
+    weights(1)
+    state(0)
+    init6()
+    for s in range(2):
+        h = order[2 * pm + s]
+        act(R("Hw", HW * s, HW * s + M), R("hb", M * h, M * h + M))
+    step_b(0, 0)
+    step_b(0, 1)
+
+    head(1)
+    choice(1)
+    prefix(1)
+    masks(2)
+    scatter(1)
+    tail(1)
+    request(1)
+    weights(2)
+    state(1)
+    places(1)
+    adds(1, [pm])
+
+    def add1(t, srcs, last=False):
+        def run():
+            adds(t, srcs, srcs[0] > 3)
+            if last:
+                answer(t)
+        return run
+
+    head(2)
+    choice(2, add1(1, peers), add1(1, [4]))
+    prefix(2, add1(1, [5]), add1(1, [6, 7], True))
+    masks(3)
+    scatter(2)
+    tail(2)
+    pointers()
+    bases(2)
+    state(2)
+    weights(3)
+    step_b(1, 0)
+    step_b(1, 1)
+    values(2)
+    request(2)
+    places(2)
+    adds(2, [pm])
+
+    head(3)
+    choice(3, add1(2, peers), add1(2, [4]))
+    prefix(3, add1(2, [5, 6, 7], True))
+    scatter(3)
+    ext(R("P1", 0, 16), OLD, "V", REG, 16)
+    products(2)
+    cp(R("rq16"), R("P2", 0, 16))
+    errors(2)
+    ext(R("P2", 0, 16), PB, "V", REG, 16)
+    rel_out(3)
+    pointers()
+    bases(3)
+    step_b(2, 0)
+    step_b(2, 1)
+    values(3)
+    request(3)
+    override(3)
+    places(3)
+    ext(R("P0", 0, 128), PR, "V", 0, 128)
+    adds(3, [pm])
+    cp(R("f16"), R("P0", 0, 128))
+    adds(3, peers)
+    adds(3, range(4, 8))
+    answer(3)
+    side = 0 if me in a else 1
+    dma("s", T.yh[:], R("Hw", HW * side, HW * side + M))
+    step_a(3)
+    step_b(3, 0)
+    step_b(3, 1)
+    for i in range(8):
+        o_, w_ = R("yo", 256 * i, 256 * i + 256), IX(R("L"), R("f16", 16 * i, 16 * i + 16))
+        if i % 2 == 0:
+            act(o_, w_)
+        else:
+            cp(o_, w_)
+            dma("s", T.yr[:, 256 * i - 256:256 * i + 256], R("yo", 256 * i - 256, 256 * i + 256))
+    for tok in dtok:
+        need("g", tok)
+    for q in "vapg":
+        need("g", ("c" + q, cnt[q]))
+    g.wait_ge(T.sem.snt, cnt["snt"])

@@ -1,56 +1,58 @@
 from concourse.bass import DstId, RemoteDMATransfer
-from concourse.mybir import AluOpType as OP, AxisListType as AX, ActivationFunctionType as AF
+from concourse.mybir import AluOpType as OP, ActivationFunctionType as AF
 
 N, M, K, CAP, RO, S = 8, 256, 960, 32, 4, 60
 W = N * M
 PS, ST = 0.0078125, 0.015625
-HB = 2048
-XB = [4096, 5312, 6528, 7744]
-AN = [0, 5056, 6272, 7488]
-LEN = 8704
-REG = W + M
+AN = [W + (M + K) * t for t in range(RO)]
+XB = [a_ + M for a_ in AN]
+LEN = XB[-1] + K
 MW = 68
-HW = M + 64
+HW = 2 * M + 64
+ROUND = 3221225472.0
+FAR = 65536.0
+SLOTS = (1, 0, 3, 2)
+ORDER = (("f", 0), ("f", 1), ("r", 1), ("f", 2), ("r", 2), ("r", 3))
 F, B, I32, U = "float32", "bfloat16", "int32", "uint16"
 
 SCRATCH = {
-    "L": ("sbuf", [128, LEN], F), "V": ("sbuf", [128, REG + M], B), "TW": ("sbuf", [128, W], B),
-    "MK": ("sbuf", [128, 7680], B), "y": ("sbuf", [128, 1920], B), "wl": ("sbuf", [128, 480], F),
-    "sl": ("sbuf", [128, 120], F), "oh": ("sbuf", [128, 16], F), "ag": ("sbuf", [128, 128], B),
-    "bli": ("sbuf", [128, 480], I32), "blu": ("sbuf", [128, 480], U),
-    "hb": ("sbuf", [128, W], B), "yo": ("sbuf", [128, W], F), "Hw": ("sbuf", [128, 2 * HW], F),
-    "bti": ("sbuf", [128, 480], I32), "btf": ("sbuf", [128, 480], F), "btu": ("sbuf", [128, 480], U),
-    "dn": ("sbuf", [128, 240], F), "wts": ("sbuf", [128, 128], B), "lags": ("sbuf", [128, 128], I32),
-    "tgs": ("sbuf", [128, 240], B), "pre": ("sbuf", [128, 128], B),
-    "c1": ("sbuf", [128, 128], F), "c2": ("sbuf", [128, 128], F), "c3": ("sbuf", [128, 128], F),
-    "c4": ("sbuf", [128, 128], F),
+    "L": ("sbuf", [128, LEN], F), "V": ("sbuf", [128, XB[-1]], B), "TW": ("sbuf", [128, W], B),
+    "MK": ("sbuf", [128, 1920], B), "y": ("sbuf", [128, 1920], B), "wl": ("sbuf", [128, 480], F),
+    "sl": ("sbuf", [128, 64], F), "oh": ("sbuf", [128, 16], F), "o8": ("sbuf", [128, 8], F),
+    "ag": ("sbuf", [128, 128], B), "rr": ("sbuf", [128, 128], B), "c2": ("sbuf", [128, 128], F),
+    "hb": ("sbuf", [128, W + M], B), "yo": ("sbuf", [128, W], F), "HA": ("sbuf", [128, HW], F),
+    "HB": ("sbuf", [128, HW], F), "yq": ("sbuf", [128, M], F),
+    "bti": ("sbuf", [128, 480], I32), "btu": ("sbuf", [128, 480], U),
+    "ws": ("sbuf", [128, M], B), "ls": ("sbuf", [128, M], I32), "wg": ("sbuf", [128, M], B),
+    "lags": ("sbuf", [128, 128], I32), "tgs": ("sbuf", [128, 240], B),
     "ioi": ("sbuf", [128, 144], I32), "iof": ("sbuf", [128, 144], F), "pci": ("sbuf", [128, 4], I32),
     "ia": ("sbuf", [128, 256], I32), "col": ("sbuf", [128, 64], F),
-    "Z": ("sbuf", [128, 144], B), "EX": ("sbuf", [128, 6 * 144], B), "CPY": ("sbuf", [128, 128], B),
+    "Z": ("sbuf", [128, 144], B), "EX": ("sbuf", [128, 8 * 144], B), "CPY": ("sbuf", [128, 128], B),
     "TA": ("sbuf", [128, W], B), "BO": ("sbuf", [128, 128], B),
-    "BK": ("sbuf", [128, 1024], B), "UU": ("sbuf", [128, 128], B), "u1": ("sbuf", [128, 384], B),
-    "ID": ("sbuf", [128, 1024], B), "I1": ("sbuf", [128, 128], B), "SG": ("sbuf", [128, 128], F),
-    "RP": ("sbuf", [128, 128], B), "Q0": ("sbuf", [128, 256], B), "RST": ("sbuf", [128, 256], B),
+    "BK": ("sbuf", [128, 1024], B), "UU": ("sbuf", [128, 128], B), "u1": ("sbuf", [128, 512], B),
+    "I1": ("sbuf", [128, 384], B), "SG": ("sbuf", [128, 128], F),
+    "RP": ("sbuf", [128, 128], B), "Q0": ("sbuf", [128, 256], B),
     "OVQ": ("sbuf", [128, 256], B), "stat": ("sbuf", [128, K], B), "c33": ("sbuf", [128, 64], F),
-    "Gr": ("sbuf", [128, K], B),
-    "Gs": ("sbuf", [128, K], B), "Dh": ("sbuf", [128, 480], B), "sel": ("sbuf", [128, 480], B),
-    "Ec": ("sbuf", [128, 64], B), "s1": ("sbuf", [128, 64], F), "nf": ("sbuf", [128, 64], F),
-    "hi": ("sbuf", [128, 480], I32), "dh": ("sbuf", [128, 240], F), "key": ("sbuf", [128, 64], F), "n16": ("sbuf", [128, 64], U),
-    "qb": ("sbuf", [128, 64], F), "gm": ("sbuf", [128, 64], F), "s2": ("sbuf", [128, 64], F),
-    "s3": ("sbuf", [128, 64], F), "of": ("sbuf", [128, 64], F), "o16": ("sbuf", [128, 64], U),
-    "xo": ("sbuf", [128, 256], U), "rq16": ("sbuf", [128, 16], U), "j16": ("sbuf", [128, 16], U),
-    "pr16": ("sbuf", [128, 16], U), "pb16": ("sbuf", [128, 16], U), "ovt": ("sbuf", [128, 256], B),
-    "Gq": ("sbuf", [128, 256], B), "RB": ("sbuf", [128, 256], F),
+    "Gr": ("sbuf", [128, K], B), "Gs": ("sbuf", [128, K], B), "Dh": ("sbuf", [128, 480], B),
+    "D8": ("sbuf", [128, 480], B), "vv": ("sbuf", [128, 480], F),
+    "T0": ("sbuf", [128, 180], F), "NT": ("sbuf", [128, 720], F), "F1": ("sbuf", [128, 180], F),
+    "FO": ("sbuf", [128, 180], F),
+    "Ec": ("sbuf", [128, 64], B), "key": ("sbuf", [128, 64], F), "n16": ("sbuf", [128, 64], U),
+    "qb": ("sbuf", [128, 64], F), "thr": ("sbuf", [128, 64], F), "s3": ("sbuf", [128, 64], F),
+    "o16": ("sbuf", [128, 256], U), "xo": ("sbuf", [128, 256], U), "rq16": ("sbuf", [128, 16], U),
+    "X4": ("sbuf", [128, 4 * M], B), "pb16": ("sbuf", [128, 32], U), "ovt": ("sbuf", [128, 256], B),
+    "RB": ("sbuf", [128, 256], F),
     "FL": ("sbuf", [128, 3 * 1024], B), "MSG": ("sbuf", [128, 3 * 4 * MW], F),
-    "RQ": ("sbuf", [128, 3 * 8 * MW], F), "ho": ("sbuf", [128, 32], U), "ht": ("sbuf", [128, 64], F),
+    "RQ": ("sbuf", [128, 3 * 8 * MW], F), "ho": ("sbuf", [128, 32], U), "ht": ("sbuf", [128, 128], F),
+    "at": ("sbuf", [128, 256], F),
     "AO": ("sbuf", [128, 3 * 256], F), "x": ("sbuf", [128, K], F), "er": ("sbuf", [128, 64], F),
     "prod": ("sbuf", [128, 480], F), "f16": ("sbuf", [128, 128], U),
     "rlh": ("sbuf", [128, 256], B), "rlf": ("sbuf", [128, 384], B), "rlq": ("sbuf", [128, 6 * MW], F),
 }
 for _b in range(8):
     SCRATCH["P%d" % _b] = ("psum", [128, 512], F)
-SEMAPHORES = (["cv", "ca", "cp", "cg", "snt", "hbs", "hbo", "rh"] + ["d%d" % i for i in range(24)]
-              + [n + str(t) for n in ("fs", "fo", "qs", "qo", "an", "rf", "rr") for t in range(4)])
+SEMAPHORES = (["cv", "ca", "cp", "cg", "snt", "hbl", "rh"] + ["d%d" % i for i in range(24)]
+              + [n + str(t) for n in ("fs", "fo", "qa", "qb", "qc", "qd", "an", "rf", "rr") for t in range(4)])
 
 
 def bits_of(es):
@@ -64,18 +66,26 @@ def layout(T, topo):
     cores = list(T.cores)
     a = [r for r in range(N) if r == 0 or topo.may_write(cores[0], cores[r])]
     b = [r for r in range(N) if r not in a]
+    assert all(sorted((a[p], b[p])) == [2 * p, 2 * p + 1] for p in range(4))
     rel = []
     for r in range(N):
         far = cores[(b if r in a else a)[0]]
         cs = [c for c in topo.cores_of(cores[r]) if c != cores[r] and topo.may_write(c, far)]
-        cs = [c for c in cs if topo.die(c) == topo.die(cores[r])] + [c for c in cs if topo.die(c) != topo.die(cores[r])]
-        rel.append(cs[:2])
+        rel.append([c for c in cs if topo.die(c) == topo.die(cores[r])] + [c for c in cs if topo.die(c) != topo.die(cores[r])])
     return cores, a, b, rel
 
 
 def xfer(topo, src_core, dst_core, es, sem, src, dst):
-    rid, pid = topo.addr(dst_core, src_core)
-    return RemoteDMATransfer(dst_ids=[DstId(rid=rid, pnc=pid)], dma_engine_mask=bits_of(es), remote_sem=sem, src=src, dst=dst)
+    to = [topo.addr(d_, src_core) for d_ in (dst_core if isinstance(dst_core, list) else [dst_core])]
+    return RemoteDMATransfer(dst_ids=[DstId(rid=rid, pnc=pid) for rid, pid in to], dma_engine_mask=bits_of(es), remote_sem=sem,
+                             srcs=[src], dsts=[dst] * len(to))
+
+
+def targets(k, mine, other, p):
+    near = [mine[(p + i) % 4] for i in (1, 2, 3)]
+    if k < 2:
+        return [(other[(p + 2 * k) % 4], 4), (other[(p + 2 * k + 1) % 4], 4)]
+    return [(near[0], 4), (near[1], 4)] if k == 2 else [(near[2], 8)]
 
 
 def relay_program(g, core, T, topo, r, k, cores, a, b):
@@ -85,21 +95,34 @@ def relay_program(g, core, T, topo, r, k, cores, a, b):
     h = len(es) // 2
     n = [0]
 
-    def fwd(sem, cnt, rsem, srcs, dst):
+    def spread(sem, cnt, rsem, src, dst):
         g.wait_ge(T.sem[sem], cnt)
-        g.remote_dma_fused([xfer(topo, core, cores[other[2 * k + i]], es[h * i:h * i + h], T.sem[rsem], srcs[i], dst)
-                            for i in range(2)], local_sem=T.sem.snt)
+        trs, e0_ = [], 0
+        for d_, n_ in targets(k, mine, other, p):
+            trs.append(xfer(topo, core, cores[d_], es[e0_:e0_ + n_], T.sem[rsem], src, dst))
+            e0_ += n_
+        g.remote_dma_fused(trs, local_sem=T.sem.snt)
+        n[0] += e0_
+
+    def flags(t):
+        c = 1024 * t + 128 * (4 + p if k < 2 else p)
+        spread("rf%d" % t, 8, "fo%d" % t, T.rlf[:, 128 * t:128 * t + 128], T.FL[:, c:c + 128])
+
+    def requests(t):
+        s = (t - 1) * 2 * MW
+        to = [(p - 1 - SLOTS[2 * k + i]) % 4 for i in range(2)]
+        cs = [((t - 1) * 8 + 4 + SLOTS[2 * k + i]) * MW for i in range(2)]
+        g.wait_ge(T.sem["rr%d" % t], 8)
+        g.remote_dma_fused([xfer(topo, core, cores[other[to[i]]], es[h * i:h * i + h], T.sem[("qc%d", "qd%d")[k] % t],
+                                 T.rlq[:, s + MW * i:s + MW * i + MW], T.RQ[:, cs[i]:cs[i] + MW]) for i in range(2)], local_sem=T.sem.snt)
         n[0] += 2 * h
 
-    fwd("rh", 8, "hbo", [T.rlh[:]] * 2, T.hb[:, M * r:M * r + M])
-    for t in range(RO):
-        if t < RO - 1:
-            c = 1024 * t + 128 * (4 + p)
-            fwd("rf%d" % t, 8, "fo%d" % t, [T.rlf[:, 128 * t:128 * t + 128]] * 2, T.FL[:, c:c + 128])
-        if t > 0:
-            c = ((t - 1) * 8 + 4 + p) * MW
-            s = (t - 1) * 2 * MW
-            fwd("rr%d" % t, 8, "qo%d" % t, [T.rlq[:, s + MW * i:s + MW * i + MW] for i in range(2)], T.RQ[:, c:c + MW])
+    spread("rh", 4, "hbl", T.rlh[:], T.hb[:, M * r:M * r + M])
+    for kind, t in ORDER:
+        if kind == "f":
+            flags(t)
+        elif k < 2:
+            requests(t)
     g.wait_ge(T.sem.snt, n[0])
 
 
@@ -113,8 +136,8 @@ def rank_program(g, core, T, topo):
         return
     mine, other = (a, b) if me in a else (b, a)
     pm = mine.index(me)
-    order = [h for p in range(4) for h in (a[p], b[p])]
-    peers = [(pm + i) % 4 for i in (1, 2, 3)]
+    peers = [(pm + i) % 4 for i in (3, 2, 1)]
+    asker = [(pm + 1 + i) % 4 for i in range(4)]
     e_off = topo.engines(core, cores[mine[peers[0]]])
     e_on = [e for e in topo.engines(core, rel[me][0]) if e not in e_off]
 
@@ -126,7 +149,7 @@ def rank_program(g, core, T, topo):
         if c0 is None:
             c0, c1 = 0, SCRATCH[name][1][1]
         p = parts if parts is not None else slice(0, 128)
-        return (T[name][p, c0:c1:step] if step > 1 else T[name][p, c0:c1], [(name, c0, c1)])
+        return (T[name][p, c0:c1:step] if step > 1 else T[name][p, c0:c1], [(name, c0, c1, step)])
 
     def IX(win, off):
         return (win[0].indirect(off[0]), win[1] + off[1], win[1])
@@ -139,25 +162,28 @@ def rank_program(g, core, T, topo):
     def deps(q, reads, writes):
         best = {}
         for regs, w in ((reads, False), (writes, True)):
-            for name, c0, c1 in regs:
+            for name, c0, c1, st in regs:
                 ps = SCRATCH[name][0] == "psum"
-                for d0, d1, w0, q0, tok in recs.get(name, []):
+                for d0, d1, w0, q0, tok, s0 in recs.get(name, []):
                     if ps and q0 != q:
                         hit = True
                     elif ps and q == "p":
                         hit = False
                     else:
-                        hit = (w or w0) and c0 < d1 and d0 < c1
+                        hit = (w or w0) and c0 < d1 and d0 < c1 and (st != s0 or (c0 - d0) % st == 0)
                     if hit and best.get(tok[0], 0) < tok[1]:
                         best[tok[0]] = tok[1]
         for s_, c_ in best.items():
             need(q, (s_, c_))
 
     def note(q, reads, writes, tok):
-        for name, c0, c1 in writes:
-            recs[name] = [x_ for x_ in recs.get(name, []) if not (c0 <= x_[0] and x_[1] <= c1)] + [(c0, c1, True, q, tok)]
-        for name, c0, c1 in reads:
-            recs[name] = [x_ for x_ in recs.get(name, []) if not (x_[3] == q and not x_[2] and x_[4][0] == tok[0] and c0 <= x_[0] and x_[1] <= c1)] + [(c0, c1, False, q, tok)]
+        def covers(c0, c1, st, x_):
+            return c0 <= x_[0] and x_[1] <= c1 and (st == 1 or (st == x_[5] and (x_[0] - c0) % st == 0))
+
+        for name, c0, c1, st in writes:
+            recs[name] = [x_ for x_ in recs.get(name, []) if not covers(c0, c1, st, x_)] + [(c0, c1, True, q, tok, st)]
+        for name, c0, c1, st in reads:
+            recs[name] = [x_ for x_ in recs.get(name, []) if not (x_[3] == q and not x_[2] and x_[4][0] == tok[0] and covers(c0, c1, st, x_))] + [(c0, c1, False, q, tok, st)]
 
     def op(q, out, ins, fn):
         reads = [x_ for i_ in ins if isinstance(i_, tuple) for x_ in i_[1]]
@@ -186,8 +212,8 @@ def rank_program(g, core, T, topo):
         else:
             op("v", out, [i0, s1, s2], lambda: g.vector.tensor_scalar(out[0], i0[0], val(s1), val(s2), o0, o1))
 
-    def red(out, in_):
-        op("v", out, [in_], lambda: g.vector.tensor_reduce(out[0], in_[0], AX.X, OP.add))
+    def scan(out, d0, d1, init_, o0, o1):
+        op("v", out, [d0, d1, init_], lambda: g.vector.tensor_tensor_scan(out[0], d0[0], d1[0], val(init_), o0, o1))
 
     def fill(out, c):
         op("v", out, [], lambda: g.vector.memset(out[0], c))
@@ -195,21 +221,18 @@ def rank_program(g, core, T, topo):
     def act(out, in_, func=AF.Identity, bias=0.0, scale=1.0):
         op("a", out, [in_, bias, scale], lambda: g.scalar.activation(out[0], in_[0], func, bias=val(bias), scale=val(scale)))
 
-    def iota(out, pat, base, cm, small=False):
-        if small:
-            op("g", out, [], lambda: g.iota(out[0], pat, base, cm, allow_small_or_imprecise_dtypes=True))
-        else:
-            op("g", out, [], lambda: g.iota(out[0], pat, base, cm))
+    def iota(out, pat, base, cm):
+        op("g", out, [], lambda: g.iota(out[0], pat, base, cm))
 
     def pick(out, in_, cmp_, c, base=0):
         op("g", out, [in_], lambda: g.affine_select(out[0], in_[0], [[-1, 128]], cmp_, c, base, 1))
 
-    def mm(lst, start=True, stop=True):
+    def mm(lst, start=True, stop=True, each=False):
         reads = [x_ for o_, l_, r_ in lst for x_ in l_[1] + r_[1]]
         writes = [x_ for o_, l_, r_ in lst for x_ in o_[1]]
         deps("p", reads, writes)
         for i_, (o_, l_, r_) in enumerate(lst):
-            ins = g.tensor.matmul(o_[0], l_[0], r_[0], start and i_ == 0, stop and i_ == len(lst) - 1)
+            ins = g.tensor.matmul(o_[0], l_[0], r_[0], each or (start and i_ == 0), each or (stop and i_ == len(lst) - 1))
         cnt["p"] += 1
         ins.then_inc(T.sem.cp, 1)
         note("p", reads, writes, ("cp", cnt["p"]))
@@ -232,490 +255,455 @@ def rank_program(g, core, T, topo):
     def lands(reg, sem, n_):
         note("r" + sem, [], reg[1], (sem, n_))
 
-    def to_all(src, dst, sems, semr, rdst):
-        send([(rel[me][k], (e_on, e_off)[k], semr, src, rdst) for k in range(2)])
-        to_peers(sems, lambda p: src, dst)
-
-    def to_peers(sem, src, dst):
-        send([(cores[mine[peers[i]]], e_off[4 * i:4 * i + 4], sem, src(peers[i]), dst) for i in range(2)])
-        send([(cores[mine[peers[2]]], e_off, sem, src(peers[2]), dst)])
+    def to_peers(sems, to, src, dst):
+        send([(cores[mine[to[i]]], e_off[4 * i:4 * i + 4], sems[0], src(i), dst(i)) for i in range(2)])
+        send([(cores[mine[to[2]]], e_off, sems[1], src(2), dst(2))])
 
     def C(i, n_=1):
         return R("col", i, i + n_)
+
+    def OH(i):
+        return R("oh", i, i + 1)
+
+    def O8(i):
+        return R("o8", i, i + 1)
 
     def ext(out, qn, src, c0, n_):
         nm, b0 = ("Z", 0) if qn is None else ("EX", 144 * qn)
         mm([(out, R(nm, b0 + 15 - i, b0 + 143 - i), R(src, c0 + i, c0 + 16 * n_, 16)) for i in range(16)])
 
-    OLD, NAME, PR, PB, REL, TAG = range(6)
-    RC, GC, PC, G15, OH, W3, MK, WREL, BETA, ALN, AL, AL2, CH, R6, SCX, WND, GSS, GSB, OVS, OVB, RSA, T0 = (
-        0, 1, 2, 3, 4, 12, 15, 18, 19, 20, 21, 22, 24, 32, 33, 34, 35, 36, 40, 44, 48, 50)
+    WGT, LAG, NAME, TAG, PR, PB, OLD, REL = range(8)
+    RC, GC, OD, EV, G15, AL2, W8, BKS, GSS, GSB, OVS, OVB, RSS, RSB, A4, WREL, CM, RRB, T0 = (
+        0, 1, 2, 3, 4, 5, 6, 14, 22, 23, 27, 28, 32, 33, 34, 37, 38, 39, 44)
 
-    for p in range(4):
-        if p != pm:
-            lands(R("hb", M * mine[p], M * mine[p] + M), "hbs", 16)
-        lands(R("hb", M * other[p], M * other[p] + M), "hbo", 16)
-        for t in range(RO - 1):
+    for r in range(N):
+        if r != me:
+            lands(R("hb", M * r, M * r + M), "hbl", 32)
+    for t in range(RO - 1):
+        for p in range(4):
             if p != pm:
-                lands(R("FL", 1024 * t + 128 * p, 1024 * t + 128 * p + 128), "fs%d" % t, 16)
-                lands(R("RQ", (8 * t + p) * MW, (8 * t + p + 1) * MW), "qs%d" % (t + 1), 16)
+                lands(R("FL", 1024 * t + 128 * p, 1024 * t + 128 * p + 128), "fo%d" % t, 32)
                 lands(R("L", AN[t + 1] + 64 * p, AN[t + 1] + 64 * p + 64), "an%d" % (t + 1), 16)
-            lands(R("FL", 1024 * t + 128 * (4 + p), 1024 * t + 128 * (5 + p)), "fo%d" % t, 16)
-            lands(R("RQ", (8 * t + 4 + p) * MW, (8 * t + 5 + p) * MW), "qo%d" % (t + 1), 16)
+            lands(R("FL", 1024 * t + 128 * (4 + p), 1024 * t + 128 * (5 + p)), "fo%d" % t, 32)
+        for s, q_ in ((0, "qa"), (1, "qa"), (2, "qb"), (4, "qc"), (5, "qc"), (6, "qd"), (7, "qd")):
+            lands(R("RQ", (8 * t + s) * MW, (8 * t + s + 1) * MW), q_ + str(t + 1), 8)
+
+    def exsel(qn, c):
+        act(R("EX", 144 * qn, 144 * qn + 144), R("Z"), scale=c)
+
+    def pairs(t):
+        c = 120 * t
+        tt(R("NT", 180 * t, 180 * t + 180, 3), R("bti", c + 60, c + 120), R("bti", c, c + 60), OP.subtract)
+        cp(R("NT", 180 * t + 1, 180 * t + 180, 3), R("bti", c, c + 60))
+
+    def region(t):
+        act(R("V", AN[t], XB[t]), R("Q0"), bias=C(RSB), scale=C(RSS))
 
     def init():
-        dma("s", R("wts"), T.wt[:])
-        dma("a", R("bti"), T.bt[:])
-        dma("s", R("lags"), T.lag[:])
+        fill(R("ws"), 0.0)
+        fill(R("ls"), 0)
+        dma("a", R("bti", 0, 120), T.bt[:, 0:120])
+        dma("s", R("ws", parts=slice(0, 128, 2)), T.wt[:])
+        dma("s", R("ls", parts=slice(1, 128, 2)), T.lag[:])
         dma("a", R("hb", M * me, M * me + M), T.e0[:, M * me:M * me + M])
+        dma("s", R("bti", 120, 480), T.bt[:, 120:480])
+        dma("s", R("lags"), T.lag[:])
         dma("s", R("tgs", parts=slice(0, 16)), T.tg[:])
         iota(R("pci", 0, 1), [[0, 1]], 0, 1)
         iota(R("ioi"), [[1, 144]], 0, 0)
-        fill(R("V", W, REG), 0.0)
-        fill(R("c33"), 33.0)
+        fill(R("T0"), 1.0)
         ts(R("pci", 1, 2), R("pci", 0, 1), 15, OP.bitwise_and)
         ts(R("pci", 2, 3), R("pci", 0, 1), 112, OP.bitwise_and)
-        cp(C(PC), R("pci", 0, 1))
+        ts(R("pci", 3, 4), R("pci", 0, 1), 1, OP.bitwise_and)
         cp(R("iof"), R("ioi"))
-        cp(C(RC, 2), R("pci", 1, 3))
+        cp(C(RC, 3), R("pci", 1, 4))
         ts(R("ia", 0, 128), R("ioi", 0, 128), 112, OP.bitwise_and)
-        ts(R("oh"), R("iof", 0, 16), C(RC), OP.is_equal, 256.0, OP.mult)
-        ts(C(OH, 8), R("iof", 0, 8), C(RC), OP.is_equal)
-        ts(C(G15), C(GC), 15.0, OP.add)
+        ts(R("oh"), R("iof", 0, 16), C(RC), OP.is_equal)
+        act(C(EV), C(OD), scale=-1.0, bias=1.0)
+        act(C(G15), C(GC), bias=15.0)
+        act(R("Q0", 0, 64), R("iof", 0, 64), scale=C(OD))
+        act(C(AL2), C(EV), scale=2.0)
+        act(C(T0 + 8, 8), R("iof", 0, 8), scale=32.0, bias=-1.0)
+        act(R("Q0", 64, 128), R("Q0", 0, 64), bias=C(EV))
+        act(C(A4), C(EV), scale=4.0)
+        act(C(T0 + 16), OH(10), scale=-1.0, bias=C(EV))
+        act(R("Q0", 128, 256), R("Q0", 0, 128), bias=C(AL2))
         ts(R("BO"), R("ia", 0, 128), C(GC), OP.is_equal)
-        act(R("u1", 0, 128), R("BO"), scale=-1.0)
-        pick(R("I1"), R("BO"), OP.is_equal, 0.0)
-        pick(R("u1", 128, 256), R("u1", 0, 128), OP.is_gt, 0.0)
-        pick(R("UU"), R("u1", 128, 256), OP.not_equal, -64.0)
-        to_all(R("hb", M * me, M * me + M), R("hb", M * me, M * me + M), "hbs", "rh", R("rlh"))
-        for i in range(1, 8):
-            pick(R("ID", 128 * i, 128 * i + 128), R("V", W, W + 128), OP.not_equal, 32.0 * i)
-        dma("g", R("L", 0, W), T.e0[:])
-        pick(R("u1", 256, 384), R("BO"), OP.is_equal, 0.0, 6)
-        red(C(BETA), R("col", OH + 1, OH + 6, 2))
-        red(C(ALN), R("col", OH, OH + 6, 2))
+        tt(R("o8"), R("oh", 0, 16, 2), R("oh", 1, 16, 2), OP.add)
         ts(R("Z"), R("iof"), C(G15), OP.is_equal)
-        for i in range(5):
-            act(R("BK", 128 * i, 128 * i + 128), R("BO"), scale=C(OH + i))
-        ts(R("Q0", 0, 64), R("iof", 0, 64), C(BETA), OP.mult)
-        tt(C(AL), C(ALN), C(OH + 6), OP.add)
-        ts(C(CH, 8), R("iof", 0, 8), C(ALN), OP.mult, 4.0, OP.mult)
-        ts(R("Q0", 64, 128), R("Q0", 0, 64), C(AL), OP.add)
-        ts(C(AL2), C(AL), 2.0, OP.mult)
-        ts(R("Q0", 128, 256), R("Q0", 0, 128), C(AL2), OP.add)
+        pick(R("u1", 128, 256), R("BO"), OP.is_gt, 0.0)
+        pick(R("u1", 0, 128), R("u1", 128, 256), OP.not_equal, 1024.0)
+        fill(R("D8"), 0.0)
+        ts(C(T0, 8), R("oh", 0, 16, 2), 64.0, OP.mult)
+        ts(C(T0 + 8, 8), C(T0 + 8, 8), OH(8), OP.mult)
+        fill(R("T0", 0, 180, 3), 0.0)
+        fill(R("c33"), 33.0)
+        tt(C(W8, 8), C(T0, 8), R("oh", 1, 16, 2), OP.add)
+        tt(C(BKS, 8), C(T0 + 8, 8), R("oh", 0, 8), OP.add)
+        fill(R("D8", 0, 480, 8), FAR)
+        ts(C(A4 + 1, 2), R("iof", 1, 3), C(T0 + 16), OP.mult, 8.0, OP.mult)
+        exsel(WGT, C(EV))
+        exsel(LAG, C(OD))
+        act(R("V", M, 2 * M), R("Q0"), bias=C(A4))
+        cp(R("V", 0, M), R("Q0"))
+        send([(rel[me][k], (e_on + e_off)[4 * k:4 * k + 4], "rh", R("hb", M * me, M * me + M), R("rlh")) for k in range(4)])
+        dma("g", R("L", 0, W), T.e0[:])
+        pick(R("I1", 0, 128), R("BO"), OP.is_equal, 0.0)
+        pick(R("u1", 256, 384), R("BO"), OP.is_equal, 0.0, 6)
         cp(R("btu", 0, 120), R("bti", 0, 120))
-        for k in range(16):
-            if k < 6:
-                act(R("TW", 128 * k, 128 * k + 128), R("wts"), scale=R("oh", k, k + 1))
+        tt(R("wg"), R("ls"), R("ws"), OP.add)
+        for i in range(3):
+            act(R("BK", 128 * i, 128 * i + 128), R("BO"), scale=C(BKS + i))
+        for h in range(8):
+            if h % 3 == 2:
+                act(R("TW", M * h, M * h + M), R("wg"), scale=O8(h))
             else:
-                ts(R("TW", 128 * k, 128 * k + 128), R("wts"), R("oh", k, k + 1), OP.mult)
-        ts(R("bli", 0, 120), R("bti", 0, 120), 127, OP.bitwise_and)
-        cp(R("blu", 0, 120), R("bli", 0, 120))
-        cp(R("btf", 0, 120), R("bti", 0, 120))
+                ts(R("TW", M * h, M * h + M), R("wg"), O8(h), OP.mult)
 
     def init2():
-        ts(R("hi", 0, 120), R("bti", 0, 120), 8, OP.arith_shift_right)
-        tt(R("dn", 0, 60), R("btf", 60, 120), R("btf", 0, 60), OP.subtract)
-        tt(R("dh", 0, 60), R("hi", 60, 120), R("hi", 0, 60), OP.subtract)
-        for h in range(N):
-            if h % 2:
-                act(R("V", M * h, M * h + M), R("Q0"), bias=C(CH + h))
-            else:
-                ts(R("V", M * h, M * h + M), R("Q0"), C(CH + h), OP.add)
-        for i in range(5, 8):
-            act(R("BK", 128 * i, 128 * i + 128), R("BO"), scale=C(OH + i))
-
-    def init2b():
-        tt(C(MK, 3), R("col", OH, OH + 6, 2), R("col", OH + 1, OH + 6, 2), OP.add)
-        ts(C(T0 + 5), C(OH + 7), 2.0, OP.mult)
-        ts(C(T0 + 4), C(MK + 1), C(OH + 7), OP.add, -1.0, OP.mult)
-        ts(C(T0 + 6), C(OH + 2), 19.0, OP.mult, C(T0 + 5), OP.add)
-        ts(C(T0 + 7), C(OH + 2), 64.0, OP.mult, C(T0 + 5), OP.add)
-        ts(C(GSS), C(T0 + 4), 1.0, OP.add)
-        ts(C(GSB, 4), R("iof", 0, 4), C(T0 + 6), OP.mult, C(T0 + 7), OP.add)
-
-    def masks(t, n_=2):
-        c, w_ = 120 * t, 120 // n_
-        for i in range(n_):
-            act(R("MK", 16 * (c + w_ * i), 16 * (c + w_ * i + w_)), IX(R("TW"), R("btu", c + w_ * i, c + w_ * i + w_)))
-
-    def weights(t):
-        ext(R("P2", 0, 120), None, "MK", 1920 * t, 120)
-        act(R("wl", 120 * t, 120 * t + 120), R("P2", 0, 120), scale=(1.0 / 256 if t == 0 else 1.0 / 65536))
+        ts(R("V", 2 * M, 4 * M), R("V", 0, 2 * M), C(A4 + 1), OP.add)
+        pairs(0)
+        ts(R("V", 4 * M, 8 * M), R("V", 0, 4 * M), C(A4 + 2), OP.add)
+        tt(C(T0 + 18), O8(1), OH(6), OP.add)
+        ts(C(T0 + 8), OH(6), 2.0, OP.mult)
+        ts(C(T0 + 9), OH(6), 64.0, OP.mult)
+        ts(C(GSS), C(T0 + 18), -1.0, OP.mult, 1.0, OP.add)
+        ts(C(T0 + 10), OH(2), 19.0, OP.mult, C(T0 + 8), OP.add)
+        ts(C(T0 + 11), OH(2), 36.0, OP.mult, C(T0 + 9), OP.add)
+        ts(C(GSB, 4), R("iof", 0, 4), C(T0 + 10), OP.mult, C(T0 + 11), OP.add)
 
     def init3():
-        ts(C(T0 + 1, 3), R("col", OH, OH + 6, 2), 64.0, OP.mult)
-        ts(C(WREL), C(OH + 6), 64.0, OP.mult, C(OH + 1), OP.add)
-        ts(R("stat"), R("V", 0, K), C(MK + 1), OP.mult)
-        tt(C(W3, 3), C(T0 + 1, 3), R("col", OH + 1, OH + 6, 2), OP.add)
-
-    def init3b():
-        cp(R("btu", 120, 240), R("bti", 120, 240))
-        ts(C(T0 + 8), C(OH + 6), 4.0, OP.mult)
-        ts(C(T0 + 9), C(OH + 4), 19.0, OP.mult)
-        ts(C(T0 + 10), C(OH + 4), 60.0, OP.mult, C(OH + 7), OP.add)
-        ts(C(RSA), C(OH), 32.0, OP.mult, C(T0 + 8), OP.add)
-        ts(C(OVS), C(MK + 2), -1.0, OP.mult, 1.0, OP.add)
-        ts(C(OVB, 4), R("iof", 0, 4), C(T0 + 9), OP.mult, C(T0 + 10), OP.add)
-        ts(R("RST"), R("Q0"), C(MK), OP.mult, C(RSA), OP.add)
-        ts(C(OVB), C(OH + 4), 32.0, OP.mult, C(OH + 7), OP.add)
-        cp(R("V", REG, REG + M), R("RST"))
+        act(R("UU"), R("u1", 0, 128), scale=-1.0)
+        for i in range(3, 8):
+            act(R("BK", 128 * i, 128 * i + 128), R("BO"), scale=C(BKS + i))
 
     def init4():
-        for qn, c in ((NAME, W3), (TAG, OH + 7), (PR, W3 + 1), (PB, W3 + 2), (REL, WREL)):
-            act(R("EX", 144 * qn, 144 * qn + 144), R("Z"), scale=C(c))
+        ts(R("stat"), R("V", 0, K), O8(1), OP.mult)
+        act(C(RSS), OH(10), scale=-1.0, bias=1.0)
+        act(C(T0 + 17), OH(10), scale=8.0)
+        act(C(T0 + 8), OH(4), scale=19.0)
+        act(C(RSB), C(T0 + 16), scale=32.0, bias=C(T0 + 17))
+        act(C(T0 + 9), OH(4), scale=32.0, bias=OH(6))
+        region(0)
 
     def init5():
-        ts(R("ia", 128, 256), R("ioi", 0, 128), 15, OP.bitwise_and)
-        ts(R("OVQ"), R("Q0"), C(MK + 2), OP.mult)
-        ts(R("RP"), R("ia", 128, 256), C(RC), OP.is_equal)
-        ts(R("SG"), R("ia", 128, 256), C(RC), OP.is_equal, -PS, OP.mult)
+        cp(R("btu", 120, 240), R("bti", 120, 240))
+        act(C(OVS), O8(2), scale=-1.0, bias=1.0)
+        act(C(OVB, 4), R("iof", 0, 4), scale=C(T0 + 8), bias=C(T0 + 9))
+        exsel(NAME, C(W8))
+        exsel(TAG, OH(6))
+        act(R("OVQ"), R("Q0"), scale=O8(2))
 
     def init6():
+        fill(R("hb", W, W + M), 0.0)
+        ts(R("ia", 128, 256), R("ioi", 0, 128), 15, OP.bitwise_and)
+        cp(R("ag"), R("lags"))
+        act(R("I1", 128, 256), R("I1", 0, 128), scale=3.0)
+        act(R("I1", 256, 384), R("I1", 0, 128), scale=-128.0)
+        act(C(RRB, 3), R("iof", 0, 3), scale=-2.0, bias=-63.0)
+
+    def init7():
+        ts(R("RP"), R("ia", 128, 256), C(RC), OP.is_equal)
+        ts(R("SG"), R("ia", 128, 256), C(RC), OP.is_equal, -PS, OP.mult)
+        pairs(1)
+
+    def init8():
         cp(R("btu", 240, 480), R("bti", 240, 480))
-        cp(R("btf", 120, 480), R("bti", 120, 480))
-        ts(R("hi", 120, 480), R("bti", 120, 480), 8, OP.arith_shift_right)
-        for t in range(1, RO):
-            tt(R("dh", 60 * t, 60 * t + 60), R("hi", 120 * t + 60, 120 * t + 120), R("hi", 120 * t, 120 * t + 60), OP.subtract)
-            tt(R("dn", 60 * t, 60 * t + 60), R("btf", 120 * t + 60, 120 * t + 120), R("btf", 120 * t, 120 * t + 60), OP.subtract)
-        fill(R("Hw", M, HW), 0.0)
-        fill(R("Hw", HW + M, 2 * HW), 0.0)
-        ts(C(T0), R("oh", 8, 9), R("oh", 9, 10), OP.add, -1.0 / 256, OP.mult)
-        ts(C(T0 + 1), R("oh", 8, 9), 0.25, OP.mult)
-        ts(R("u1", 0, 128), R("u1", 256, 384), C(MK + 1), OP.mult)
-        tt(C(T0 + 2), C(T0), C(GSS), OP.add)
-        ts(C(WND), R("oh", 9, 10), 1.0 / 256, OP.mult, C(T0 + 1), OP.add)
-        ts(R("u1", 128, 256), R("I1"), C(T0 + 2), OP.mult)
-        act(R("EX", 144 * OLD, 144 * OLD + 144), R("Z"), scale=C(WND))
+        tt(C(T0), O8(0), O8(2), OP.add)
+        ts(C(WREL), OH(10), 64.0, OP.mult, OH(1), OP.add)
+        tt(C(CM), C(T0), OH(10), OP.add)
+        ts(R("u1", 0, 128), R("u1", 256, 384), O8(1), OP.mult)
+        ts(R("u1", 128, 256), R("I1", 0, 128), C(CM), OP.mult)
+        fill(R("HA", 2 * M, HW), 0.0)
         tt(R("CPY"), R("u1", 0, 128), R("u1", 128, 256), OP.add)
+        pairs(2)
+        pairs(3)
+
+    def init9():
+        exsel(PR, C(W8 + 1))
+        region(1)
+
+    def init10():
+        act(R("HA", 0, 2 * M), R("hb", 2 * M * pm, 2 * M * pm + 2 * M))
+        act(R("HB"), R("hb", 0, HW), scale=0.0)
+
+    def masks(t, parts=range(3)):
+        for i in parts:
+            act(R("MK", 640 * i, 640 * i + 640), IX(R("TW"), R("btu", 120 * t + 40 * i, 120 * t + 40 * i + 40)))
+
+    def weights(t, bank="P3", mid=None):
+        ext(R(bank, 0, 120), WGT, "MK", 0, 120)
+        if mid:
+            mid()
+        act(R("wl", 120 * t, 120 * t + 120), R(bank, 0, 120))
+
+    def state(t):
+        own = R("FL", 1024 * t + 128 * pm, 1024 * t + 128 * pm + 128)
+        act(R("rr"), R("P0", 0, 128), AF.Relu, bias=C(RRB + t))
+        mm([(R("P4", 128, 256), own, R("I1", 128, 256))])
+        mm([(R("P0", 0, 128), R("I1", 0, 128), R("ag")), (R("P0", 0, 128), R("rr"), R("I1", 128, 256)),
+            (R("P0", 0, 128), own, R("I1", 256, 384))], True, False)
+        act(R("c2"), R("P4", 128, 256))
 
     def head(t):
         f0 = 1024 * (t - 1)
-        cp(R("V", REG, REG + M), R("RST"))
-        mm([(R("P0", 0, 128), R("I1"), R("pre"))]
-           + [(R("P0", 0, 128), R("I1"), R("FL", f0 + 128 * p, f0 + 128 * p + 128)) for p in peers], True, False)
-        mm([(R("P0", 0, 128), R("I1"), R("FL", f0 + 128 * p, f0 + 128 * p + 128)) for p in range(4, 8)], False, True)
+        mm([(R("P0", 0, 128), R("FL", f0 + 128 * p, f0 + 128 * p + 128), R("I1", 0, 128)) for p in range(8) if p != pm], False, True)
         tt(R("ag"), R("P0", 0, 128), R("c2"), OP.max)
+        for k in range(16):
+            if k % 3 == 2:
+                act(R("TA", 128 * k, 128 * k + 128), R("ag"), scale=OH(k))
+            else:
+                ts(R("TA", 128 * k, 128 * k + 128), R("ag"), OH(k), OP.mult)
 
-    def choice(t, mid=None, end=None):
-        c = 120 * t
+    def ages(t, cut=(30, 30)):
+        c, tab = 120 * t, "TA" if t else "TW"
+        for h in (0, 60):
+            n_ = cut[h // 60]
+            act(R("y", 16 * h, 16 * (h + n_)), IX(R(tab), R("btu", c + h, c + h + n_)))
+            if n_ < 60:
+                cp(R("y", 16 * (h + n_), 16 * h + 960), IX(R(tab), R("btu", c + h + n_, c + h + 60)))
+            ext(R(("P1", "P3")[h // 60], 0, 60), None if t else LAG, "y", 16 * h, 60)
+            if t == 0:
+                ext(R(("P2", "P5")[h // 60], 0, 60), WGT, "y", 16 * h, 60)
         if t == 0:
-            for c0 in range(0, 120, 20):
-                c1 = c0 + 20
-                tt(R("y", 16 * c0, 16 * c1), IX(R("lags"), R("blu", c0, c1)), R("MK", 16 * c0, 16 * c1), OP.min)
-                if c1 % 60 == 0:
-                    ext(R("P1", c1 - 60, c1), None, "y", 16 * (c1 - 60), 60)
-                if c1 == 100:
-                    weights(0)
-        else:
-            for k in range(16):
-                if k % 3 == 2:
-                    act(R("TA", 128 * k, 128 * k + 128), R("ag"), scale=R("oh", k, k + 1))
-                else:
-                    ts(R("TA", 128 * k, 128 * k + 128), R("ag"), R("oh", k, k + 1), OP.mult)
-            for h in (0, 60):
-                act(R("y", 16 * h, 16 * h + 480), IX(R("TA"), R("btu", c + h, c + h + 30)))
-                cp(R("y", 16 * h + 480, 16 * h + 960), IX(R("TA"), R("btu", c + h + 30, c + h + 60)))
-                ext(R("P1", h, h + 60), None, "y", 16 * h, 60)
-        if mid:
-            mid()
-        k = [R("P4", 64 * i, 64 * i + 60) for i in range(6)]
+            act(R("wl", 0, 60), R("P2", 0, 60))
+            act(R("wl", 60, 120), R("P5", 0, 60))
+
+    def choice(t, end=None):
+        c = 120 * t
+        k = [R("P4", 64 * i, 64 * i + 60) for i in range(2)]
         tt(R("sl", 0, 60), R("P1", 0, 60), R("wl", c, c + 60), OP.mult)
-        tt(k[0], R("P1", 60, 120), R("wl", c + 60, c + 120), OP.mult)
-        tt(k[1], k[0], R("sl", 0, 60), OP.is_gt)
-        tt(R("s3", 0, 60), k[0], R("sl", 0, 60), OP.max)
-        tt(k[2], k[1], R("dh", 60 * t, 60 * t + 60), OP.mult)
-        ts(R("gm", 0, 60), R("s3", 0, 60), 4.0, OP.is_lt, 8.0, OP.mult)
-        tt(k[3], k[1], R("dn", 60 * t, 60 * t + 60), OP.mult)
-        tt(k[4], k[2], R("hi", c, c + 60), OP.add)
-        tt(R("nf", 0, 60), k[3], R("btf", c, c + 60), OP.add)
-        tt(R("key", 0, 60), k[4], R("gm", 0, 60), OP.add)
-        cp(R("n16", 0, 60), R("nf", 0, 60))
+        tt(k[0], R("P3", 0, 60), R("wl", c + 60, c + 120), OP.mult)
+        tt(k[1], k[0], R("sl", 0, 60), OP.max)
+        tt(R("T0", 1, 180, 3), k[0], R("sl", 0, 60), OP.is_gt)
+        ts(R("NT", 180 * t + 2, 180 * t + 180, 3), k[1], 4.0, OP.is_lt, float(W), OP.mult)
+        scan(R("F1"), R("T0"), R("NT", 180 * t, 180 * t + 180), 0.0, OP.mult, OP.add)
+        ts(R("key", 0, 60), R("F1", 2, 180, 3), -127.5, OP.add, ROUND, OP.add)
+        cp(R("n16", 0, 60), R("F1", 1, 180, 3))
         for i in range(8):
-            ts(R("Dh", 60 * i, 60 * i + 60), R("key", 0, 60), float(order[i]), OP.is_equal)
-        act(R("Gr", 0, 480), IX(R("V", 0, W), R("n16", 0, 30)))
-        mm([(R("P2", 0, 60), R("Z", 15 - i, 143 - i), R("Dh", 60 * i, 60 * i + 60)) for i in range(8)])
+            ts(R("Dh", i, 480, 8), R("key", 0, 60), ROUND + 256.0 * i, OP.is_equal)
+        for h in range(2):
+            src = IX(R("V", 0, W), R("n16", 30 * h, 30 * h + 30))
+            if t == 0:
+                act(R("Gs", 480 * h, 480 * h + 480), src, bias=C(GSB), scale=C(GSS))
+            else:
+                act(R("Gr", 480 * h, 480 * h + 480), src)
+        mm([(R("P2", 0, 60), R("Z", 15 - i, 143 - i), R("Dh", i, 480, 8)) for i in range(8)])
         mm([(R("P3", 0, 480), R("UU"), R("Dh"))], True, False)
-        mm([(R("P0", 0, 60), R("ID", 128 * i, 128 * i + 128), R("Dh", 60 * i, 60 * i + 60)) for i in range(1, 8)])
+        ts(R("thr", 0, 60), R("key", 0, 60), -(ROUND + 7936.0), OP.add, 0.125, OP.mult)
+        ts(R("qb", 0, 60), R("F1", 1, 180, 3), -1.0, OP.mult, float(AN[t] + 1024), OP.add)
         if end:
             end()
-        act(R("Gr", 480, 960), IX(R("V", 0, W), R("n16", 30, 60)))
 
     def carry(t, h):
-        if t == 0:
-            act(R("Gs", 480 * h, 480 * h + 480), R("Gr", 480 * h, 480 * h + 480), bias=C(GSB + t), scale=C(GSS))
-        else:
-            pb = ("P5", "P7")[h]
-            mm([(R(pb, 0, 480), R("CPY"), R("Gr", 480 * h, 480 * h + 480))])
-            act(R("Gs", 480 * h, 480 * h + 480), R(pb, 0, 480), bias=C(GSB + t))
+        pb = ("P5", "P7")[h]
+        mm([(R(pb, 0, 480), R("CPY"), R("Gr", 480 * h, 480 * h + 480))])
+        act(R("Gs", 480 * h, 480 * h + 480), R(pb, 0, 480), bias=C(GSB + t))
 
-    def prefix(t, mid=None, end=None):
-        o_, d0, d1 = R("Ec", 0, 60), R("c33", 0, 60), R("P2", 0, 60)
-        op("v", o_, [d0, d1], lambda: g.vector.tensor_tensor_scan(o_[0], d0[0], d1[0], 0.0, OP.min, OP.add))
-        mm([(R("P3", 60 * i, 60 * i + 60), R("BK", 128 * i, 128 * i + 128), R("Ec", 0, 60)) for i in range(8)], False, True)
-        tt(R("s1", 0, 60), R("P0", 0, 60), R("nf", 0, 60), OP.subtract)
-        ts(R("qb", 0, 60), R("s1", 0, 60), float(REG + 63), OP.add)
+    def prefix(t, mid=None):
+        scan(R("Ec", 0, 60), R("c33", 0, 60), R("P2", 0, 60), OH(8), OP.min, OP.add)
+        mm([(R("P3", i, 480, 8), R("BK", 128 * i, 128 * i + 128), R("Ec", 0, 60)) for i in range(8)], False, True)
         if mid:
             mid()
-        carry(t, 0)
-        tt(R("sel"), R("P3", 0, 480), R("Dh"), OP.mult)
-        mm([(R("P1", 0, 60), R("I1"), R("sel", 60 * i, 60 * i + 60)) for i in range(8)])
-        carry(t, 1)
-        if end:
-            end()
-        tt(R("P1", 64, 124), R("P1", 0, 60), R("qb", 0, 60), OP.add)
-        ts(R("gm", 0, 60), R("P1", 0, 60), -31.5, OP.is_le)
-        tt(R("P1", 128, 188), R("P1", 64, 124), R("gm", 0, 60), OP.mult)
-        tt(R("of", 0, 60), R("P1", 128, 188), R("nf", 0, 60), OP.add)
-        cp(R("o16", 0, 60), R("of", 0, 60))
         if t > 0:
+            carry(t, 0)
+            carry(t, 1)
             ext(R("P4", 0, 60), PR, "Gr", 0, 60)
+        scan(R("vv"), R("D8"), R("P3", 0, 480), 0.0, OP.add, OP.min)
+        tt(R("T0", 1, 180, 3), R("vv", 7, 480, 8), R("thr", 0, 60), OP.is_lt)
+        tt(R("F1", 0, 180, 3), R("vv", 7, 480, 8), R("qb", 0, 60), OP.add)
+        scan(R("FO"), R("T0"), R("F1"), 0.0, OP.mult, OP.add)
+        cp(R("o16", 64 * t, 64 * t + 60), R("FO", 1, 180, 3))
 
-    def scatter(t):
-        tt(IX(R("V"), R("o16", 0, 60)), R("Gs"), R("stat"), OP.add)
-        ext(R("P2", 0, 16), NAME, "V", REG, 16)
-        act(R("ovt"), R("V", REG, REG + M), bias=C(OVB + t), scale=(C(OVS) if t > 0 else 1.0))
+    def scatter(t, c0=0, c1=60):
+        tt(IX(R("V", 0, XB[t]), R("o16", 64 * t + c0, 64 * t + c1)), R("Gs", 16 * c0, 16 * c1), R("stat", 16 * c0, 16 * c1), OP.add)
+
+    def granted(t):
+        act(R("ovt"), R("V", AN[t], XB[t]), bias=C(OVB + t), scale=C(OVS))
 
     def places(t):
-        o_ = R("xo", 64 * t, 64 * t + 60)
-        if t == 0:
-            ts(R("s2", 0, 60), R("gm", 0, 60), float(HB), OP.mult)
-            tt(R("s3", 0, 60), R("s2", 0, 60), R("nf", 0, 60), OP.add)
-        else:
-            tt(R("s1", 0, 60), R("of", 0, 60), R("P4", 0, 60), OP.subtract)
-            ts(R("s2", 0, 60), R("s1", 0, 60), float(AN[t] - REG), OP.add)
-            tt(R("s1", 0, 60), R("s2", 0, 60), R("gm", 0, 60), OP.mult)
-            tt(R("s3", 0, 60), R("s1", 0, 60), R("P4", 0, 60), OP.add)
-        cp(o_, R("s3", 0, 60))
+        tt(R("s3", 0, 60), R("P4", 0, 60), R("FO", 1, 180, 3), OP.max)
+        cp(R("xo", 64 * t, 64 * t + 60), R("s3", 0, 60))
+
+    def names(t):
+        ext(R("P2", 0, 16), NAME, "V", AN[t], 16)
 
     def override(t):
-        if t == 0:
-            cp(IX(R("V", 0, REG), R("rq16")), R("ovt"))
-        else:
-            tt(IX(R("V", 0, REG), R("rq16")), R("ovt"), R("OVQ"), OP.add)
+        cp(R("rq16"), R("P1", 48, 64) if t == RO - 1 else R("P2", 0, 16))
+        tt(IX(R("V", 0, W + M), R("rq16")), R("ovt"), R("OVQ"), OP.add)
 
-    def rel_out(t):
-        ext(R("P3", 0, 16), REL, "V", REG, 16)
-        for p in range(4):
-            c = ((t - 1) * 4 + p) * MW + 64
-            act(R("MSG", c, c + 4), R("P3", 4 * p, 4 * p + 4))
+    def tags(t):
+        mm([(R("P0", k, 128, 16), R("V", 128 * k, 128 * k + 128), R("EX", 144 * TAG + 15, 144 * TAG + 143, 16)) for k in range(16)], each=True)
 
     def flags(t):
-        mm([(R("P0", 0, 128), R("EX", 144 * TAG + 15 - k, 144 * TAG + 143 - k), R("V", 128 * k, 128 * k + 128)) for k in range(16)])
-        if t == 0:
-            places(0)
-            init5()
         own = R("FL", 1024 * t + 128 * pm, 1024 * t + 128 * pm + 128)
-        ts(own, R("P0", 0, 128), 2 * t + 2.5, OP.is_ge)
-        send([(rel[me][k], (e_on, e_off)[k], "rf%d" % t, own, R("rlf", 128 * t, 128 * t + 128)) for k in range(2)])
-        if t != 1:
-            flags_near(t)
+        ts(own, R("P0", 0, 128), 2 * t + 64.5, OP.is_ge)
+        send([(rel[me][k::2], (e_on, e_off)[k], "rf%d" % t, own, R("rlf", 128 * t, 128 * t + 128)) for k in range(2)])
 
-    def flags_near(t):
-        own = R("FL", 1024 * t + 128 * pm, 1024 * t + 128 * pm + 128)
-        to_peers("fs%d" % t, lambda p: own, own)
+    def lists(t):
+        cols = (W8 + 2, W8 + 4, WREL, W8)[:4 if t == RO - 1 else 3]
+        for i, c in enumerate(cols):
+            if i == 2 or t < RO - 1:
+                act(R("X4", M * i, M * i + M), R("V", AN[t], XB[t]), scale=C(c))
+            else:
+                ts(R("X4", M * i, M * i + M), R("V", AN[t], XB[t]), C(c), OP.mult)
+        ext(R("P1", 0, 16 * len(cols)), None, "X4", 0, 16 * len(cols))
 
-    def tail(t):
-        cp(R("rq16"), R("P2", 0, 16))
-        if t > 0:
-            ext(R("P1", 0, 16), OLD, "V", REG, 16)
-            ext(R("P2", 0, 16), PB, "V", REG, 16)
-        override(t)
-        if t == 1:
-            pointers()
-            values(1)
-        if t == 2:
-            products(1)
-        flags(t)
-        if t == 2:
-            errors(1)
-        if t > 0:
-            rel_out(t)
+    def block(t, j):
+        c = ((t - 1) * 4 + j) * MW
+        return ((pm - 1 - SLOTS[j]) % 4,) + ((c + 4, c) if SLOTS[j] % 2 else (c, c + 64))
 
-    def pointers():
-        cp(R("pb16"), R("P2", 0, 16))
-        cp(R("pr16"), R("P1", 0, 16))
+    def runs(t, part, w_):
+        out = []
+        for j in range(4):
+            blk = block(t, j)
+            if out and out[-1][0] + out[-1][2] == blk[0] and out[-1][1] + w_ * out[-1][2] == blk[part]:
+                out[-1][2] += 1
+            else:
+                out.append([blk[0], blk[part], 1])
+        return out
 
-    def state(t):
-        ts(R("c1"), R("P0", 0, 128), 2 * t + 1.5, OP.is_ge, 3.0, OP.mult)
-        ts(R("c3"), R("P0", 0, 128), 2 * t + 2.5, OP.is_ge, -128.0, OP.mult)
-        ts(R("c2"), R("P0", 0, 128), 2 * t + 2.5, OP.is_ge, 3.0, OP.mult)
-        tt(R("c4"), R("c1"), R("lags" if t == 0 else "ag"), OP.add)
-        tt(R("pre"), R("c4"), R("c3"), OP.add)
-
-    def bases(t):
-        act(R("RB"), IX(R("L", 0, XB[t - 1]), R("pb16")))
+    def pointers(t):
+        cp(R("pb16"), R("P1", 0, 32))
+        act(R("RB"), IX(R("L", 0, XB[t - 1]), R("pb16", 0, 16)))
+        for p, c, n_ in runs(t, 2, 4):
+            act(R("MSG", c, c + 4 * n_), R("P1", 32 + 4 * p, 32 + 4 * p + 4 * n_))
 
     def values(t):
-        win = R("L", 0, AN[t])
-        m0 = (t - 1) * 4 * MW
-        if t == 1:
-            bases(t)
-        for p in range(4):
-            tt(R("MSG", m0 + p * MW, m0 + p * MW + 64), IX(win, R("pr16", 4 * p, 4 * p + 4)), R("RB", 64 * p, 64 * p + 64), OP.subtract)
+        for p, c, n_ in runs(t, 1, 64):
+            tt(R("MSG", c, c + 64 * n_), IX(R("L", 0, AN[t]), R("pb16", 16 + 4 * p, 16 + 4 * p + 4 * n_)), R("RB", 64 * p, 64 * p + 64 * n_), OP.subtract)
 
     def request(t):
         m0 = (t - 1) * 4 * MW
         s = (t - 1) * 2 * MW
         send([(rel[me][k], (e_on, e_off)[k], "rr%d" % t, R("MSG", m0 + 2 * k * MW, m0 + (2 * k + 2) * MW), R("rlq", s, s + 2 * MW)) for k in range(2)])
-        if t == 1:
-            flags_near(t)
-        c = ((t - 1) * 8 + pm) * MW
-        to_peers("qs%d" % t, lambda p: R("MSG", m0 + p * MW, m0 + (p + 1) * MW), R("RQ", c, c + MW))
 
-    def adds(t, srcs, alone=False):
-        blk = []
-        for s in srcs:
-            nm, c = ("MSG", ((t - 1) * 4 + s) * MW) if s == pm else ("RQ", ((t - 1) * 8 + s) * MW)
-            cp(R("ho", 4 * s, 4 * s + 4), R(nm, c + 64, c + MW))
-            blk.append((s, nm, c))
-        for s, nm, c in blk:
+    def request_near(t):
+        m0 = (t - 1) * 4 * MW
+        to_peers(("qa%d" % t, "qb%d" % t), peers, lambda i: R("MSG", m0 + SLOTS.index(i) * MW, m0 + (SLOTS.index(i) + 1) * MW),
+                 lambda i: R("RQ", ((t - 1) * 8 + i) * MW, ((t - 1) * 8 + i + 1) * MW))
+
+    def at(t, *groups):
+        for slots in groups:
+            s0 = slots[0]
+            nm, c = ("MSG", block(t, 2)[2]) if s0 == 3 else ("RQ", ((t - 1) * 8 + s0) * MW + 64)
+            cp(R("ho", 4 * s0, 4 * s0 + 4 * len(slots)), R(nm, c, c + 4 * len(slots)))
+
+    def adds(t, slots, alone=False):
+        cv = [("MSG", block(t, 2)[1]) if s == 3 else ("RQ", ((t - 1) * 8 + s) * MW + 4 * (s % 2)) for s in slots]
+        ws = [IX(R(("HB", "HA")[s % 2]), R("ho", 4 * s, 4 * s + 4)) for s in slots]
+        hs = [R("ht", 64 * (s % 2), 64 * (s % 2) + 64) for s in slots]
+        vs = [R(nm, c, c + 64) for nm, c in cv]
+        for i in range(len(slots)):
             if alone:
-                ws = [IX(R("Hw", HW * h, HW * h + HW), R("ho", 4 * s + 2 * h, 4 * s + 2 * h + 2)) for h in range(2)]
-                for h in range(2):
-                    tt(R("ht", 32 * h, 32 * h + 32), ws[h], R(nm, c + 32 * h, c + 32 * h + 32), OP.add)
-                for h in range(2):
-                    cp(ws[h], R("ht", 32 * h, 32 * h + 32))
-                continue
-            for h in range(2):
-                w_ = IX(R("Hw", HW * h, HW * h + HW), R("ho", 4 * s + 2 * h, 4 * s + 2 * h + 2))
-                act(R("ht", 32 * h, 32 * h + 32), w_)
-                tt(w_, R("ht", 32 * h, 32 * h + 32), R(nm, c + 32 * h, c + 32 * h + 32), OP.add)
+                tt(hs[i], ws[i], vs[i], OP.add)
+            else:
+                act(hs[i], ws[i])
+        for i in range(len(slots)):
+            if alone:
+                cp(ws[i], hs[i])
+            else:
+                tt(ws[i], hs[i], vs[i], OP.add)
 
     def answer(t):
         a0 = 256 * (t - 1)
         for h in range(2):
-            for i, p in enumerate(peers + [pm]):
-                c = a0 + 64 * p + 32 * h
-                w_ = IX(R("Hw", HW * h, HW * h + HW), R("ho", 4 * p + 2 * h, 4 * p + 2 * h + 2))
-                if h == 1 and i < 3 and t == RO - 1:
-                    cp(R("AO", c, c + 32), w_)
-                else:
-                    act(R("AO", c, c + 32), w_)
+            act(R("at", 128 * h, 128 * h + 128), IX(R("HA"), R("ho", 8 * h, 8 * h + 8)))
+        for h in range(2):
+            tt(R("AO", a0 + 128 * h, a0 + 128 * h + 128), IX(R("HB"), R("ho", 8 * h, 8 * h + 8)), R("at", 128 * h, 128 * h + 128), OP.add)
         mineslot = R("L", AN[t] + 64 * pm, AN[t] + 64 * pm + 64)
-        to_peers("an%d" % t, lambda p: R("AO", a0 + 64 * p, a0 + 64 * p + 64), mineslot)
-        act(mineslot, R("AO", a0 + 64 * pm, a0 + 64 * pm + 64))
+        to_peers(("an%d" % t,) * 2, asker, lambda i: R("AO", a0 + 64 * i, a0 + 64 * i + 64), lambda i: mineslot)
+        act(mineslot, R("AO", a0 + 192, a0 + 256))
 
-    def step_a(t):
-        products(t)
-        errors(t)
+    def own(t):
+        at(t, [3])
+        adds(t, [3], True)
 
-    def products(t):
-        win = R("L", 0, XB[t])
-        c = 64 * t
-        cuts = ((0, 8), (8, 20), (20, 30))
+    def near(t, alone=False):
+        at(t, [0, 1])
+        adds(t, [0, 1], alone)
+        at(t, [2])
+        adds(t, [2], alone)
+
+    def far(t, alone=False):
+        at(t, [4, 5], [6, 7])
+        adds(t, [4, 5], alone)
+        adds(t, [6, 7], alone)
+        answer(t)
+
+    def slots(t, c0, c1):
+        return IX(R("L", 0, XB[t]), R("xo" if t else "o16", 64 * t + c0, 64 * t + c1))
+
+    def partners(t, cuts=((0, 8), (8, 20), (20, 30))):
         for c0, c1 in cuts:
-            act(R("x", 480 + 16 * c0, 480 + 16 * c1), IX(win, R("xo", c + 30 + c0, c + 30 + c1)))
+            act(R("x", 480 + 16 * c0, 480 + 16 * c1), slots(t, 30 + c0, 30 + c1))
+
+    def firsts(t):
+        act(R("x", 0, 480), slots(t, 0, 30))
+
+    def products(t, cuts=((0, 8), (8, 20), (20, 30))):
         for c0, c1 in cuts:
-            tt(R("prod", 16 * c0, 16 * c1), IX(win, R("xo", c + c0, c + c1)), R("x", 480 + 16 * c0, 480 + 16 * c1), OP.mult)
-        act(R("x", 0, 480), IX(win, R("xo", c, c + 30)))
+            tt(R("prod", 16 * c0, 16 * c1), slots(t, c0, c1), R("x", 480 + 16 * c0, 480 + 16 * c1), OP.mult)
 
     def errors(t):
         top = slice(0, 16)
         mm([(R("P5", 0, 60), R("RP", parts=top), R("tgs", 60 * t, 60 * t + 60, parts=top))], True, False)
         for k0, k1 in ((0, 2), (2, 5), (5, 8)):
             mm([(R("P5", 0, 60), R("SG"), R("prod", 60 * k, 60 * k + 60)) for k in range(k0, k1)], False, k1 == 8)
+
+    def squash(t):
         act(R("er", 0, 60), R("P5", 0, 60), AF.Tanh)
         act(R("P6", 0, 60), R("er", 0, 60), scale=ST)
 
-    def step_b(t, h):
+    def step(t, h):
         for k in range(8):
             c = 480 * (1 - h) + 60 * k
-            tt(R("P7", 60 * k, 60 * k + 60), R("P6", 0, 60), R("x", c, c + 60), OP.mult)
-        tt(R("L", XB[t] + 480 * h, XB[t] + 480 * h + 480), R("P7", 0, 480), R("x", 480 * h, 480 * h + 480), OP.add)
+            tt(R(("P7", "P5")[h], 60 * k, 60 * k + 60), R("P6", 0, 60), R("x", c, c + 60), OP.mult)
+
+    def stepped(t, h):
+        tt(R("L", XB[t] + 480 * h, XB[t] + 480 * h + 480), R(("P7", "P5")[h], 0, 480), R("x", 480 * h, 480 * h + 480), OP.add)
+
+    def steps(t):
+        step(t, 0)
+        step(t, 1)
+        stepped(t, 0)
+        stepped(t, 1)
 
     init()
-    masks(0, 6)
-    choice(0, init2, init2b)
-    prefix(0, init3, init3b)
-    init4()
-    masks(1)
-    scatter(0)
-    act(R("L", HB, HB + W), R("hb"))
-    act(R("P6", 0, 8), R("iof", 0, 8), AF.Tanh)
-    tail(0)
-    step_a(0)
-    weights(1)
-    state(0)
-    init6()
-    for s in range(2):
-        h = order[2 * pm + s]
-        act(R("Hw", HW * s, HW * s + M), R("hb", M * h, M * h + M))
-    step_b(0, 0)
-    step_b(0, 1)
+    ages(0); init2(); init3(); choice(0, init4); init5(); prefix(0); masks(1); scatter(0)
+    granted(0); names(0); weights(1); init6(); override(0); tags(0)
+    act(R("L", AN[0], XB[0]), IX(R("hb"), R("rq16")))
+    partners(0); init7(); flags(0); products(0); state(0); firsts(0); errors(0); squash(0); init8()
 
-    head(1)
-    choice(1)
-    prefix(1)
-    masks(2)
-    scatter(1)
-    tail(1)
-    request(1)
-    weights(2)
-    state(1)
-    places(1)
-    adds(1, [pm])
+    head(1); ages(1, (60, 40)); steps(0); init9(); choice(1); prefix(1); region(2); masks(2); scatter(1)
+    granted(1); names(1); lists(1); override(1); tags(1); init10(); pointers(1)
+    flags(1); values(1); request(1); request_near(1); state(1); weights(2); places(1); own(1); near(1)
 
-    def add1(t, srcs, last=False):
-        def run():
-            adds(t, srcs, srcs[0] > 3)
-            if last:
-                answer(t)
-        return run
+    head(2); ages(2, (60, 40)); far(1, True); choice(2); prefix(2); partners(1, ((0, 30),))
+    scatter(2, 0, 30); products(1, ((0, 16), (16, 30))); firsts(1); errors(1); region(3); masks(3, [0]); squash(1)
+    scatter(2, 30, 60); granted(2); names(2); lists(2); step(1, 0); override(2); tags(2); step(1, 1); pointers(2)
+    flags(2); state(2); stepped(1, 0); stepped(1, 1); values(2); request(2); request_near(2)
+    masks(3, [1, 2]); places(2); own(2)
 
-    head(2)
-    choice(2, add1(1, peers), add1(1, [4]))
-    prefix(2, add1(1, [5]), add1(1, [6, 7], True))
-    masks(3)
-    scatter(2)
-    tail(2)
-    pointers()
-    bases(2)
-    state(2)
-    weights(3)
-    step_b(1, 0)
-    step_b(1, 1)
-    values(2)
-    request(2)
-    places(2)
-    adds(2, [pm])
-
-    head(3)
-    choice(3, add1(2, peers), add1(2, [4]))
-    prefix(3, add1(2, [5, 6, 7], True))
-    scatter(3)
-    ext(R("P1", 0, 16), OLD, "V", REG, 16)
-    products(2)
-    cp(R("rq16"), R("P2", 0, 16))
-    errors(2)
-    ext(R("P2", 0, 16), PB, "V", REG, 16)
-    rel_out(3)
-    pointers()
-    bases(3)
-    step_b(2, 0)
-    step_b(2, 1)
-    values(3)
-    request(3)
-    override(3)
-    places(3)
+    head(3); weights(3, "P2", lambda: ages(3, (60, 60))); near(2, True); far(2, True); choice(3); prefix(3)
+    partners(2, ((0, 30),)); scatter(3, 0, 30); products(2, ((0, 16), (16, 30))); firsts(2); errors(2); squash(2)
+    scatter(3, 30, 60); lists(3); step(2, 0); step(2, 1); pointers(3); stepped(2, 0); stepped(2, 1)
+    values(3); request(3); request_near(3); granted(3); override(3); places(3)
     ext(R("P0", 0, 128), PR, "V", 0, 128)
-    adds(3, [pm])
+    own(3)
     cp(R("f16"), R("P0", 0, 128))
-    adds(3, peers)
-    adds(3, range(4, 8))
-    answer(3)
-    side = 0 if me in a else 1
-    dma("s", T.yh[:], R("Hw", HW * side, HW * side + M))
-    step_a(3)
-    step_b(3, 0)
-    step_b(3, 1)
-    for i in range(8):
-        o_, w_ = R("yo", 256 * i, 256 * i + 256), IX(R("L"), R("f16", 16 * i, 16 * i + 16))
-        if i % 2 == 0:
-            act(o_, w_)
-        else:
-            cp(o_, w_)
-            dma("s", T.yr[:, 256 * i - 256:256 * i + 256], R("yo", 256 * i - 256, 256 * i + 256))
+    near(3); far(3)
+    side = M * (me % 2)
+    tt(R("yq"), R("HA", side, side + M), R("HB", side, side + M), OP.add)
+    dma("s", T.yh[:], R("yq"))
+    partners(3); products(3); firsts(3); errors(3); squash(3); steps(3)
+    c0 = 0
+    for n_ in (256, 512, 640, 640):
+        h = n_ // 32 * 16
+        act(R("yo", c0, c0 + h), IX(R("L"), R("f16", c0 // 16, (c0 + h) // 16)))
+        cp(R("yo", c0 + h, c0 + n_), IX(R("L"), R("f16", (c0 + h) // 16, (c0 + n_) // 16)))
+        dma("s", T.yr[:, c0:c0 + n_], R("yo", c0, c0 + n_))
+        c0 += n_
     for tok in dtok:
         need("g", tok)
     for q in "vapg":

@@ -8,17 +8,18 @@ AN = [W + (M + K) * t for t in range(RO)]
 XB = [a_ + M for a_ in AN]
 LEN = XB[-1] + K
 MW = 68
+BW = 72
 HW = 2 * M + 64
 ROUND = 3221225472.0
+EIGHTS = 100663296.0
 FAR = 65536.0
 SLOTS = (1, 0, 3, 2)
-ORDER = (("f", 0), ("f", 1), ("r", 1), ("f", 2), ("r", 2), ("r", 3))
 F, B, I32, U = "float32", "bfloat16", "int32", "uint16"
 
 SCRATCH = {
     "L": ("sbuf", [128, LEN], F), "V": ("sbuf", [128, XB[-1]], B), "TW": ("sbuf", [128, W], B),
     "MK": ("sbuf", [128, 1920], B), "y": ("sbuf", [128, 1920], B), "wl": ("sbuf", [128, 480], F),
-    "sl": ("sbuf", [128, 64], F), "oh": ("sbuf", [128, 16], F), "o8": ("sbuf", [128, 8], F),
+    "sl": ("sbuf", [128, 64], F), "lim": ("sbuf", [128, 64], F), "oh": ("sbuf", [128, 16], F), "o8": ("sbuf", [128, 8], F),
     "ag": ("sbuf", [128, 128], B), "rr": ("sbuf", [128, 128], B), "c2": ("sbuf", [128, 128], F),
     "hb": ("sbuf", [128, W + M], B), "yo": ("sbuf", [128, W], F), "HA": ("sbuf", [128, HW], F),
     "HB": ("sbuf", [128, HW], F), "yq": ("sbuf", [128, M], F),
@@ -34,7 +35,7 @@ SCRATCH = {
     "RP": ("sbuf", [128, 128], B), "Q0": ("sbuf", [128, 256], B),
     "OVQ": ("sbuf", [128, 256], B), "stat": ("sbuf", [128, K], B), "c33": ("sbuf", [128, 64], F),
     "Gr": ("sbuf", [128, K], B), "Gs": ("sbuf", [128, K], B), "Dh": ("sbuf", [128, 480], B),
-    "D8": ("sbuf", [128, 480], B), "vv": ("sbuf", [128, 480], F),
+    "D8": ("sbuf", [128, 480], B),
     "T0": ("sbuf", [128, 180], F), "NT": ("sbuf", [128, 720], F), "F1": ("sbuf", [128, 180], F),
     "FO": ("sbuf", [128, 180], F),
     "Ec": ("sbuf", [128, 64], B), "key": ("sbuf", [128, 64], F), "n16": ("sbuf", [128, 64], U),
@@ -42,17 +43,18 @@ SCRATCH = {
     "o16": ("sbuf", [128, 256], U), "xo": ("sbuf", [128, 256], U), "rq16": ("sbuf", [128, 16], U),
     "X4": ("sbuf", [128, 4 * M], B), "pb16": ("sbuf", [128, 32], U), "ovt": ("sbuf", [128, 256], B),
     "RB": ("sbuf", [128, 256], F),
-    "FL": ("sbuf", [128, 3 * 1024], B), "MSG": ("sbuf", [128, 3 * 4 * MW], F),
+    "FL": ("sbuf", [128, 3 * 1024], B), "MSG": ("sbuf", [128, 3 * 4 * BW], F),
     "RQ": ("sbuf", [128, 3 * 8 * MW], F), "ho": ("sbuf", [128, 32], U), "ht": ("sbuf", [128, 128], F),
     "at": ("sbuf", [128, 256], F),
     "AO": ("sbuf", [128, 3 * 256], F), "x": ("sbuf", [128, K], F), "er": ("sbuf", [128, 64], F),
     "prod": ("sbuf", [128, 480], F), "f16": ("sbuf", [128, 128], U),
-    "rlh": ("sbuf", [128, 256], B), "rlf": ("sbuf", [128, 384], B), "rlq": ("sbuf", [128, 6 * MW], F),
+    "rlh": ("sbuf", [128, 256], B), "rlf": ("sbuf", [128, 384], B), "rlq": ("sbuf", [128, 6 * BW], F),
+    "rla": ("sbuf", [128, 128], F), "rlx": ("sbuf", [128, M], F), "HX": ("sbuf", [128, 2 * M], F),
 }
 for _b in range(8):
     SCRATCH["P%d" % _b] = ("psum", [128, 512], F)
-SEMAPHORES = (["cv", "ca", "cp", "cg", "snt", "hbl", "rh"] + ["d%d" % i for i in range(24)]
-              + [n + str(t) for n in ("fs", "fo", "qa", "qb", "qc", "qd", "an", "rf", "rr") for t in range(4)])
+SEMAPHORES = (["cv", "ca", "cp", "cg", "snt", "hbl", "rh", "rx", "sx", "hx"] + ["d%d" % i for i in range(24)]
+              + [n + str(t) for n in ("fs", "fo", "qa", "qb", "qc", "qd", "an", "rf", "rr", "ra") for t in range(4)])
 
 
 def bits_of(es):
@@ -71,21 +73,14 @@ def layout(T, topo):
     for r in range(N):
         far = cores[(b if r in a else a)[0]]
         cs = [c for c in topo.cores_of(cores[r]) if c != cores[r] and topo.may_write(c, far)]
-        rel.append([c for c in cs if topo.die(c) == topo.die(cores[r])] + [c for c in cs if topo.die(c) != topo.die(cores[r])])
+        rel.append(sorted(cs, key=lambda c: topo.die(c) != topo.die(cores[r])))
     return cores, a, b, rel
 
 
 def xfer(topo, src_core, dst_core, es, sem, src, dst):
     to = [topo.addr(d_, src_core) for d_ in (dst_core if isinstance(dst_core, list) else [dst_core])]
     return RemoteDMATransfer(dst_ids=[DstId(rid=rid, pnc=pid) for rid, pid in to], dma_engine_mask=bits_of(es), remote_sem=sem,
-                             srcs=[src], dsts=[dst] * len(to))
-
-
-def targets(k, mine, other, p):
-    near = [mine[(p + i) % 4] for i in (1, 2, 3)]
-    if k < 2:
-        return [(other[(p + 2 * k) % 4], 4), (other[(p + 2 * k + 1) % 4], 4)]
-    return [(near[0], 4), (near[1], 4)] if k == 2 else [(near[2], 8)]
+                             srcs=[src], dsts=dst if isinstance(dst, list) else [dst])
 
 
 def relay_program(g, core, T, topo, r, k, cores, a, b):
@@ -94,35 +89,51 @@ def relay_program(g, core, T, topo, r, k, cores, a, b):
     es = topo.engines(core, cores[other[0]])
     h = len(es) // 2
     n = [0]
+    pair = [(other[(p + 2 * k + i) % 4], h) for i in range(2)]
 
-    def spread(sem, cnt, rsem, src, dst):
+    def spread(sem, cnt, rsem, src, dst, to):
         g.wait_ge(T.sem[sem], cnt)
         trs, e0_ = [], 0
-        for d_, n_ in targets(k, mine, other, p):
+        for d_, n_ in to:
             trs.append(xfer(topo, core, cores[d_], es[e0_:e0_ + n_], T.sem[rsem], src, dst))
             e0_ += n_
         g.remote_dma_fused(trs, local_sem=T.sem.snt)
         n[0] += e0_
 
     def flags(t):
-        c = 1024 * t + 128 * (4 + p if k < 2 else p)
-        spread("rf%d" % t, 8, "fo%d" % t, T.rlf[:, 128 * t:128 * t + 128], T.FL[:, c:c + 128])
+        c = 1024 * t + 128 * (4 + p)
+        spread("fs%d" % t, 8, "fo%d" % t, T.rlf[:, 128 * t:128 * t + 128], T.FL[:, c:c + 128], pair)
 
     def requests(t):
-        s = (t - 1) * 2 * MW
         to = [(p - 1 - SLOTS[2 * k + i]) % 4 for i in range(2)]
         cs = [((t - 1) * 8 + 4 + SLOTS[2 * k + i]) * MW for i in range(2)]
-        g.wait_ge(T.sem["rr%d" % t], 8)
+        w_ = MW if t == RO - 1 else BW // 2
+        s = [(t - 1) * 2 * BW + (MW * i if t == RO - 1 else BW * i + w_ * (other[to[i]] % 2)) for i in range(2)]
+        g.wait_ge(T.sem["rr%d" % t], 8 if t == RO - 1 else 4)
         g.remote_dma_fused([xfer(topo, core, cores[other[to[i]]], es[h * i:h * i + h], T.sem[("qc%d", "qd%d")[k] % t],
-                                 T.rlq[:, s + MW * i:s + MW * i + MW], T.RQ[:, cs[i]:cs[i] + MW]) for i in range(2)], local_sem=T.sem.snt)
+                                 T.rlq[:, s[i]:s[i] + w_], T.RQ[:, cs[i]:cs[i] + w_]) for i in range(2)], local_sem=T.sem.snt)
         n[0] += 2 * h
 
-    spread("rh", 4, "hbl", T.rlh[:], T.hb[:, M * r:M * r + M])
-    for kind, t in ORDER:
-        if kind == "f":
-            flags(t)
-        elif k < 2:
-            requests(t)
+    def answers(t):
+        g.wait_ge(T.sem["ra%d" % t], 8)
+        c = 64 * t - 64
+        g.remote_dma_fused([xfer(topo, core, cores[other[(p + 2 * k + 1 + i) % 4]], es[h * i:h * i + h], T.sem["an%d" % t],
+                                 T.rla[:, c + 32 * i:c + 32 * i + 32], T.L[:, AN[t] + 32 * r:AN[t] + 32 * r + 32]) for i in range(2)], local_sem=T.sem.snt)
+        n[0] += 2 * h
+
+    if k >= 2:
+        near = [mine[(p + i) % 4] for i in (1, 2, 3)]
+        spread("hbl", 8, "hbl", T.rlh[:], T.hb[:, M * r:M * r + M], [(near[0], h), (near[1], h)] if k == 2 else [(near[2], 2 * h)])
+        spread("rx", 8, "hx", T.rlx[:], T.HX[:, M * (k - 2):M * (k - 1)], [(other[p], 2 * h)])
+        g.wait_ge(T.sem.snt, n[0])
+        return
+    spread("hbl", 8, "hbl", T.rlh[:], T.hb[:, M * r:M * r + M], pair)
+    flags(0)
+    for t in range(1, RO - 1):
+        flags(t)
+        requests(t)
+        answers(t)
+    requests(RO - 1)
     g.wait_ge(T.sem.snt, n[0])
 
 
@@ -259,6 +270,10 @@ def rank_program(g, core, T, topo):
         send([(cores[mine[to[i]]], e_off[4 * i:4 * i + 4], sems[0], src(i), dst(i)) for i in range(2)])
         send([(cores[mine[to[2]]], e_off, sems[1], src(2), dst(2))])
 
+    def to_all(src, rdst, sem):
+        send([(rel[me][0], e_on, sem, src, rdst),
+              ([rel[me][1]] + [cores[mine[p]] for p in peers], e_off, sem, src, ([rdst[0]] + [src[0]] * 3,))])
+
     def C(i, n_=1):
         return R("col", i, i + n_)
 
@@ -279,12 +294,17 @@ def rank_program(g, core, T, topo):
     for r in range(N):
         if r != me:
             lands(R("hb", M * r, M * r + M), "hbl", 32)
+            for t in range(1, RO - 1):
+                lands(R("L", AN[t] + 32 * r, AN[t] + 32 * r + 32), "an%d" % t, 32)
+    lands(R("HX"), "hx", 16)
+    side = M * (me % 2)
     for t in range(RO - 1):
         for p in range(4):
             if p != pm:
-                lands(R("FL", 1024 * t + 128 * p, 1024 * t + 128 * p + 128), "fo%d" % t, 32)
-                lands(R("L", AN[t + 1] + 64 * p, AN[t + 1] + 64 * p + 64), "an%d" % (t + 1), 16)
-            lands(R("FL", 1024 * t + 128 * (4 + p), 1024 * t + 128 * (5 + p)), "fo%d" % t, 32)
+                lands(R("FL", 1024 * t + 128 * p, 1024 * t + 128 * p + 128), "fs%d" % t, 24)
+                if t == RO - 2:
+                    lands(R("L", AN[t + 1] + 64 * p, AN[t + 1] + 64 * p + 64), "an%d" % (t + 1), 16)
+            lands(R("FL", 1024 * t + 128 * (4 + p), 1024 * t + 128 * (5 + p)), "fo%d" % t, 16)
         for s, q_ in ((0, "qa"), (1, "qa"), (2, "qb"), (4, "qc"), (5, "qc"), (6, "qd"), (7, "qd")):
             lands(R("RQ", (8 * t + s) * MW, (8 * t + s + 1) * MW), q_ + str(t + 1), 8)
 
@@ -294,7 +314,7 @@ def rank_program(g, core, T, topo):
     def pairs(t):
         c = 120 * t
         tt(R("NT", 180 * t, 180 * t + 180, 3), R("bti", c + 60, c + 120), R("bti", c, c + 60), OP.subtract)
-        cp(R("NT", 180 * t + 1, 180 * t + 180, 3), R("bti", c, c + 60))
+        ts(R("NT", 180 * t + 1, 180 * t + 180, 3), R("bti", c, c + 60), float(M), OP.add)
 
     def region(t):
         act(R("V", AN[t], XB[t]), R("Q0"), bias=C(RSB), scale=C(RSS))
@@ -302,10 +322,10 @@ def rank_program(g, core, T, topo):
     def init():
         fill(R("ws"), 0.0)
         fill(R("ls"), 0)
+        dma("a", R("hb", M * me, M * me + M), T.e0[:, M * me:M * me + M])
         dma("a", R("bti", 0, 120), T.bt[:, 0:120])
         dma("s", R("ws", parts=slice(0, 128, 2)), T.wt[:])
         dma("s", R("ls", parts=slice(1, 128, 2)), T.lag[:])
-        dma("a", R("hb", M * me, M * me + M), T.e0[:, M * me:M * me + M])
         dma("s", R("bti", 120, 480), T.bt[:, 120:480])
         dma("s", R("lags"), T.lag[:])
         dma("s", R("tgs", parts=slice(0, 16)), T.tg[:])
@@ -338,22 +358,29 @@ def rank_program(g, core, T, topo):
         ts(C(T0 + 8, 8), C(T0 + 8, 8), OH(8), OP.mult)
         fill(R("T0", 0, 180, 3), 0.0)
         fill(R("c33"), 33.0)
+        fill(R("NT", 2, 180, 3), 0.0)
         tt(C(W8, 8), C(T0, 8), R("oh", 1, 16, 2), OP.add)
         tt(C(BKS, 8), C(T0 + 8, 8), R("oh", 0, 8), OP.add)
         fill(R("D8", 0, 480, 8), FAR)
         ts(C(A4 + 1, 2), R("iof", 1, 3), C(T0 + 16), OP.mult, 8.0, OP.mult)
         exsel(WGT, C(EV))
-        exsel(LAG, C(OD))
+        act(C(T0 + 19), C(OD), scale=7.0, bias=1.0)
+        exsel(LAG, C(T0 + 19))
         act(R("V", M, 2 * M), R("Q0"), bias=C(A4))
         cp(R("V", 0, M), R("Q0"))
-        send([(rel[me][k], (e_on + e_off)[4 * k:4 * k + 4], "rh", R("hb", M * me, M * me + M), R("rlh")) for k in range(4)])
+        send([(rel[me][k::2], (e_on, e_off)[k], "hbl", R("hb", M * me, M * me + M), ([T.rlh[:]] * 2,)) for k in range(2)])
         dma("g", R("L", 0, W), T.e0[:])
         pick(R("I1", 0, 128), R("BO"), OP.is_equal, 0.0)
         pick(R("u1", 256, 384), R("BO"), OP.is_equal, 0.0, 6)
         cp(R("btu", 0, 120), R("bti", 0, 120))
         tt(R("wg"), R("ls"), R("ws"), OP.add)
-        for i in range(3):
-            act(R("BK", 128 * i, 128 * i + 128), R("BO"), scale=C(BKS + i))
+        act(C(T0 + 18), O8(1), bias=OH(6))
+        act(C(RSS), OH(6), scale=2.0)
+        act(C(RSB), OH(6), scale=64.0)
+        act(C(GSS), C(T0 + 18), scale=-1.0, bias=1.0)
+        act(C(OVS), OH(2), scale=19.0, bias=C(RSS))
+        act(C(OVB), OH(2), scale=36.0, bias=C(RSB))
+        act(C(GSB, 4), R("iof", 0, 4), scale=C(OVS), bias=C(OVB))
         for h in range(8):
             if h % 3 == 2:
                 act(R("TW", M * h, M * h + M), R("wg"), scale=O8(h))
@@ -363,22 +390,19 @@ def rank_program(g, core, T, topo):
     def init2():
         ts(R("V", 2 * M, 4 * M), R("V", 0, 2 * M), C(A4 + 1), OP.add)
         pairs(0)
-        ts(R("V", 4 * M, 8 * M), R("V", 0, 4 * M), C(A4 + 2), OP.add)
-        tt(C(T0 + 18), O8(1), OH(6), OP.add)
-        ts(C(T0 + 8), OH(6), 2.0, OP.mult)
-        ts(C(T0 + 9), OH(6), 64.0, OP.mult)
-        ts(C(GSS), C(T0 + 18), -1.0, OP.mult, 1.0, OP.add)
-        ts(C(T0 + 10), OH(2), 19.0, OP.mult, C(T0 + 8), OP.add)
-        ts(C(T0 + 11), OH(2), 36.0, OP.mult, C(T0 + 9), OP.add)
-        ts(C(GSB, 4), R("iof", 0, 4), C(T0 + 10), OP.mult, C(T0 + 11), OP.add)
+        act(R("V", 4 * M, 6 * M), R("V", 0, 2 * M), bias=C(A4 + 2))
+        ts(R("V", 6 * M, 8 * M), R("V", 2 * M, 4 * M), C(A4 + 2), OP.add)
 
     def init3():
         act(R("UU"), R("u1", 0, 128), scale=-1.0)
-        for i in range(3, 8):
+        for i in range(8):
             act(R("BK", 128 * i, 128 * i + 128), R("BO"), scale=C(BKS + i))
 
-    def init4():
+    def static():
         ts(R("stat"), R("V", 0, K), O8(1), OP.mult)
+
+    def init4():
+        cp(R("btu", 120, 240), R("bti", 120, 240))
         act(C(RSS), OH(10), scale=-1.0, bias=1.0)
         act(C(T0 + 17), OH(10), scale=8.0)
         act(C(T0 + 8), OH(4), scale=19.0)
@@ -387,7 +411,6 @@ def rank_program(g, core, T, topo):
         region(0)
 
     def init5():
-        cp(R("btu", 120, 240), R("bti", 120, 240))
         act(C(OVS), O8(2), scale=-1.0, bias=1.0)
         act(C(OVB, 4), R("iof", 0, 4), scale=C(T0 + 8), bias=C(T0 + 9))
         exsel(NAME, C(W8))
@@ -401,13 +424,15 @@ def rank_program(g, core, T, topo):
         act(R("I1", 128, 256), R("I1", 0, 128), scale=3.0)
         act(R("I1", 256, 384), R("I1", 0, 128), scale=-128.0)
         act(C(RRB, 3), R("iof", 0, 3), scale=-2.0, bias=-63.0)
+        act(R("HB"), R("TW", 0, HW), AF.Tanh, scale=0.0)
 
     def init7():
         ts(R("RP"), R("ia", 128, 256), C(RC), OP.is_equal)
         ts(R("SG"), R("ia", 128, 256), C(RC), OP.is_equal, -PS, OP.mult)
-        pairs(1)
 
     def init8():
+        pairs(1)
+        fill(R("NT", 182, 720, 3), 0.0)
         cp(R("btu", 240, 480), R("bti", 240, 480))
         tt(C(T0), O8(0), O8(2), OP.add)
         ts(C(WREL), OH(10), 64.0, OP.mult, OH(1), OP.add)
@@ -421,11 +446,11 @@ def rank_program(g, core, T, topo):
 
     def init9():
         exsel(PR, C(W8 + 1))
+        exsel(PB, C(W8 + 2))
         region(1)
 
     def init10():
         act(R("HA", 0, 2 * M), R("hb", 2 * M * pm, 2 * M * pm + 2 * M))
-        act(R("HB"), R("hb", 0, HW), scale=0.0)
 
     def masks(t, parts=range(3)):
         for i in parts:
@@ -447,7 +472,8 @@ def rank_program(g, core, T, topo):
 
     def head(t):
         f0 = 1024 * (t - 1)
-        mm([(R("P0", 0, 128), R("FL", f0 + 128 * p, f0 + 128 * p + 128), R("I1", 0, 128)) for p in range(8) if p != pm], False, True)
+        for part in (peers, range(4, 8)):
+            mm([(R("P0", 0, 128), R("FL", f0 + 128 * p, f0 + 128 * p + 128), R("I1", 0, 128)) for p in part], False, part is not peers)
         tt(R("ag"), R("P0", 0, 128), R("c2"), OP.max)
         for k in range(16):
             if k % 3 == 2:
@@ -455,7 +481,7 @@ def rank_program(g, core, T, topo):
             else:
                 ts(R("TA", 128 * k, 128 * k + 128), R("ag"), OH(k), OP.mult)
 
-    def ages(t, cut=(30, 30)):
+    def ages(t, cut=(30, 30), mid=None):
         c, tab = 120 * t, "TA" if t else "TW"
         for h in (0, 60):
             n_ = cut[h // 60]
@@ -463,35 +489,61 @@ def rank_program(g, core, T, topo):
             if n_ < 60:
                 cp(R("y", 16 * (h + n_), 16 * h + 960), IX(R(tab), R("btu", c + h + n_, c + h + 60)))
             ext(R(("P1", "P3")[h // 60], 0, 60), None if t else LAG, "y", 16 * h, 60)
-            if t == 0:
-                ext(R(("P2", "P5")[h // 60], 0, 60), WGT, "y", 16 * h, 60)
-        if t == 0:
-            act(R("wl", 0, 60), R("P2", 0, 60))
-            act(R("wl", 60, 120), R("P5", 0, 60))
+            if mid and h == 0:
+                mid()
+
+    spare = []
+
+    def gap(n_=1):
+        for _ in range(min(n_, len(spare))):
+            spare.pop(0)()
+
+    def first(t, parts=(0, 1)):
+        lim = 4.0 if t else 32.0
+        if 0 in parts:
+            tt(R("sl", 0, 60), R("P1", 0, 60) if t else R("P5", 0, 60), R("wl", 120 * t, 120 * t + 60), OP.mult)
+        if 1 in parts:
+            ts(R("lim", 0, 60), R("sl", 0, 60), lim, OP.is_lt, lim, OP.mult)
 
     def choice(t, end=None):
         c = 120 * t
         k = [R("P4", 64 * i, 64 * i + 60) for i in range(2)]
-        tt(R("sl", 0, 60), R("P1", 0, 60), R("wl", c, c + 60), OP.mult)
-        tt(k[0], R("P3", 0, 60), R("wl", c + 60, c + 120), OP.mult)
-        tt(k[1], k[0], R("sl", 0, 60), OP.max)
+        src = [R("P1", 0, 60), R("P3", 0, 60)]
+        wl = [R("wl", c + 60 * h, c + 60 * h + 60) for h in range(2)]
+        if t == 0:
+            for h in range(2):
+                ts(R("FO", 64 * h, 64 * h + 60), src[h], -2.0, OP.add, EIGHTS, OP.add)
+            for h in range(2):
+                ts(wl[h], R("FO", 64 * h, 64 * h + 60), -EIGHTS, OP.add)
+            for h in range(2):
+                tt(R("P5", 64 * h, 64 * h + 60), src[h], wl[h], OP.subtract)
+                src[h] = R("P5", 64 * h, 64 * h + 60)
+            first(0, [0])
+        tt(k[0], src[1], wl[1], OP.mult)
+        if t == 0:
+            first(0, [1])
+        gap()
         tt(R("T0", 1, 180, 3), k[0], R("sl", 0, 60), OP.is_gt)
-        ts(R("NT", 180 * t + 2, 180 * t + 180, 3), k[1], 4.0, OP.is_lt, float(W), OP.mult)
+        tt(R("T0", 2, 180, 3), k[0], R("lim", 0, 60), OP.is_ge)
+        gap()
         scan(R("F1"), R("T0"), R("NT", 180 * t, 180 * t + 180), 0.0, OP.mult, OP.add)
+        gap()
         ts(R("key", 0, 60), R("F1", 2, 180, 3), -127.5, OP.add, ROUND, OP.add)
-        cp(R("n16", 0, 60), R("F1", 1, 180, 3))
+        ts(R("n16", 0, 60), R("F1", 1, 180, 3), -float(M), OP.add)
         for i in range(8):
-            ts(R("Dh", i, 480, 8), R("key", 0, 60), ROUND + 256.0 * i, OP.is_equal)
+            ts(R("Dh", i, 480, 8), R("key", 0, 60), ROUND + 256.0 * (i + 1), OP.is_equal)
         for h in range(2):
             src = IX(R("V", 0, W), R("n16", 30 * h, 30 * h + 30))
             if t == 0:
                 act(R("Gs", 480 * h, 480 * h + 480), src, bias=C(GSB), scale=C(GSS))
             else:
                 act(R("Gr", 480 * h, 480 * h + 480), src)
-        mm([(R("P2", 0, 60), R("Z", 15 - i, 143 - i), R("Dh", i, 480, 8)) for i in range(8)])
+        for i0 in (0, 4):
+            mm([(R("P2", 0, 60), R("Z", 15 - i, 143 - i), R("Dh", i, 480, 8)) for i in range(i0, i0 + 4)], i0 == 0, i0 == 4)
         mm([(R("P3", 0, 480), R("UU"), R("Dh"))], True, False)
-        ts(R("thr", 0, 60), R("key", 0, 60), -(ROUND + 7936.0), OP.add, 0.125, OP.mult)
-        ts(R("qb", 0, 60), R("F1", 1, 180, 3), -1.0, OP.mult, float(AN[t] + 1024), OP.add)
+        ts(R("thr", 0, 60), R("key", 0, 60), -(ROUND + 8192.0), OP.add, 0.125, OP.mult)
+        ts(R("qb", 0, 60), R("F1", 1, 180, 3), -1.0, OP.mult, float(AN[t] + 1024 + M), OP.add)
+        gap(3)
         if end:
             end()
 
@@ -503,17 +555,18 @@ def rank_program(g, core, T, topo):
     def prefix(t, mid=None):
         scan(R("Ec", 0, 60), R("c33", 0, 60), R("P2", 0, 60), OH(8), OP.min, OP.add)
         mm([(R("P3", i, 480, 8), R("BK", 128 * i, 128 * i + 128), R("Ec", 0, 60)) for i in range(8)], False, True)
+        gap(len(spare))
         if mid:
             mid()
         if t > 0:
             carry(t, 0)
             carry(t, 1)
             ext(R("P4", 0, 60), PR, "Gr", 0, 60)
-        scan(R("vv"), R("D8"), R("P3", 0, 480), 0.0, OP.add, OP.min)
-        tt(R("T0", 1, 180, 3), R("vv", 7, 480, 8), R("thr", 0, 60), OP.is_lt)
-        tt(R("F1", 0, 180, 3), R("vv", 7, 480, 8), R("qb", 0, 60), OP.add)
+        scan(R("P2", 0, 480), R("D8"), R("P3", 0, 480), 0.0, OP.add, OP.min)
+        tt(R("T0", 1, 180, 3), R("P2", 7, 480, 8), R("thr", 0, 60), OP.is_lt)
+        tt(R("F1", 0, 180, 3), R("P2", 7, 480, 8), R("qb", 0, 60), OP.add)
         scan(R("FO"), R("T0"), R("F1"), 0.0, OP.mult, OP.add)
-        cp(R("o16", 64 * t, 64 * t + 60), R("FO", 1, 180, 3))
+        ts(R("o16", 64 * t, 64 * t + 60), R("FO", 1, 180, 3), -float(M), OP.add)
 
     def scatter(t, c0=0, c1=60):
         tt(IX(R("V", 0, XB[t]), R("o16", 64 * t + c0, 64 * t + c1)), R("Gs", 16 * c0, 16 * c1), R("stat", 16 * c0, 16 * c1), OP.add)
@@ -521,9 +574,12 @@ def rank_program(g, core, T, topo):
     def granted(t):
         act(R("ovt"), R("V", AN[t], XB[t]), bias=C(OVB + t), scale=C(OVS))
 
-    def places(t):
-        tt(R("s3", 0, 60), R("P4", 0, 60), R("FO", 1, 180, 3), OP.max)
-        cp(R("xo", 64 * t, 64 * t + 60), R("s3", 0, 60))
+    def places(t, parts=(0, 1)):
+        if 0 in parts:
+            ts(R("key", 0, 60), R("P4", 0, 60), float(M), OP.add)
+        if 1 in parts:
+            tt(R("s3", 0, 60), R("key", 0, 60), R("FO", 1, 180, 3), OP.max)
+            ts(R("xo", 64 * t, 64 * t + 60), R("s3", 0, 60), -float(M), OP.add)
 
     def names(t):
         ext(R("P2", 0, 16), NAME, "V", AN[t], 16)
@@ -538,19 +594,22 @@ def rank_program(g, core, T, topo):
     def flags(t):
         own = R("FL", 1024 * t + 128 * pm, 1024 * t + 128 * pm + 128)
         ts(own, R("P0", 0, 128), 2 * t + 64.5, OP.is_ge)
-        send([(rel[me][k::2], (e_on, e_off)[k], "rf%d" % t, own, R("rlf", 128 * t, 128 * t + 128)) for k in range(2)])
+        to_all(own, R("rlf", 128 * t, 128 * t + 128), "fs%d" % t)
 
     def lists(t):
         cols = (W8 + 2, W8 + 4, WREL, W8)[:4 if t == RO - 1 else 3]
-        for i, c in enumerate(cols):
-            if i == 2 or t < RO - 1:
-                act(R("X4", M * i, M * i + M), R("V", AN[t], XB[t]), scale=C(c))
-            else:
-                ts(R("X4", M * i, M * i + M), R("V", AN[t], XB[t]), C(c), OP.mult)
-        ext(R("P1", 0, 16 * len(cols)), None, "X4", 0, 16 * len(cols))
+        i0 = 1 if t == RO - 1 else 0
+        if i0:
+            ext(R("P2", 0, 16), PB, "V", AN[t], 16)
+        for i, c in list(enumerate(cols))[i0:]:
+            act(R("X4", M * i, M * i + M), R("V", AN[t], XB[t]), scale=C(c))
+        ext(R("P1", 16 * i0, 16 * len(cols)), None, "X4", M * i0, 16 * (len(cols) - i0))
 
     def block(t, j):
-        c = ((t - 1) * 4 + j) * MW
+        if t < RO - 1:
+            c = ((t - 1) * 4 + j) * BW
+            return (pm - 1 - SLOTS[j]) % 4, c + 4, c
+        c = (t - 1) * 4 * BW + j * MW
         return ((pm - 1 - SLOTS[j]) % 4,) + ((c + 4, c) if SLOTS[j] % 2 else (c, c + 64))
 
     def runs(t, part, w_):
@@ -563,73 +622,129 @@ def rank_program(g, core, T, topo):
                 out.append([blk[0], blk[part], 1])
         return out
 
-    def pointers(t):
-        cp(R("pb16"), R("P1", 0, 32))
+    def bases(t, out, in_):
+        cp(out, in_)
         act(R("RB"), IX(R("L", 0, XB[t - 1]), R("pb16", 0, 16)))
-        for p, c, n_ in runs(t, 2, 4):
-            act(R("MSG", c, c + 4 * n_), R("P1", 32 + 4 * p, 32 + 4 * p + 4 * n_))
+
+    def pointers(t):
+        if t == RO - 1:
+            cp(R("pb16", 16, 32), R("P1", 16, 32))
+        else:
+            bases(t, R("pb16"), R("P1", 0, 32))
+        if t == RO - 1:
+            for p, c, n_ in runs(t, 2, 4):
+                act(R("MSG", c, c + 4 * n_), R("P1", 32 + 4 * p, 32 + 4 * p + 4 * n_))
+            return
+        for j in range(4):
+            p, _, c = block(t, j)
+            for h in range(2):
+                act(R("MSG", c + 68 * h, c + 68 * h + 4), R("P1", 32 + 4 * p, 36 + 4 * p))
 
     def values(t):
         for p, c, n_ in runs(t, 1, 64):
             tt(R("MSG", c, c + 64 * n_), IX(R("L", 0, AN[t]), R("pb16", 16 + 4 * p, 16 + 4 * p + 4 * n_)), R("RB", 64 * p, 64 * p + 64 * n_), OP.subtract)
 
     def request(t):
-        m0 = (t - 1) * 4 * MW
-        s = (t - 1) * 2 * MW
-        send([(rel[me][k], (e_on, e_off)[k], "rr%d" % t, R("MSG", m0 + 2 * k * MW, m0 + (2 * k + 2) * MW), R("rlq", s, s + 2 * MW)) for k in range(2)])
+        m0, s, w_ = (t - 1) * 4 * BW, (t - 1) * 2 * BW, 2 * (MW if t == RO - 1 else BW)
+        es = (e_on, e_off) if t == RO - 1 else (e_on[:4], e_on[4:])
+        send([(rel[me][k], es[k], "rr%d" % t, R("MSG", m0 + k * w_, m0 + (k + 1) * w_), R("rlq", s, s + w_)) for k in range(2)])
 
     def request_near(t):
-        m0 = (t - 1) * 4 * MW
-        to_peers(("qa%d" % t, "qb%d" % t), peers, lambda i: R("MSG", m0 + SLOTS.index(i) * MW, m0 + (SLOTS.index(i) + 1) * MW),
-                 lambda i: R("RQ", ((t - 1) * 8 + i) * MW, ((t - 1) * 8 + i + 1) * MW))
+        w_ = MW if t == RO - 1 else BW // 2
+        c = [(t - 1) * 4 * BW + (MW * SLOTS.index(i) if t == RO - 1 else BW * SLOTS.index(i) + w_ * (mine[peers[i]] % 2)) for i in range(3)]
+        to_peers(("qa%d" % t, "qb%d" % t), peers, lambda i: R("MSG", c[i], c[i] + w_),
+                 lambda i: R("RQ", ((t - 1) * 8 + i) * MW, ((t - 1) * 8 + i) * MW + w_))
 
     def at(t, *groups):
         for slots in groups:
             s0 = slots[0]
             nm, c = ("MSG", block(t, 2)[2]) if s0 == 3 else ("RQ", ((t - 1) * 8 + s0) * MW + 64)
-            cp(R("ho", 4 * s0, 4 * s0 + 4 * len(slots)), R(nm, c, c + 4 * len(slots)))
+            if t == RO - 1:
+                cp(R("ho", 4 * s0, 4 * s0 + 4 * len(slots)), R(nm, c, c + 4 * len(slots)))
+            elif s0 == 3:
+                cp(R("ho", 6, 8), R(nm, c + 2 * (me % 2), c + 2 * (me % 2) + 2))
+            else:
+                c += 34 * (me % 2) - 64
+                for h in range(2):
+                    cp(R("ho", 2 * s0 + h, 2 * s0 + 2 * len(slots), 2), R(nm, c + h, c + h + MW * (len(slots) - 1) + 1, MW))
 
-    def adds(t, slots, alone=False):
-        cv = [("MSG", block(t, 2)[1]) if s == 3 else ("RQ", ((t - 1) * 8 + s) * MW + 4 * (s % 2)) for s in slots]
-        ws = [IX(R(("HB", "HA")[s % 2]), R("ho", 4 * s, 4 * s + 4)) for s in slots]
-        hs = [R("ht", 64 * (s % 2), 64 * (s % 2) + 64) for s in slots]
-        vs = [R(nm, c, c + 64) for nm, c in cv]
+    def adds(t, slots, alone=False, mid=None):
+        n_, c0 = (4, 0) if t == RO - 1 else (2, 32 * (me % 2))
+        cv = [("MSG", block(t, 2)[1]) if s == 3 else ("RQ", ((t - 1) * 8 + s) * MW + (4 * (s % 2) if n_ == 4 else 4 - 36 * (me % 2))) for s in slots]
+        ws = [IX(R(("HB", "HA")[s % 2]), R("ho", n_ * s, n_ * s + n_)) for s in slots]
+        hs = [R("ht", 64 * (s % 2), 64 * (s % 2) + 16 * n_) for s in slots]
+        vs = [R(nm, c + c0, c + c0 + 16 * n_) for nm, c in cv]
         for i in range(len(slots)):
             if alone:
                 tt(hs[i], ws[i], vs[i], OP.add)
             else:
                 act(hs[i], ws[i])
+        if mid:
+            mid()
         for i in range(len(slots)):
             if alone:
                 cp(ws[i], hs[i])
             else:
                 tt(ws[i], hs[i], vs[i], OP.add)
 
-    def answer(t):
+    def answer_near(t, w_, c):
         a0 = 256 * (t - 1)
+        to_peers(("an%d" % t,) * 2, asker, lambda i: R("AO", a0 + w_ * i, a0 + w_ * i + w_), lambda i: R("L", c, c + w_))
+        act(R("L", c, c + w_), R("AO", a0 + 3 * w_, a0 + 4 * w_))
+
+    def hand_over():
+        src = [R(nm, side, side + M) for nm in ("HA", "HB")]
+        deps("g", src[0][1] + src[1][1], [])
+        g.remote_dma_fused([xfer(topo, core, rel[me][2 + k], (e_on, e_off)[k], T.sem.rx, src[k][0], T.rlx[:]) for k in range(2)], local_sem=T.sem.sx)
+        note("x", src[0][1] + src[1][1], [], ("sx", 16))
+        dtok.append(("sx", 16))
+
+    def take_over():
+        for k, nm in enumerate(("HA", "HB")):
+            act(R(nm, M - side, 2 * M - side), R("HX", M * k, M * k + M))
+
+    def sums():
+        return [[IX(R(nm), R("ho", 8 * h, 8 * h + 8)) for h in range(2)] for nm in ("HA", "HB")]
+
+    def home(t):
+        a0, (ha, hb) = 256 * (t - 1), sums()
+        at(t, [0, 1])
+        adds(t, [0, 1], mid=lambda: at(t, [2]))
+        adds(t, [2], mid=lambda: at(t, [4, 5]))
+        adds(t, [5], mid=lambda: at(t, [6, 7]))
+        for s in (4, 7, 6):
+            adds(t, [s])
         for h in range(2):
-            act(R("at", 128 * h, 128 * h + 128), IX(R("HA"), R("ho", 8 * h, 8 * h + 8)))
+            act(R("at", 128 * h, 128 * h + 128), ha[h])
         for h in range(2):
-            tt(R("AO", a0 + 128 * h, a0 + 128 * h + 128), IX(R("HB"), R("ho", 8 * h, 8 * h + 8)), R("at", 128 * h, 128 * h + 128), OP.add)
-        mineslot = R("L", AN[t] + 64 * pm, AN[t] + 64 * pm + 64)
-        to_peers(("an%d" % t,) * 2, asker, lambda i: R("AO", a0 + 64 * i, a0 + 64 * i + 64), lambda i: mineslot)
-        act(mineslot, R("AO", a0 + 192, a0 + 256))
+            tt(R("AO", a0 + 128 * h, a0 + 128 * h + 128), hb[h], R("at", 128 * h, 128 * h + 128), OP.add)
+        answer_near(t, 64, AN[t] + 64 * pm)
+
+    def keep(t):
+        a0, (ha, hb) = 256 * (t - 1), sums()
+        at(t, [0, 1, 2])
+        adds(t, [0, 1], True)
+        at(t, [4, 5, 6, 7])
+        adds(t, [2, 5], True)
+        adds(t, [4, 7], True, lambda: first(t + 1, [0]))
+        adds(t, [6], True, lambda: (cp(R("at", 128, 256), ha[1]), first(t + 1, [1])))
+        cp(R("at", 0, 128), ha[0])
+        tt(R("AO", a0 + 128, a0 + 256), hb[1], R("at", 128, 256), OP.add)
+        send([(rel[me][k], (e_on, e_off)[k], "ra%d" % t, R("AO", a0 + 128 + 64 * k, a0 + 192 + 64 * k), R("rla", 64 * t - 64, 64 * t)) for k in range(2)])
+
+        def rest():
+            tt(R("AO", a0, a0 + 128), hb[0], R("at", 0, 128), OP.add)
+            answer_near(t, 32, AN[t] + 32 * me)
+            if t == RO - 2:
+                hand_over()
+        spare.append(rest)
 
     def own(t):
         at(t, [3])
         adds(t, [3], True)
 
-    def near(t, alone=False):
-        at(t, [0, 1])
-        adds(t, [0, 1], alone)
-        at(t, [2])
-        adds(t, [2], alone)
-
-    def far(t, alone=False):
-        at(t, [4, 5], [6, 7])
-        adds(t, [4, 5], alone)
-        adds(t, [6, 7], alone)
-        answer(t)
+    def starts():
+        act(R("L", AN[0], XB[0]), IX(R("hb"), R("rq16")))
 
     def slots(t, c0, c1):
         return IX(R("L", 0, XB[t]), R("xo" if t else "o16", 64 * t + c0, 64 * t + c1))
@@ -647,21 +762,30 @@ def rank_program(g, core, T, topo):
 
     def errors(t):
         top = slice(0, 16)
-        mm([(R("P5", 0, 60), R("RP", parts=top), R("tgs", 60 * t, 60 * t + 60, parts=top))], True, False)
-        for k0, k1 in ((0, 2), (2, 5), (5, 8)):
-            mm([(R("P5", 0, 60), R("SG"), R("prod", 60 * k, 60 * k + 60)) for k in range(k0, k1)], False, k1 == 8)
+        out = R("P5" if t else "P6", 64, 124)
+        mm([(out, R("RP", parts=top), R("tgs", 60 * t, 60 * t + 60, parts=top))], True, False)
+        for k0, k1 in (((0, 2), (2, 4), (4, 6), (6, 8)) if t == RO - 1 else ((0, 2), (2, 5), (5, 8))):
+            mm([(out, R("SG"), R("prod", 60 * k, 60 * k + 60)) for k in range(k0, k1)], False, k1 == 8)
 
     def squash(t):
-        act(R("er", 0, 60), R("P5", 0, 60), AF.Tanh)
+        if t == RO - 1:
+            act(R("yo", 480, K), R("x", 480, K), scale=ST)
+            act(R("P6", 0, 60), R("P5", 64, 124), AF.Tanh)
+            act(R("yo", 0, 480), R("x", 0, 480), scale=ST)
+            return
+        act(R("er", 0, 60), R("P5" if t else "P6", 64, 124), AF.Tanh)
         act(R("P6", 0, 60), R("er", 0, 60), scale=ST)
 
-    def step(t, h):
-        for k in range(8):
+    def bank(t, h):
+        return ("P7", "P5")[h] if t else ("P0", "P7")[h]
+
+    def step(t, h, ks=range(8)):
+        for k in ks:
             c = 480 * (1 - h) + 60 * k
-            tt(R(("P7", "P5")[h], 60 * k, 60 * k + 60), R("P6", 0, 60), R("x", c, c + 60), OP.mult)
+            tt(R(bank(t, h), 60 * k, 60 * k + 60), R("P6", 0, 60), R("yo" if t == RO - 1 else "x", c, c + 60), OP.mult)
 
     def stepped(t, h):
-        tt(R("L", XB[t] + 480 * h, XB[t] + 480 * h + 480), R(("P7", "P5")[h], 0, 480), R("x", 480 * h, 480 * h + 480), OP.add)
+        tt(R("L", XB[t] + 480 * h, XB[t] + 480 * h + 480), R(bank(t, h), 0, 480), R("x", 480 * h, 480 * h + 480), OP.add)
 
     def steps(t):
         step(t, 0)
@@ -670,33 +794,36 @@ def rank_program(g, core, T, topo):
         stepped(t, 1)
 
     init()
-    ages(0); init2(); init3(); choice(0, init4); init5(); prefix(0); masks(1); scatter(0)
-    granted(0); names(0); weights(1); init6(); override(0); tags(0)
-    act(R("L", AN[0], XB[0]), IX(R("hb"), R("rq16")))
-    partners(0); init7(); flags(0); products(0); state(0); firsts(0); errors(0); squash(0); init8()
+    ages(0); init2(); init3(); choice(0, init4); init5(); prefix(0, static); masks(1); scatter(0)
+    granted(0); names(0); init6(); override(0); starts(); partners(0); tags(0); init7(); flags(0)
+    products(0); state(0); errors(0); init8(); weights(1, "P3", lambda: (firsts(0), squash(0)))
+    init9(); init10(); step(0, 1); stepped(0, 1)
 
-    head(1); ages(1, (60, 40)); steps(0); init9(); choice(1); prefix(1); region(2); masks(2); scatter(1)
-    granted(1); names(1); lists(1); override(1); tags(1); init10(); pointers(1)
-    flags(1); values(1); request(1); request_near(1); state(1); weights(2); places(1); own(1); near(1)
+    head(1); ages(1); spare.extend(lambda k=k: step(0, 0, [k]) for k in range(8)); first(1); choice(1); prefix(1)
+    region(2); masks(2); scatter(1)
+    granted(1); names(1); lists(1); stepped(0, 0); override(1); tags(1); pointers(1); places(1, [0])
+    flags(1); values(1); request(1); request_near(1); state(1); weights(2); places(1, [1]); own(1)
 
-    head(2); ages(2, (60, 40)); far(1, True); choice(2); prefix(2); partners(1, ((0, 30),))
+    head(2); ages(2, (60, 54)); keep(1); choice(2); prefix(2); partners(1, ((0, 16), (16, 30)))
     scatter(2, 0, 30); products(1, ((0, 16), (16, 30))); firsts(1); errors(1); region(3); masks(3, [0]); squash(1)
     scatter(2, 30, 60); granted(2); names(2); lists(2); step(1, 0); override(2); tags(2); step(1, 1); pointers(2)
-    flags(2); state(2); stepped(1, 0); stepped(1, 1); values(2); request(2); request_near(2)
-    masks(3, [1, 2]); places(2); own(2)
+    flags(2); state(2); stepped(1, 0); stepped(1, 1); places(2, [0]); values(2); request(2); request_near(2)
+    masks(3, [1, 2]); places(2, [1]); own(2)
 
-    head(3); weights(3, "P2", lambda: ages(3, (60, 60))); near(2, True); far(2, True); choice(3); prefix(3)
-    partners(2, ((0, 30),)); scatter(3, 0, 30); products(2, ((0, 16), (16, 30))); firsts(2); errors(2); squash(2)
-    scatter(3, 30, 60); lists(3); step(2, 0); step(2, 1); pointers(3); stepped(2, 0); stepped(2, 1)
-    values(3); request(3); request_near(3); granted(3); override(3); places(3)
+    head(3)
+    ext(R("P2", 0, 120), WGT, "MK", 0, 120)
+    ages(3, (60, 54), lambda: act(R("wl", 360, 480), R("P2", 0, 120))); keep(2); choice(3); prefix(3)
+    partners(2, ((0, 16), (16, 30))); scatter(3, 0, 30); products(2, ((0, 16), (16, 30))); firsts(2); errors(2); squash(2)
+    scatter(3, 30, 60); lists(3); step(2, 0); bases(3, R("pb16", 0, 16), R("P2", 0, 16)); step(2, 1); stepped(2, 0)
+    pointers(3); stepped(2, 1); values(3); request(3); request_near(3); take_over(); granted(3); override(3); places(3)
     ext(R("P0", 0, 128), PR, "V", 0, 128)
     own(3)
     cp(R("f16"), R("P0", 0, 128))
-    near(3); far(3)
-    side = M * (me % 2)
+    home(3)
     tt(R("yq"), R("HA", side, side + M), R("HB", side, side + M), OP.add)
     dma("s", T.yh[:], R("yq"))
-    partners(3); products(3); firsts(3); errors(3); squash(3); steps(3)
+    partners(3, ((0, 8), (8, 16), (16, 30))); products(3, ((0, 8), (8, 16), (16, 24), (24, 30)))
+    firsts(3); errors(3); squash(3); steps(3)
     c0 = 0
     for n_ in (256, 512, 640, 640):
         h = n_ // 32 * 16

from concourse.bass import DstId, RemoteDMATransfer
from concourse.mybir import AluOpType as OP, ActivationFunctionType as AF

N, M, K, CAP, RO, S = 8, 256, 960, 32, 4, 60
W = N * M
PS, ST = 0.0078125, 0.015625
AN = [W + (M + K) * t for t in range(RO)]
XB = [a_ + M for a_ in AN]
LEN = XB[-1] + K
MW = 68
BW = 72
HW = 2 * M + 64
ROUND = 3221225472.0
EIGHTS = 100663296.0
FAR = 65536.0
SLOTS = (1, 0, 3, 2)
F, B, I32, U = "float32", "bfloat16", "int32", "uint16"

SCRATCH = {
    "L": ("sbuf", [128, LEN], F), "V": ("sbuf", [128, XB[-1]], B), "TW": ("sbuf", [128, W], B),
    "MK": ("sbuf", [128, 1920], B), "y": ("sbuf", [128, 1920], B), "wl": ("sbuf", [128, 480], F),
    "sl": ("sbuf", [128, 64], F), "lim": ("sbuf", [128, 64], F), "oh": ("sbuf", [128, 16], F), "o8": ("sbuf", [128, 8], F),
    "ag": ("sbuf", [128, 128], B), "rr": ("sbuf", [128, 128], B), "c2": ("sbuf", [128, 128], F),
    "hb": ("sbuf", [128, W + M], B), "yo": ("sbuf", [128, W], F), "HA": ("sbuf", [128, HW], F),
    "HB": ("sbuf", [128, HW], F), "yq": ("sbuf", [128, M], F),
    "bti": ("sbuf", [128, 480], I32), "btu": ("sbuf", [128, 480], U),
    "ws": ("sbuf", [128, M], B), "ls": ("sbuf", [128, M], I32), "wg": ("sbuf", [128, M], B),
    "lags": ("sbuf", [128, 128], I32), "tgs": ("sbuf", [128, 240], B),
    "ioi": ("sbuf", [128, 144], I32), "iof": ("sbuf", [128, 144], F), "pci": ("sbuf", [128, 4], I32),
    "ia": ("sbuf", [128, 256], I32), "col": ("sbuf", [128, 64], F),
    "Z": ("sbuf", [128, 144], B), "EX": ("sbuf", [128, 8 * 144], B), "CPY": ("sbuf", [128, 128], B),
    "TA": ("sbuf", [128, W], B), "BO": ("sbuf", [128, 128], B),
    "BK": ("sbuf", [128, 1024], B), "UU": ("sbuf", [128, 128], B), "u1": ("sbuf", [128, 512], B),
    "I1": ("sbuf", [128, 384], B), "SG": ("sbuf", [128, 128], F),
    "RP": ("sbuf", [128, 128], B), "Q0": ("sbuf", [128, 256], B),
    "OVQ": ("sbuf", [128, 256], B), "stat": ("sbuf", [128, K], B), "c33": ("sbuf", [128, 64], F),
    "Gr": ("sbuf", [128, K], B), "Gs": ("sbuf", [128, K], B), "Dh": ("sbuf", [128, 480], B),
    "D8": ("sbuf", [128, 480], B),
    "T0": ("sbuf", [128, 180], F), "NT": ("sbuf", [128, 720], F), "F1": ("sbuf", [128, 180], F),
    "FO": ("sbuf", [128, 180], F),
    "Ec": ("sbuf", [128, 64], B), "key": ("sbuf", [128, 64], F), "n16": ("sbuf", [128, 64], U),
    "qb": ("sbuf", [128, 64], F), "thr": ("sbuf", [128, 64], F), "s3": ("sbuf", [128, 64], F),
    "o16": ("sbuf", [128, 256], U), "xo": ("sbuf", [128, 256], U), "rq16": ("sbuf", [128, 16], U),
    "X4": ("sbuf", [128, 4 * M], B), "pb16": ("sbuf", [128, 32], U), "ovt": ("sbuf", [128, 256], B),
    "RB": ("sbuf", [128, 256], F),
    "FL": ("sbuf", [128, 3 * 1024], B), "MSG": ("sbuf", [128, 3 * 4 * BW], F),
    "RQ": ("sbuf", [128, 3 * 8 * MW], F), "ho": ("sbuf", [128, 32], U), "ht": ("sbuf", [128, 128], F),
    "at": ("sbuf", [128, 256], F),
    "AO": ("sbuf", [128, 3 * 256], F), "x": ("sbuf", [128, K], F), "er": ("sbuf", [128, 64], F),
    "prod": ("sbuf", [128, 480], F), "f16": ("sbuf", [128, 128], U),
    "rlh": ("sbuf", [128, 256], B), "rlf": ("sbuf", [128, 384], B), "rlq": ("sbuf", [128, 6 * BW], F),
    "rla": ("sbuf", [128, 128], F), "rlx": ("sbuf", [128, M], F), "HX": ("sbuf", [128, 2 * M], F),
}
for _b in range(8):
    SCRATCH["P%d" % _b] = ("psum", [128, 512], F)
SEMAPHORES = (["cv", "ca", "cp", "cg", "snt", "hbl", "rh", "rx", "sx", "hx"] + ["d%d" % i for i in range(24)]
              + [n + str(t) for n in ("fs", "fo", "qa", "qb", "qc", "qd", "an", "rf", "rr", "ra") for t in range(4)])


def bits_of(es):
    m = 0
    for e in es:
        m |= 1 << e
    return m


def layout(T, topo):
    cores = list(T.cores)
    a = [r for r in range(N) if r == 0 or topo.may_write(cores[0], cores[r])]
    b = [r for r in range(N) if r not in a]
    assert all(sorted((a[p], b[p])) == [2 * p, 2 * p + 1] for p in range(4))
    rel = []
    for r in range(N):
        far = cores[(b if r in a else a)[0]]
        cs = [c for c in topo.cores_of(cores[r]) if c != cores[r] and topo.may_write(c, far)]
        rel.append(sorted(cs, key=lambda c: topo.die(c) != topo.die(cores[r])))
    return cores, a, b, rel


def xfer(topo, src_core, dst_core, es, sem, src, dst):
    to = [topo.addr(d_, src_core) for d_ in (dst_core if isinstance(dst_core, list) else [dst_core])]
    return RemoteDMATransfer(dst_ids=[DstId(rid=rid, pnc=pid) for rid, pid in to], dma_engine_mask=bits_of(es), remote_sem=sem,
                             srcs=[src], dsts=dst if isinstance(dst, list) else [dst])


def relay_program(g, core, T, topo, r, k, cores, a, b):
    mine, other = (a, b) if r in a else (b, a)
    p = mine.index(r)
    es = topo.engines(core, cores[other[0]])
    h = len(es) // 2
    n = [0]
    pair = [(other[(p + 2 * k + i) % 4], h) for i in range(2)]

    def spread(sem, cnt, rsem, src, dst, to):
        g.wait_ge(T.sem[sem], cnt)
        trs, e0_ = [], 0
        for d_, n_ in to:
            trs.append(xfer(topo, core, cores[d_], es[e0_:e0_ + n_], T.sem[rsem], src, dst))
            e0_ += n_
        g.remote_dma_fused(trs, local_sem=T.sem.snt)
        n[0] += e0_

    def flags(t):
        c = 1024 * t + 128 * (4 + p)
        spread("fs%d" % t, 8, "fo%d" % t, T.rlf[:, 128 * t:128 * t + 128], T.FL[:, c:c + 128], pair)

    def requests(t):
        to = [(p - 1 - SLOTS[2 * k + i]) % 4 for i in range(2)]
        cs = [((t - 1) * 8 + 4 + SLOTS[2 * k + i]) * MW for i in range(2)]
        w_ = MW if t == RO - 1 else BW // 2
        s = [(t - 1) * 2 * BW + (MW * i if t == RO - 1 else BW * i + w_ * (other[to[i]] % 2)) for i in range(2)]
        g.wait_ge(T.sem["rr%d" % t], 8 if t == RO - 1 else 4)
        g.remote_dma_fused([xfer(topo, core, cores[other[to[i]]], es[h * i:h * i + h], T.sem[("qc%d", "qd%d")[k] % t],
                                 T.rlq[:, s[i]:s[i] + w_], T.RQ[:, cs[i]:cs[i] + w_]) for i in range(2)], local_sem=T.sem.snt)
        n[0] += 2 * h

    def answers(t):
        g.wait_ge(T.sem["ra%d" % t], 8)
        c = 64 * t - 64
        g.remote_dma_fused([xfer(topo, core, cores[other[(p + 2 * k + 1 + i) % 4]], es[h * i:h * i + h], T.sem["an%d" % t],
                                 T.rla[:, c + 32 * i:c + 32 * i + 32], T.L[:, AN[t] + 32 * r:AN[t] + 32 * r + 32]) for i in range(2)], local_sem=T.sem.snt)
        n[0] += 2 * h

    if k >= 2:
        near = [mine[(p + i) % 4] for i in (1, 2, 3)]
        spread("hbl", 8, "hbl", T.rlh[:], T.hb[:, M * r:M * r + M], [(near[0], h), (near[1], h)] if k == 2 else [(near[2], 2 * h)])
        spread("rx", 8, "hx", T.rlx[:], T.HX[:, M * (k - 2):M * (k - 1)], [(other[p], 2 * h)])
        g.wait_ge(T.sem.snt, n[0])
        return
    spread("hbl", 8, "hbl", T.rlh[:], T.hb[:, M * r:M * r + M], pair)
    flags(0)
    for t in range(1, RO - 1):
        flags(t)
        requests(t)
        answers(t)
    requests(RO - 1)
    g.wait_ge(T.sem.snt, n[0])


def rank_program(g, core, T, topo):
    cores, a, b, rel = layout(T, topo)
    me = T.rank_of(core)
    if me is None:
        for r in range(N):
            if core in rel[r]:
                relay_program(g, core, T, topo, r, rel[r].index(core), cores, a, b)
        return
    mine, other = (a, b) if me in a else (b, a)
    pm = mine.index(me)
    peers = [(pm + i) % 4 for i in (3, 2, 1)]
    asker = [(pm + 1 + i) % 4 for i in range(4)]
    e_off = topo.engines(core, cores[mine[peers[0]]])
    e_on = [e for e in topo.engines(core, rel[me][0]) if e not in e_off]

    QU = {"v": g.vector, "a": g.scalar, "p": g.tensor, "g": g, "s": g.sync}
    recs, waited, cnt = {}, {q: {} for q in QU}, {"v": 0, "a": 0, "p": 0, "g": 0, "d": 0, "snt": 0}
    dtok = []

    def R(name, c0=None, c1=None, step=1, parts=None):
        if c0 is None:
            c0, c1 = 0, SCRATCH[name][1][1]
        p = parts if parts is not None else slice(0, 128)
        return (T[name][p, c0:c1:step] if step > 1 else T[name][p, c0:c1], [(name, c0, c1, step)])

    def IX(win, off):
        return (win[0].indirect(off[0]), win[1] + off[1], win[1])

    def need(q, tok):
        if waited[q].get(tok[0], 0) < tok[1]:
            QU[q].wait_ge(T.sem[tok[0]], tok[1])
            waited[q][tok[0]] = tok[1]

    def deps(q, reads, writes):
        best = {}
        for regs, w in ((reads, False), (writes, True)):
            for name, c0, c1, st in regs:
                ps = SCRATCH[name][0] == "psum"
                for d0, d1, w0, q0, tok, s0 in recs.get(name, []):
                    if ps and q0 != q:
                        hit = True
                    elif ps and q == "p":
                        hit = False
                    else:
                        hit = (w or w0) and c0 < d1 and d0 < c1 and (st != s0 or (c0 - d0) % st == 0)
                    if hit and best.get(tok[0], 0) < tok[1]:
                        best[tok[0]] = tok[1]
        for s_, c_ in best.items():
            need(q, (s_, c_))

    def note(q, reads, writes, tok):
        def covers(c0, c1, st, x_):
            return c0 <= x_[0] and x_[1] <= c1 and (st == 1 or (st == x_[5] and (x_[0] - c0) % st == 0))

        for name, c0, c1, st in writes:
            recs[name] = [x_ for x_ in recs.get(name, []) if not covers(c0, c1, st, x_)] + [(c0, c1, True, q, tok, st)]
        for name, c0, c1, st in reads:
            recs[name] = [x_ for x_ in recs.get(name, []) if not (x_[3] == q and not x_[2] and x_[4][0] == tok[0] and covers(c0, c1, st, x_))] + [(c0, c1, False, q, tok, st)]

    def op(q, out, ins, fn):
        reads = [x_ for i_ in ins if isinstance(i_, tuple) for x_ in i_[1]]
        if len(out) == 3:
            writes = out[2]
            reads = reads + [x_ for x_ in out[1] if x_ not in writes]
        else:
            writes = out[1]
        deps(q, reads, writes)
        cnt[q] += 1
        fn().then_inc(T.sem["c" + q], 1)
        note(q, reads, writes, ("c" + q, cnt[q]))

    def val(x_):
        return x_[0] if isinstance(x_, tuple) else x_

    def cp(out, in_):
        op("v", out, [in_], lambda: g.vector.tensor_copy(out[0], in_[0]))

    def tt(out, i0, i1, o):
        op("v", out, [i0, i1], lambda: g.vector.tensor_tensor(out[0], i0[0], i1[0], o))

    def ts(out, i0, s1, o0, s2=None, o1=None):
        if o1 is None:
            op("v", out, [i0, s1], lambda: g.vector.tensor_scalar(out[0], i0[0], val(s1), None, o0))
        else:
            op("v", out, [i0, s1, s2], lambda: g.vector.tensor_scalar(out[0], i0[0], val(s1), val(s2), o0, o1))

    def scan(out, d0, d1, init_, o0, o1):
        op("v", out, [d0, d1, init_], lambda: g.vector.tensor_tensor_scan(out[0], d0[0], d1[0], val(init_), o0, o1))

    def fill(out, c):
        op("v", out, [], lambda: g.vector.memset(out[0], c))

    def act(out, in_, func=AF.Identity, bias=0.0, scale=1.0):
        op("a", out, [in_, bias, scale], lambda: g.scalar.activation(out[0], in_[0], func, bias=val(bias), scale=val(scale)))

    def iota(out, pat, base, cm):
        op("g", out, [], lambda: g.iota(out[0], pat, base, cm))

    def pick(out, in_, cmp_, c, base=0):
        op("g", out, [in_], lambda: g.affine_select(out[0], in_[0], [[-1, 128]], cmp_, c, base, 1))

    def mm(lst, start=True, stop=True, each=False):
        reads = [x_ for o_, l_, r_ in lst for x_ in l_[1] + r_[1]]
        writes = [x_ for o_, l_, r_ in lst for x_ in o_[1]]
        deps("p", reads, writes)
        for i_, (o_, l_, r_) in enumerate(lst):
            ins = g.tensor.matmul(o_[0], l_[0], r_[0], each or (start and i_ == 0), each or (stop and i_ == len(lst) - 1))
        cnt["p"] += 1
        ins.then_inc(T.sem.cp, 1)
        note("p", reads, writes, ("cp", cnt["p"]))

    def dma(q, out, in_):
        reads = in_[1] if isinstance(in_, tuple) else []
        writes = out[1] if isinstance(out, tuple) else []
        deps(q, reads, writes)
        tok = ("d%d" % cnt["d"], 16)
        cnt["d"] += 1
        QU[q].dma_start(val(out), val(in_)).then_inc(T.sem[tok[0]], 16)
        note("d" + tok[0], reads, writes, tok)
        dtok.append(tok)

    def send(items):
        deps("g", [x_ for it in items for x_ in it[3][1]], [])
        g.remote_dma_fused([xfer(topo, core, d_, es, T.sem[s_], src[0], dst[0]) for d_, es, s_, src, dst in items], local_sem=T.sem.snt)
        cnt["snt"] += sum(len(it[1]) for it in items)

    def lands(reg, sem, n_):
        note("r" + sem, [], reg[1], (sem, n_))

    def to_peers(sems, to, src, dst):
        send([(cores[mine[to[i]]], e_off[4 * i:4 * i + 4], sems[0], src(i), dst(i)) for i in range(2)])
        send([(cores[mine[to[2]]], e_off, sems[1], src(2), dst(2))])

    def to_all(src, rdst, sem):
        send([(rel[me][0], e_on, sem, src, rdst),
              ([rel[me][1]] + [cores[mine[p]] for p in peers], e_off, sem, src, ([rdst[0]] + [src[0]] * 3,))])

    def C(i, n_=1):
        return R("col", i, i + n_)

    def OH(i):
        return R("oh", i, i + 1)

    def O8(i):
        return R("o8", i, i + 1)

    def ext(out, qn, src, c0, n_):
        nm, b0 = ("Z", 0) if qn is None else ("EX", 144 * qn)
        mm([(out, R(nm, b0 + 15 - i, b0 + 143 - i), R(src, c0 + i, c0 + 16 * n_, 16)) for i in range(16)])

    WGT, LAG, NAME, TAG, PR, PB, OLD, REL = range(8)
    RC, GC, OD, EV, G15, AL2, W8, BKS, GSS, GSB, OVS, OVB, RSS, RSB, A4, WREL, CM, RRB, T0 = (
        0, 1, 2, 3, 4, 5, 6, 14, 22, 23, 27, 28, 32, 33, 34, 37, 38, 39, 44)

    for r in range(N):
        if r != me:
            lands(R("hb", M * r, M * r + M), "hbl", 32)
            for t in range(1, RO - 1):
                lands(R("L", AN[t] + 32 * r, AN[t] + 32 * r + 32), "an%d" % t, 32)
    lands(R("HX"), "hx", 16)
    side = M * (me % 2)
    for t in range(RO - 1):
        for p in range(4):
            if p != pm:
                lands(R("FL", 1024 * t + 128 * p, 1024 * t + 128 * p + 128), "fs%d" % t, 24)
                if t == RO - 2:
                    lands(R("L", AN[t + 1] + 64 * p, AN[t + 1] + 64 * p + 64), "an%d" % (t + 1), 16)
            lands(R("FL", 1024 * t + 128 * (4 + p), 1024 * t + 128 * (5 + p)), "fo%d" % t, 16)
        for s, q_ in ((0, "qa"), (1, "qa"), (2, "qb"), (4, "qc"), (5, "qc"), (6, "qd"), (7, "qd")):
            lands(R("RQ", (8 * t + s) * MW, (8 * t + s + 1) * MW), q_ + str(t + 1), 8)

    def exsel(qn, c):
        act(R("EX", 144 * qn, 144 * qn + 144), R("Z"), scale=c)

    def pairs(t):
        c = 120 * t
        tt(R("NT", 180 * t, 180 * t + 180, 3), R("bti", c + 60, c + 120), R("bti", c, c + 60), OP.subtract)
        ts(R("NT", 180 * t + 1, 180 * t + 180, 3), R("bti", c, c + 60), float(M), OP.add)

    def region(t):
        act(R("V", AN[t], XB[t]), R("Q0"), bias=C(RSB), scale=C(RSS))

    def init():
        fill(R("ws"), 0.0)
        fill(R("ls"), 0)
        dma("a", R("hb", M * me, M * me + M), T.e0[:, M * me:M * me + M])
        dma("a", R("bti", 0, 120), T.bt[:, 0:120])
        dma("s", R("ws", parts=slice(0, 128, 2)), T.wt[:])
        dma("s", R("ls", parts=slice(1, 128, 2)), T.lag[:])
        dma("s", R("bti", 120, 480), T.bt[:, 120:480])
        dma("s", R("lags"), T.lag[:])
        dma("s", R("tgs", parts=slice(0, 16)), T.tg[:])
        iota(R("pci", 0, 1), [[0, 1]], 0, 1)
        iota(R("ioi"), [[1, 144]], 0, 0)
        fill(R("T0"), 1.0)
        ts(R("pci", 1, 2), R("pci", 0, 1), 15, OP.bitwise_and)
        ts(R("pci", 2, 3), R("pci", 0, 1), 112, OP.bitwise_and)
        ts(R("pci", 3, 4), R("pci", 0, 1), 1, OP.bitwise_and)
        cp(R("iof"), R("ioi"))
        cp(C(RC, 3), R("pci", 1, 4))
        ts(R("ia", 0, 128), R("ioi", 0, 128), 112, OP.bitwise_and)
        ts(R("oh"), R("iof", 0, 16), C(RC), OP.is_equal)
        act(C(EV), C(OD), scale=-1.0, bias=1.0)
        act(C(G15), C(GC), bias=15.0)
        act(R("Q0", 0, 64), R("iof", 0, 64), scale=C(OD))
        act(C(AL2), C(EV), scale=2.0)
        act(C(T0 + 8, 8), R("iof", 0, 8), scale=32.0, bias=-1.0)
        act(R("Q0", 64, 128), R("Q0", 0, 64), bias=C(EV))
        act(C(A4), C(EV), scale=4.0)
        act(C(T0 + 16), OH(10), scale=-1.0, bias=C(EV))
        act(R("Q0", 128, 256), R("Q0", 0, 128), bias=C(AL2))
        ts(R("BO"), R("ia", 0, 128), C(GC), OP.is_equal)
        tt(R("o8"), R("oh", 0, 16, 2), R("oh", 1, 16, 2), OP.add)
        ts(R("Z"), R("iof"), C(G15), OP.is_equal)
        pick(R("u1", 128, 256), R("BO"), OP.is_gt, 0.0)
        pick(R("u1", 0, 128), R("u1", 128, 256), OP.not_equal, 1024.0)
        fill(R("D8"), 0.0)
        ts(C(T0, 8), R("oh", 0, 16, 2), 64.0, OP.mult)
        ts(C(T0 + 8, 8), C(T0 + 8, 8), OH(8), OP.mult)
        fill(R("T0", 0, 180, 3), 0.0)
        fill(R("c33"), 33.0)
        fill(R("NT", 2, 180, 3), 0.0)
        tt(C(W8, 8), C(T0, 8), R("oh", 1, 16, 2), OP.add)
        tt(C(BKS, 8), C(T0 + 8, 8), R("oh", 0, 8), OP.add)
        fill(R("D8", 0, 480, 8), FAR)
        ts(C(A4 + 1, 2), R("iof", 1, 3), C(T0 + 16), OP.mult, 8.0, OP.mult)
        exsel(WGT, C(EV))
        act(C(T0 + 19), C(OD), scale=7.0, bias=1.0)
        exsel(LAG, C(T0 + 19))
        act(R("V", M, 2 * M), R("Q0"), bias=C(A4))
        cp(R("V", 0, M), R("Q0"))
        send([(rel[me][k::2], (e_on, e_off)[k], "hbl", R("hb", M * me, M * me + M), ([T.rlh[:]] * 2,)) for k in range(2)])
        dma("g", R("L", 0, W), T.e0[:])
        pick(R("I1", 0, 128), R("BO"), OP.is_equal, 0.0)
        pick(R("u1", 256, 384), R("BO"), OP.is_equal, 0.0, 6)
        cp(R("btu", 0, 120), R("bti", 0, 120))
        tt(R("wg"), R("ls"), R("ws"), OP.add)
        act(C(T0 + 18), O8(1), bias=OH(6))
        act(C(RSS), OH(6), scale=2.0)
        act(C(RSB), OH(6), scale=64.0)
        act(C(GSS), C(T0 + 18), scale=-1.0, bias=1.0)
        act(C(OVS), OH(2), scale=19.0, bias=C(RSS))
        act(C(OVB), OH(2), scale=36.0, bias=C(RSB))
        act(C(GSB, 4), R("iof", 0, 4), scale=C(OVS), bias=C(OVB))
        for h in range(8):
            if h % 3 == 2:
                act(R("TW", M * h, M * h + M), R("wg"), scale=O8(h))
            else:
                ts(R("TW", M * h, M * h + M), R("wg"), O8(h), OP.mult)

    def init2():
        ts(R("V", 2 * M, 4 * M), R("V", 0, 2 * M), C(A4 + 1), OP.add)
        pairs(0)
        act(R("V", 4 * M, 6 * M), R("V", 0, 2 * M), bias=C(A4 + 2))
        ts(R("V", 6 * M, 8 * M), R("V", 2 * M, 4 * M), C(A4 + 2), OP.add)

    def init3():
        act(R("UU"), R("u1", 0, 128), scale=-1.0)
        for i in range(8):
            act(R("BK", 128 * i, 128 * i + 128), R("BO"), scale=C(BKS + i))

    def static():
        ts(R("stat"), R("V", 0, K), O8(1), OP.mult)

    def init4():
        cp(R("btu", 120, 240), R("bti", 120, 240))
        act(C(RSS), OH(10), scale=-1.0, bias=1.0)
        act(C(T0 + 17), OH(10), scale=8.0)
        act(C(T0 + 8), OH(4), scale=19.0)
        act(C(RSB), C(T0 + 16), scale=32.0, bias=C(T0 + 17))
        act(C(T0 + 9), OH(4), scale=32.0, bias=OH(6))
        region(0)

    def init5():
        act(C(OVS), O8(2), scale=-1.0, bias=1.0)
        act(C(OVB, 4), R("iof", 0, 4), scale=C(T0 + 8), bias=C(T0 + 9))
        exsel(NAME, C(W8))
        exsel(TAG, OH(6))
        act(R("OVQ"), R("Q0"), scale=O8(2))

    def init6():
        fill(R("hb", W, W + M), 0.0)
        ts(R("ia", 128, 256), R("ioi", 0, 128), 15, OP.bitwise_and)
        cp(R("ag"), R("lags"))
        act(R("I1", 128, 256), R("I1", 0, 128), scale=3.0)
        act(R("I1", 256, 384), R("I1", 0, 128), scale=-128.0)
        act(C(RRB, 3), R("iof", 0, 3), scale=-2.0, bias=-63.0)
        act(R("HB"), R("TW", 0, HW), AF.Tanh, scale=0.0)

    def init7():
        ts(R("RP"), R("ia", 128, 256), C(RC), OP.is_equal)
        ts(R("SG"), R("ia", 128, 256), C(RC), OP.is_equal, -PS, OP.mult)

    def init8():
        pairs(1)
        fill(R("NT", 182, 720, 3), 0.0)
        cp(R("btu", 240, 480), R("bti", 240, 480))
        tt(C(T0), O8(0), O8(2), OP.add)
        ts(C(WREL), OH(10), 64.0, OP.mult, OH(1), OP.add)
        tt(C(CM), C(T0), OH(10), OP.add)
        ts(R("u1", 0, 128), R("u1", 256, 384), O8(1), OP.mult)
        ts(R("u1", 128, 256), R("I1", 0, 128), C(CM), OP.mult)
        fill(R("HA", 2 * M, HW), 0.0)
        tt(R("CPY"), R("u1", 0, 128), R("u1", 128, 256), OP.add)
        pairs(2)
        pairs(3)

    def init9():
        exsel(PR, C(W8 + 1))
        exsel(PB, C(W8 + 2))
        region(1)

    def init10():
        act(R("HA", 0, 2 * M), R("hb", 2 * M * pm, 2 * M * pm + 2 * M))

    def masks(t, parts=range(3)):
        for i in parts:
            act(R("MK", 640 * i, 640 * i + 640), IX(R("TW"), R("btu", 120 * t + 40 * i, 120 * t + 40 * i + 40)))

    def weights(t, bank="P3", mid=None):
        ext(R(bank, 0, 120), WGT, "MK", 0, 120)
        if mid:
            mid()
        act(R("wl", 120 * t, 120 * t + 120), R(bank, 0, 120))

    def state(t):
        own = R("FL", 1024 * t + 128 * pm, 1024 * t + 128 * pm + 128)
        act(R("rr"), R("P0", 0, 128), AF.Relu, bias=C(RRB + t))
        mm([(R("P4", 128, 256), own, R("I1", 128, 256))])
        mm([(R("P0", 0, 128), R("I1", 0, 128), R("ag")), (R("P0", 0, 128), R("rr"), R("I1", 128, 256)),
            (R("P0", 0, 128), own, R("I1", 256, 384))], True, False)
        act(R("c2"), R("P4", 128, 256))

    def head(t):
        f0 = 1024 * (t - 1)
        for part in (peers, range(4, 8)):
            mm([(R("P0", 0, 128), R("FL", f0 + 128 * p, f0 + 128 * p + 128), R("I1", 0, 128)) for p in part], False, part is not peers)
        tt(R("ag"), R("P0", 0, 128), R("c2"), OP.max)
        for k in range(16):
            if k % 3 == 2:
                act(R("TA", 128 * k, 128 * k + 128), R("ag"), scale=OH(k))
            else:
                ts(R("TA", 128 * k, 128 * k + 128), R("ag"), OH(k), OP.mult)

    def ages(t, cut=(30, 30), mid=None):
        c, tab = 120 * t, "TA" if t else "TW"
        for h in (0, 60):
            n_ = cut[h // 60]
            act(R("y", 16 * h, 16 * (h + n_)), IX(R(tab), R("btu", c + h, c + h + n_)))
            if n_ < 60:
                cp(R("y", 16 * (h + n_), 16 * h + 960), IX(R(tab), R("btu", c + h + n_, c + h + 60)))
            ext(R(("P1", "P3")[h // 60], 0, 60), None if t else LAG, "y", 16 * h, 60)
            if mid and h == 0:
                mid()

    spare = []

    def gap(n_=1):
        for _ in range(min(n_, len(spare))):
            spare.pop(0)()

    def first(t, parts=(0, 1)):
        lim = 4.0 if t else 32.0
        if 0 in parts:
            tt(R("sl", 0, 60), R("P1", 0, 60) if t else R("P5", 0, 60), R("wl", 120 * t, 120 * t + 60), OP.mult)
        if 1 in parts:
            ts(R("lim", 0, 60), R("sl", 0, 60), lim, OP.is_lt, lim, OP.mult)

    def choice(t, end=None):
        c = 120 * t
        k = [R("P4", 64 * i, 64 * i + 60) for i in range(2)]
        src = [R("P1", 0, 60), R("P3", 0, 60)]
        wl = [R("wl", c + 60 * h, c + 60 * h + 60) for h in range(2)]
        if t == 0:
            for h in range(2):
                ts(R("FO", 64 * h, 64 * h + 60), src[h], -2.0, OP.add, EIGHTS, OP.add)
            for h in range(2):
                ts(wl[h], R("FO", 64 * h, 64 * h + 60), -EIGHTS, OP.add)
            for h in range(2):
                tt(R("P5", 64 * h, 64 * h + 60), src[h], wl[h], OP.subtract)
                src[h] = R("P5", 64 * h, 64 * h + 60)
            first(0, [0])
        tt(k[0], src[1], wl[1], OP.mult)
        if t == 0:
            first(0, [1])
        gap()
        tt(R("T0", 1, 180, 3), k[0], R("sl", 0, 60), OP.is_gt)
        tt(R("T0", 2, 180, 3), k[0], R("lim", 0, 60), OP.is_ge)
        gap()
        scan(R("F1"), R("T0"), R("NT", 180 * t, 180 * t + 180), 0.0, OP.mult, OP.add)
        gap()
        ts(R("key", 0, 60), R("F1", 2, 180, 3), -127.5, OP.add, ROUND, OP.add)
        ts(R("n16", 0, 60), R("F1", 1, 180, 3), -float(M), OP.add)
        for i in range(8):
            ts(R("Dh", i, 480, 8), R("key", 0, 60), ROUND + 256.0 * (i + 1), OP.is_equal)
        for h in range(2):
            src = IX(R("V", 0, W), R("n16", 30 * h, 30 * h + 30))
            if t == 0:
                act(R("Gs", 480 * h, 480 * h + 480), src, bias=C(GSB), scale=C(GSS))
            else:
                act(R("Gr", 480 * h, 480 * h + 480), src)
        for i0 in (0, 4):
            mm([(R("P2", 0, 60), R("Z", 15 - i, 143 - i), R("Dh", i, 480, 8)) for i in range(i0, i0 + 4)], i0 == 0, i0 == 4)
        mm([(R("P3", 0, 480), R("UU"), R("Dh"))], True, False)
        ts(R("thr", 0, 60), R("key", 0, 60), -(ROUND + 8192.0), OP.add, 0.125, OP.mult)
        ts(R("qb", 0, 60), R("F1", 1, 180, 3), -1.0, OP.mult, float(AN[t] + 1024 + M), OP.add)
        gap(3)
        if end:
            end()

    def carry(t, h):
        pb = ("P5", "P7")[h]
        mm([(R(pb, 0, 480), R("CPY"), R("Gr", 480 * h, 480 * h + 480))])
        act(R("Gs", 480 * h, 480 * h + 480), R(pb, 0, 480), bias=C(GSB + t))

    def prefix(t, mid=None):
        scan(R("Ec", 0, 60), R("c33", 0, 60), R("P2", 0, 60), OH(8), OP.min, OP.add)
        mm([(R("P3", i, 480, 8), R("BK", 128 * i, 128 * i + 128), R("Ec", 0, 60)) for i in range(8)], False, True)
        gap(len(spare))
        if mid:
            mid()
        if t > 0:
            carry(t, 0)
            carry(t, 1)
            ext(R("P4", 0, 60), PR, "Gr", 0, 60)
        scan(R("P2", 0, 480), R("D8"), R("P3", 0, 480), 0.0, OP.add, OP.min)
        tt(R("T0", 1, 180, 3), R("P2", 7, 480, 8), R("thr", 0, 60), OP.is_lt)
        tt(R("F1", 0, 180, 3), R("P2", 7, 480, 8), R("qb", 0, 60), OP.add)
        scan(R("FO"), R("T0"), R("F1"), 0.0, OP.mult, OP.add)
        ts(R("o16", 64 * t, 64 * t + 60), R("FO", 1, 180, 3), -float(M), OP.add)

    def scatter(t, c0=0, c1=60):
        tt(IX(R("V", 0, XB[t]), R("o16", 64 * t + c0, 64 * t + c1)), R("Gs", 16 * c0, 16 * c1), R("stat", 16 * c0, 16 * c1), OP.add)

    def granted(t):
        act(R("ovt"), R("V", AN[t], XB[t]), bias=C(OVB + t), scale=C(OVS))

    def places(t, parts=(0, 1)):
        if 0 in parts:
            ts(R("key", 0, 60), R("P4", 0, 60), float(M), OP.add)
        if 1 in parts:
            tt(R("s3", 0, 60), R("key", 0, 60), R("FO", 1, 180, 3), OP.max)
            ts(R("xo", 64 * t, 64 * t + 60), R("s3", 0, 60), -float(M), OP.add)

    def names(t):
        ext(R("P2", 0, 16), NAME, "V", AN[t], 16)

    def override(t):
        cp(R("rq16"), R("P1", 48, 64) if t == RO - 1 else R("P2", 0, 16))
        tt(IX(R("V", 0, W + M), R("rq16")), R("ovt"), R("OVQ"), OP.add)

    def tags(t):
        mm([(R("P0", k, 128, 16), R("V", 128 * k, 128 * k + 128), R("EX", 144 * TAG + 15, 144 * TAG + 143, 16)) for k in range(16)], each=True)

    def flags(t):
        own = R("FL", 1024 * t + 128 * pm, 1024 * t + 128 * pm + 128)
        ts(own, R("P0", 0, 128), 2 * t + 64.5, OP.is_ge)
        to_all(own, R("rlf", 128 * t, 128 * t + 128), "fs%d" % t)

    def lists(t):
        cols = (W8 + 2, W8 + 4, WREL, W8)[:4 if t == RO - 1 else 3]
        i0 = 1 if t == RO - 1 else 0
        if i0:
            ext(R("P2", 0, 16), PB, "V", AN[t], 16)
        for i, c in list(enumerate(cols))[i0:]:
            act(R("X4", M * i, M * i + M), R("V", AN[t], XB[t]), scale=C(c))
        ext(R("P1", 16 * i0, 16 * len(cols)), None, "X4", M * i0, 16 * (len(cols) - i0))

    def block(t, j):
        if t < RO - 1:
            c = ((t - 1) * 4 + j) * BW
            return (pm - 1 - SLOTS[j]) % 4, c + 4, c
        c = (t - 1) * 4 * BW + j * MW
        return ((pm - 1 - SLOTS[j]) % 4,) + ((c + 4, c) if SLOTS[j] % 2 else (c, c + 64))

    def runs(t, part, w_):
        out = []
        for j in range(4):
            blk = block(t, j)
            if out and out[-1][0] + out[-1][2] == blk[0] and out[-1][1] + w_ * out[-1][2] == blk[part]:
                out[-1][2] += 1
            else:
                out.append([blk[0], blk[part], 1])
        return out

    def bases(t, out, in_):
        cp(out, in_)
        act(R("RB"), IX(R("L", 0, XB[t - 1]), R("pb16", 0, 16)))

    def pointers(t):
        if t == RO - 1:
            cp(R("pb16", 16, 32), R("P1", 16, 32))
        else:
            bases(t, R("pb16"), R("P1", 0, 32))
        if t == RO - 1:
            for p, c, n_ in runs(t, 2, 4):
                act(R("MSG", c, c + 4 * n_), R("P1", 32 + 4 * p, 32 + 4 * p + 4 * n_))
            return
        for j in range(4):
            p, _, c = block(t, j)
            for h in range(2):
                act(R("MSG", c + 68 * h, c + 68 * h + 4), R("P1", 32 + 4 * p, 36 + 4 * p))

    def values(t):
        for p, c, n_ in runs(t, 1, 64):
            tt(R("MSG", c, c + 64 * n_), IX(R("L", 0, AN[t]), R("pb16", 16 + 4 * p, 16 + 4 * p + 4 * n_)), R("RB", 64 * p, 64 * p + 64 * n_), OP.subtract)

    def request(t):
        m0, s, w_ = (t - 1) * 4 * BW, (t - 1) * 2 * BW, 2 * (MW if t == RO - 1 else BW)
        es = (e_on, e_off) if t == RO - 1 else (e_on[:4], e_on[4:])
        send([(rel[me][k], es[k], "rr%d" % t, R("MSG", m0 + k * w_, m0 + (k + 1) * w_), R("rlq", s, s + w_)) for k in range(2)])

    def request_near(t):
        w_ = MW if t == RO - 1 else BW // 2
        c = [(t - 1) * 4 * BW + (MW * SLOTS.index(i) if t == RO - 1 else BW * SLOTS.index(i) + w_ * (mine[peers[i]] % 2)) for i in range(3)]
        to_peers(("qa%d" % t, "qb%d" % t), peers, lambda i: R("MSG", c[i], c[i] + w_),
                 lambda i: R("RQ", ((t - 1) * 8 + i) * MW, ((t - 1) * 8 + i) * MW + w_))

    def at(t, *groups):
        for slots in groups:
            s0 = slots[0]
            nm, c = ("MSG", block(t, 2)[2]) if s0 == 3 else ("RQ", ((t - 1) * 8 + s0) * MW + 64)
            if t == RO - 1:
                cp(R("ho", 4 * s0, 4 * s0 + 4 * len(slots)), R(nm, c, c + 4 * len(slots)))
            elif s0 == 3:
                cp(R("ho", 6, 8), R(nm, c + 2 * (me % 2), c + 2 * (me % 2) + 2))
            else:
                c += 34 * (me % 2) - 64
                for h in range(2):
                    cp(R("ho", 2 * s0 + h, 2 * s0 + 2 * len(slots), 2), R(nm, c + h, c + h + MW * (len(slots) - 1) + 1, MW))

    def adds(t, slots, alone=False, mid=None):
        n_, c0 = (4, 0) if t == RO - 1 else (2, 32 * (me % 2))
        cv = [("MSG", block(t, 2)[1]) if s == 3 else ("RQ", ((t - 1) * 8 + s) * MW + (4 * (s % 2) if n_ == 4 else 4 - 36 * (me % 2))) for s in slots]
        ws = [IX(R(("HB", "HA")[s % 2]), R("ho", n_ * s, n_ * s + n_)) for s in slots]
        hs = [R("ht", 64 * (s % 2), 64 * (s % 2) + 16 * n_) for s in slots]
        vs = [R(nm, c + c0, c + c0 + 16 * n_) for nm, c in cv]
        for i in range(len(slots)):
            if alone:
                tt(hs[i], ws[i], vs[i], OP.add)
            else:
                act(hs[i], ws[i])
        if mid:
            mid()
        for i in range(len(slots)):
            if alone:
                cp(ws[i], hs[i])
            else:
                tt(ws[i], hs[i], vs[i], OP.add)

    def answer_near(t, w_, c):
        a0 = 256 * (t - 1)
        to_peers(("an%d" % t,) * 2, asker, lambda i: R("AO", a0 + w_ * i, a0 + w_ * i + w_), lambda i: R("L", c, c + w_))
        act(R("L", c, c + w_), R("AO", a0 + 3 * w_, a0 + 4 * w_))

    def hand_over():
        src = [R(nm, side, side + M) for nm in ("HA", "HB")]
        deps("g", src[0][1] + src[1][1], [])
        g.remote_dma_fused([xfer(topo, core, rel[me][2 + k], (e_on, e_off)[k], T.sem.rx, src[k][0], T.rlx[:]) for k in range(2)], local_sem=T.sem.sx)
        note("x", src[0][1] + src[1][1], [], ("sx", 16))
        dtok.append(("sx", 16))

    def take_over():
        for k, nm in enumerate(("HA", "HB")):
            act(R(nm, M - side, 2 * M - side), R("HX", M * k, M * k + M))

    def sums():
        return [[IX(R(nm), R("ho", 8 * h, 8 * h + 8)) for h in range(2)] for nm in ("HA", "HB")]

    def home(t):
        a0, (ha, hb) = 256 * (t - 1), sums()
        at(t, [0, 1])
        adds(t, [0, 1], mid=lambda: at(t, [2]))
        adds(t, [2], mid=lambda: at(t, [4, 5]))
        adds(t, [5], mid=lambda: at(t, [6, 7]))
        for s in (4, 7, 6):
            adds(t, [s])
        for h in range(2):
            act(R("at", 128 * h, 128 * h + 128), ha[h])
        for h in range(2):
            tt(R("AO", a0 + 128 * h, a0 + 128 * h + 128), hb[h], R("at", 128 * h, 128 * h + 128), OP.add)
        answer_near(t, 64, AN[t] + 64 * pm)

    def keep(t):
        a0, (ha, hb) = 256 * (t - 1), sums()
        at(t, [0, 1, 2])
        adds(t, [0, 1], True)
        at(t, [4, 5, 6, 7])
        adds(t, [2, 5], True)
        adds(t, [4, 7], True, lambda: first(t + 1, [0]))
        adds(t, [6], True, lambda: (cp(R("at", 128, 256), ha[1]), first(t + 1, [1])))
        cp(R("at", 0, 128), ha[0])
        tt(R("AO", a0 + 128, a0 + 256), hb[1], R("at", 128, 256), OP.add)
        send([(rel[me][k], (e_on, e_off)[k], "ra%d" % t, R("AO", a0 + 128 + 64 * k, a0 + 192 + 64 * k), R("rla", 64 * t - 64, 64 * t)) for k in range(2)])

        def rest():
            tt(R("AO", a0, a0 + 128), hb[0], R("at", 0, 128), OP.add)
            answer_near(t, 32, AN[t] + 32 * me)
            if t == RO - 2:
                hand_over()
        spare.append(rest)

    def own(t):
        at(t, [3])
        adds(t, [3], True)

    def starts():
        act(R("L", AN[0], XB[0]), IX(R("hb"), R("rq16")))

    def slots(t, c0, c1):
        return IX(R("L", 0, XB[t]), R("xo" if t else "o16", 64 * t + c0, 64 * t + c1))

    def partners(t, cuts=((0, 8), (8, 20), (20, 30))):
        for c0, c1 in cuts:
            act(R("x", 480 + 16 * c0, 480 + 16 * c1), slots(t, 30 + c0, 30 + c1))

    def firsts(t):
        act(R("x", 0, 480), slots(t, 0, 30))

    def products(t, cuts=((0, 8), (8, 20), (20, 30))):
        for c0, c1 in cuts:
            tt(R("prod", 16 * c0, 16 * c1), slots(t, c0, c1), R("x", 480 + 16 * c0, 480 + 16 * c1), OP.mult)

    def errors(t):
        top = slice(0, 16)
        out = R("P5" if t else "P6", 64, 124)
        mm([(out, R("RP", parts=top), R("tgs", 60 * t, 60 * t + 60, parts=top))], True, False)
        for k0, k1 in (((0, 2), (2, 4), (4, 6), (6, 8)) if t == RO - 1 else ((0, 2), (2, 5), (5, 8))):
            mm([(out, R("SG"), R("prod", 60 * k, 60 * k + 60)) for k in range(k0, k1)], False, k1 == 8)

    def squash(t):
        if t == RO - 1:
            act(R("yo", 480, K), R("x", 480, K), scale=ST)
            act(R("P6", 0, 60), R("P5", 64, 124), AF.Tanh)
            act(R("yo", 0, 480), R("x", 0, 480), scale=ST)
            return
        act(R("er", 0, 60), R("P5" if t else "P6", 64, 124), AF.Tanh)
        act(R("P6", 0, 60), R("er", 0, 60), scale=ST)

    def bank(t, h):
        return ("P7", "P5")[h] if t else ("P0", "P7")[h]

    def step(t, h, ks=range(8)):
        for k in ks:
            c = 480 * (1 - h) + 60 * k
            tt(R(bank(t, h), 60 * k, 60 * k + 60), R("P6", 0, 60), R("yo" if t == RO - 1 else "x", c, c + 60), OP.mult)

    def stepped(t, h):
        tt(R("L", XB[t] + 480 * h, XB[t] + 480 * h + 480), R(bank(t, h), 0, 480), R("x", 480 * h, 480 * h + 480), OP.add)

    def steps(t):
        step(t, 0)
        step(t, 1)
        stepped(t, 0)
        stepped(t, 1)

    init()
    ages(0); init2(); init3(); choice(0, init4); init5(); prefix(0, static); masks(1); scatter(0)
    granted(0); names(0); init6(); override(0); starts(); partners(0); tags(0); init7(); flags(0)
    products(0); state(0); errors(0); init8(); weights(1, "P3", lambda: (firsts(0), squash(0)))
    init9(); init10(); step(0, 1); stepped(0, 1)

    head(1); ages(1); spare.extend(lambda k=k: step(0, 0, [k]) for k in range(8)); first(1); choice(1); prefix(1)
    region(2); masks(2); scatter(1)
    granted(1); names(1); lists(1); stepped(0, 0); override(1); tags(1); pointers(1); places(1, [0])
    flags(1); values(1); request(1); request_near(1); state(1); weights(2); places(1, [1]); own(1)

    head(2); ages(2, (60, 54)); keep(1); choice(2); prefix(2); partners(1, ((0, 16), (16, 30)))
    scatter(2, 0, 30); products(1, ((0, 16), (16, 30))); firsts(1); errors(1); region(3); masks(3, [0]); squash(1)
    scatter(2, 30, 60); granted(2); names(2); lists(2); step(1, 0); override(2); tags(2); step(1, 1); pointers(2)
    flags(2); state(2); stepped(1, 0); stepped(1, 1); places(2, [0]); values(2); request(2); request_near(2)
    masks(3, [1, 2]); places(2, [1]); own(2)

    head(3)
    ext(R("P2", 0, 120), WGT, "MK", 0, 120)
    ages(3, (60, 54), lambda: act(R("wl", 360, 480), R("P2", 0, 120))); keep(2); choice(3); prefix(3)
    partners(2, ((0, 16), (16, 30))); scatter(3, 0, 30); products(2, ((0, 16), (16, 30))); firsts(2); errors(2); squash(2)
    scatter(3, 30, 60); lists(3); step(2, 0); bases(3, R("pb16", 0, 16), R("P2", 0, 16)); step(2, 1); stepped(2, 0)
    pointers(3); stepped(2, 1); values(3); request(3); request_near(3); take_over(); granted(3); override(3); places(3)
    ext(R("P0", 0, 128), PR, "V", 0, 128)
    own(3)
    cp(R("f16"), R("P0", 0, 128))
    home(3)
    tt(R("yq"), R("HA", side, side + M), R("HB", side, side + M), OP.add)
    dma("s", T.yh[:], R("yq"))
    partners(3, ((0, 8), (8, 16), (16, 30))); products(3, ((0, 8), (8, 16), (16, 24), (24, 30)))
    firsts(3); errors(3); squash(3); steps(3)
    c0 = 0
    for n_ in (256, 512, 640, 640):
        h = n_ // 32 * 16
        act(R("yo", c0, c0 + h), IX(R("L"), R("f16", c0 // 16, (c0 + h) // 16)))
        cp(R("yo", c0 + h, c0 + n_), IX(R("L"), R("f16", (c0 + h) // 16, (c0 + n_) // 16)))
        dma("s", T.yr[:, c0:c0 + n_], R("yo", c0, c0 + n_))
        c0 += n_
    for tok in dtok:
        need("g", tok)
    for q in "vapg":
        need("g", ("c" + q, cnt[q]))
    g.wait_ge(T.sem.snt, cnt["snt"])
